import numpy as np, ml_dtypes
CORES = [10,34,74,98]
N = 4
BF = ml_dtypes.bfloat16
def gentries(a):
    return np.ascontiguousarray(a.reshape(8, 16, -1).transpose(0, 2, 1)).reshape(8, -1)
def gtable(e):
    e = np.asarray(e); return np.ascontiguousarray(e.reshape(8, -1, 16).transpose(0, 2, 1)).reshape(128, -1).astype(np.int32)
W, LW, M, K, CAP, RO = 4096, 12, 1024, 256, 128, 4
def h1(v):
    return ((v * v >> 3) + v) & (W - 1)
def h2(v):
    return ((v * v >> 5) + 37 * v + 1) & (W - 1)
def parts(rng):
    X = rng.integers(0, 16, (N, 8, 16, W)); F = rng.integers(0, W, (N, 8, 16, W)); LG = rng.integers(0, M, (N, 8, W))
    for q in range(N):
        for g in range(8):
            v = rng.permutation(M)[:7 * M // 10]
            LG[q, g, np.where(rng.random(len(v)) < 0.5, h1(v), h2(v))] = v
    LE = (rng.random((N, 8, W)) < rng.choice(np.array([0.3, 0.5, 0.7, 0.9]), (N, 8, 1))).astype(np.int64)
    XL = rng.integers(0, 16, (N, 8, 16, M)); LF = rng.integers(0, M, (N, 8, 16, M))
    return X, F, LG, LE, XL, LF, rng.integers(0, W, (N, 8, 16, K)), rng.integers(0, 16, (N, 8, 16, K))
def pack(X, F, LG, LE, XL, LF, C, Q):
    def bf(a): return np.ascontiguousarray(a).reshape(N, 128, -1).astype(np.float32).astype(BF)
    F = np.ascontiguousarray(F).reshape(N, 128, W)
    return {"xr": bf(X), "fd": (F[..., :W // 2] + W * F[..., W // 2:]).astype(np.int32), "tg": (2 * LG + LE).astype(np.int32), "xl": bf(XL),
            "lf": np.ascontiguousarray(LF).reshape(N, 128, M).astype(np.int32), "cx": np.stack([gtable(a.transpose(0, 2, 1).reshape(8, -1)) for a in C]), "qx": bf(Q)}
def setup_inputs(rng):
    return pack(*parts(rng))
def setup_inputs_spread(rng):
    X, F, LG, LE, XL, LF, C, Q = parts(rng)
    def small(n): return np.minimum((np.exp2(4.2 * rng.random((N, 8, 1, n))) * rng.random((N, 8, 16, n))).astype(np.int64), 15)
    def low(n, top): return np.minimum((top * rng.random((N, 8, 16, n)) ** rng.choice(np.array([1.0, 2.0, 4.0]), (N, 8, 1, n))).astype(np.int64), top - 1)
    LE = (rng.random((N, 8, W)) < rng.random((N, 8, 1))).astype(np.int64)
    return pack(small(W), low(W, W), LG, LE, small(M), low(M, M), low(K, W), small(K))
def setup_inputs_ends(rng):
    X, F, LG, LE, XL, LF, C, Q = parts(rng); h = W // 2
    def faces(n):
        kind = rng.integers(0, 3, (N, 8, 1, n)); a = 15 * np.where(kind == 2, rng.integers(0, 2, (N, 8, 16, n)), kind)
        near = (rng.random((N, 8, 1, n)) < 0.25) & (np.arange(16)[:, None] == rng.integers(0, 16, (N, 8, 1, n)))
        return np.abs(a - near.astype(np.int64))
    def ends(a, top): return np.where(rng.random(a.shape) < 0.66, top * rng.integers(0, 2, a.shape), a)
    X, XL, Q = faces(W), faces(M), faces(K)
    X[..., 0] = 0; X[..., W - 1] = 0; X[..., 1] = 15; X[..., W - 2] = 15
    X[..., 2] = 0; X[..., 0, 2] = 1; X[..., W - 3] = 0; X[..., 15, W - 3] = 1
    m = rng.random((N, 8, 16, h)) < 0.66; e = (W - 1) * rng.integers(0, 2, m.shape)
    F = np.concatenate([np.where(m, e, F[..., :h]), np.where(m, e, F[..., h:])], axis=-1)
    m = rng.random((N, 8, W)) < 0.66; e = (rng.random((N, 8, W)) < 0.6).astype(np.int64)
    LG = np.where(m, (M - 1) * e, LG); LE = np.where(m, e, LE)
    LG[..., 0] = 0; LE[..., 0] = 0; LG[..., W - 1] = M - 1; LE[..., W - 1] = 1
    LF = ends(LF, M - 1); C = ends(C, W - 1)
    for k in (0, 1, K - 1): Q[..., k] = 15; C[..., k] = (W - 1) * rng.integers(0, 2, (N, 8, 16))
    Q[..., K - 2] = 0; C[..., K - 2] = (W - 1) * rng.integers(0, 2, (N, 8, 16))
    for k in (2, K - 3): Q[..., k] = 0; C[..., :15, k] = 1; C[..., 15, k] = W - 1
    for k, v in ((3, 2), (K - 4, W - 3)): Q[..., k] = 15; C[..., :15, k] = (W - 1) * rng.integers(0, 2, (N, 8, 15)); C[..., 15, k] = v
    return pack(X, F, LG, LE, XL, LF, C, Q)
def setup_inputs_corners(rng):
    X, F, LG, LE, XL, LF, C, Q = parts(rng); cnt = (0, 1, CAP - 1, CAP, CAP + 1, K); a = np.arange(M)
    for g in (2, 7):
        LG[:, g] = LG[0, g]; res = a[(LG[0, g][h1(a)] == a) | (LG[0, g][h2(a)] == a)]; LF[:, g] = rng.choice(res, (N, 16, M))
    v = LG[:, 3]; c = np.arange(W)
    for _ in range(3): v = np.where((h1(v) == c) | (h2(v) == c), (v + 1) % M, v)
    LG[:, 3] = v
    few = np.array([0, 1, M - 2, M - 1]); LF[:, 5] = rng.choice(few, (N, 16, M)); LG[:, 6] = rng.choice(few, (N, W))
    LE[:, 4] = 1; LE[0, 0] = 0
    for q in range(N):
        for g in range(8):
            b = rng.permutation(W)[:4 * K].reshape(K, 4)
            C[q, g] = b[np.arange(K)[None, :], rng.integers(0, 4, (16, K))]
            ask = np.zeros(K, np.int64); ask[rng.permutation(K)[:cnt[(q + g) % 6]]] = 1
            if g == 7:
                o = C[q, g][np.argmin(far(X[q, g], C[q, g], Q[q, g]), axis=0), np.arange(K)]; LE[q, g] = 0; LE[q, g, o] = ask
            else: LE[q, g, b] = ask[:, None]
    return pack(X, F, LG, LE, XL, LF, C, Q)
def setup_inputs_ties(rng):
    X, F, LG, LE, XL, LF, C, Q = parts(rng)
    pal = rng.integers(6, 10, (N, 8, 16, 6))
    X = np.take_along_axis(pal, rng.integers(0, 6, (N, 8, 1, W)), 3); XL = np.take_along_axis(pal, rng.integers(0, 6, (N, 8, 1, M)), 3)
    for q in range(N):
        for g in range(8):
            v = rng.permutation(M)[:M // 2]; LG[q, g, h2(v)] = v; LG[q, g, h1(v)] = v
    return pack(X, F, LG, LE, XL, LF, C, Q)
def setup_inputs_alike(rng):
    X, F, LG, LE, XL, LF, C, Q = parts(rng)
    for g in range(8):
        s = rng.permutation(M); w = s[:64]; pl = np.concatenate([h1(w), h2(w)])
        pair = s[:6]; few = np.concatenate([pair, pair ^ 1])
        for q in range(N):
            if g % 2 == 0:
                pool = rng.permutation(W)[:40]; C[q, g] = rng.choice(pool, (16, K)); F[q, g, :, ::2] = rng.choice(pool, (16, W // 2))
                LE[q, g, pool] = rng.random(40) < 0.8; LG[q, g, pool] = rng.choice(few, 40); LF[q, g] = rng.choice(s[:24], (16, M))
            else:
                C[q, g] = rng.choice(pl, (16, K)); LE[q, g, pl] = 1; LG[q, g, pl] = rng.choice(s[64:], 128); LF[q, g] = rng.choice(w, (16, M))
    return pack(X, F, LG, LE, XL, LF, C, Q)
def check_inputs(d):
    bad = []
    for k, lo, hi in (("xr", 0, 15), ("fd", 0, W * W - 1), ("tg", 0, 2 * M - 1), ("xl", 0, 15), ("lf", 0, M - 1), ("cx", 0, W - 1), ("qx", 0, 15)):
        a = np.asarray(d[k]).astype(np.float64)
        if not (np.min(a) >= lo and np.max(a) <= hi): bad.append("range of " + k)
        elif np.any(a != np.floor(a)): bad.append("whole numbers of " + k)
    return bad
def lowest(key, use):
    ix = np.flatnonzero(use); m = np.zeros(len(key), bool); m[ix[np.unique(key[ix], return_index=True)[1]]] = True
    return m
def far(x, c, q):
    return np.add.reduce(np.abs(x[:, c] - q[:, None, :]), axis=0)
def reference(xr, fd, tg, xl, lf, cx, qx):
    def whole(a): return a.astype(np.float32).astype(np.int64).reshape(N, 8, 16, -1)
    X, XL, Q = whole(xr), whole(xl), whole(qx)
    fi = fd.astype(np.int64); F = np.concatenate([fi & (W - 1), fi >> LW], axis=-1).reshape(N, 8, 16, W)
    LG = tg.astype(np.int64) >> 1; LE = tg.astype(np.int64) & 1; LF = lf.astype(np.int64).reshape(N, 8, 16, M)
    C = np.ascontiguousarray(np.stack([gentries(a) for a in cx]).astype(np.int64).reshape(N, 8, K, 16).transpose(0, 1, 3, 2))
    lane = np.arange(K)
    for t in range(RO):
        asked = {}; back = {}
        for r in range(N):
            for g in range(8):
                c = C[r, g]; o = c[np.argmin(far(X[r, g], c, Q[r, g]), axis=0), lane]
                s = np.flatnonzero(lowest(o, LE[r, g][o] == 1))[:CAP]
                asked[r, g] = (o, s, LG[r, g][o[s]], LG[r, g][c[:, s]])
        for r in range(N):
            p = (r + 1 + t % (N - 1)) % N
            for g in range(8):
                o, s, n, sent = asked[r, g]
                back[r, g] = (XL[p, g][:, n], LF[p, g][:, n])
                w = lowest(n ^ 1, np.ones(len(n), bool)); LF[p, g][:, (n ^ 1)[w]] = sent[:, w]
        for r in range(N):
            for g in range(8):
                o, s, n, sent = asked[r, g]; a, v = back[r, g]; q = Q[r, g][:, s]; j = np.arange(len(s))
                c1, c2 = h1(v), h2(v); in1 = LG[r, g][c1] == v; in2 = LG[r, g][c2] == v
                sh = np.where(in1, c1, np.where(in2, c2, np.where(far(X[r, g], c2, q) > far(X[r, g], c1, q), c2, c1)))
                new = ~(in1 | in2); i = np.argmax(new, axis=0); pl = sh[i, j]; w = lowest(pl, np.any(new, axis=0))
                LG[r, g][pl[w]] = v[i, j][w]; LE[r, g][pl[w]] = 1
                F[r, g][:, o[s]] = sh; X[r, g][:, o[s]] = a; LE[r, g][o[s]] = 0
                C[r, g] = F[r, g][:, o]; Q[r, g] = (Q[r, g] + X[r, g][:, o]) >> 1
    return {"yc": C.reshape(N, 128, K).astype(np.float32), "yq": Q.reshape(N, 128, K).astype(np.float32).astype(BF), "yt": (2 * LG + LE).astype(np.float32), "yl": LF.reshape(N, 128, M).astype(np.float32)}

@@ -1,0 +1,733 @@
+import numpy as np
+from concourse.mybir import AluOpType as O, AxisListType, ActivationFunctionType as F
+
+STEPS = 4
+CHOICE = "svss"
+CL1, CL2, CU2 = 2, 3, 1
+TRANS = "vsvs"
+CEAT = 1
+HALF = 32
+SUMV = 7
+
+
+def _scratch():
+    S = {}
+
+    def sb(n, w, d="float32"):
+        S[n] = ("sbuf", [128] + (w if isinstance(w, list) else [w]), d)
+    B, I, U = "bfloat16", "int32", "uint16"
+    sb("V", 4224, B); sb("FW", 4224, I); sb("FD", 2048, I)
+    for k in range(6):
+        sb("E%d" % k, 136)
+    sb("LFF", 1280, I); sb("LFH", 1024, I); sb("YL", 1280); sb("MX", 8, U)
+    for k in range(3):
+        sb("LF%d" % k, 1280, I); sb("U%d" % k, 1024, U)
+        sb("XL%d" % k, 1152, B)
+    sb("XLH", 1024, B); sb("HU", 1024, U)
+    sb("CI", 256, I); sb("CF", 384); sb("CU", 256, U); sb("Q", 384, B); sb("CE", [16, 16]); sb("CO", [16, 16])
+    for k in range(4):
+        sb("XG%d" % k, 1024, B); sb("XD%d" % k, 1024, B); sb("AB%d" % k, 512, B)
+    for k in range(2):
+        sb("GS%d" % k, 1024, B); sb("SX%d" % k, 1024, B)
+    sb("KEY", [16, 32]); sb("KT", 512); sb("SCN", 512); sb("RST", 512)
+    sb("OI", 16, I); sb("OF", 16); sb("OU", 16, U)
+    sb("VO", 256); sb("XO", 256, B); sb("DD", 384, B); sb("OR", 256, U); sb("EQ", [16, 272], B); sb("CA", 256); sb("PX", 256)
+    sb("ONE", 256); sb("JS", 256, B); sb("JV", 256, B); sb("LS", 8); sb("T2", 1); sb("RL", 8); sb("CBP", 8); sb("INV", 8); sb("H8", 8); sb("LU", 8, U)
+    sb("DDR", 128, B); sb("CR", 128); sb("CRU", 128, U); sb("QR", 128, B)
+    sb("WNF", 8); sb("NU", 8, U); sb("OUR", 8, U); sb("NR", 128, U); sb("A", 128, B); sb("BI", 128, I); sb("BS", 128)
+    sb("SQ", 128, I); sb("S5", 128, I); sb("H", 256, I); sb("CCU", 256, U); sb("D12", 128)
+    sb("IN", 256, B); sb("INB", 128); sb("M2", 128); sb("SEL", 128); sb("SS", 128, I); sb("N12", 128, B); sb("NEW", 128, B)
+    sb("K1", 128); sb("KK", 128); sb("KKE", [8, 16]); sb("KKO", [8, 16]); sb("PEN", [8, 16]); sb("KEC", [8, 32]); sb("KTC", 256); sb("SNC", 256)
+    sb("KI", 8, I); sb("PI", 8, I); sb("BW", 8, I); sb("BU", 8, U); sb("PF", 8); sb("PU", 8, U); sb("P2", 8); sb("PU2", 8, U)
+    sb("GP", 128); sb("XP", 128, B); sb("DP", 128, B); sb("DB", 128, B); sb("ZC", 128, B); sb("NV", 128, B); sb("PLR", 128, U)
+    sb("EQ2", [8, 144], B); sb("FL", 128, B); sb("FS", 8)
+    sb("VL", 128, B); sb("QF", 256); sb("SF", 136); sb("BA", 384, I); sb("NA", 16, U)
+    sb("NI", 8, I); sb("N1", 8, I); sb("MF", 8); sb("MU", 8, U)
+    sb("YQ", 256, B); sb("TX", 5 * 256, B); sb("TD", 5 * 256, B); sb("TE", 256); sb("TE2", 256); sb("TY", 256); sb("TW", 256)
+    sb("COL", 64); sb("IP", 4, I); sb("BO", 128); sb("BO1", 128); sb("TF4", 80)
+    for n in ("ZK", "ZKN", "ZT", "ZTN", "ZN", "Z1"):
+        sb(n, 144, B)
+    for n in ("ID", "NID", "RN", "RE", "RL128", "RD", "RB", "KEEP", "TRI"):
+        sb(n, 128, B)
+    for n in range(5):
+        sb("TI%d" % n, 128, B); sb("TJ%d" % n, 128, B)
+    sb("ON128", 128); sb("IDF", 128); sb("LTF", 128); sb("J16", 16); sb("POW", 20); sb("DDM", 128, B); sb("CT", 256); sb("CT2", 256)
+    sb("SC8", 8); sb("SW8", 8); sb("SW2", 8); sb("DSC", 8); sb("DSM", 8); sb("CB", 8); sb("I8", 8)
+    sb("TGL", 256, I); sb("NM", 256, I); sb("DI", 9 * 256, I); sb("DG", 9 * 256, B)
+    sb("NB", 64, I); sb("NBD", 256, I); sb("NBB", 320, B); sb("DIG", 1024, B); sb("PJ", 8, I); sb("PJD", 24, I); sb("PD", 40, B)
+    for n in ("ps0", "ps1", "ps2", "ps3", "PA", "PT", "PR", "PC"):
+        S[n] = ("psum", [128, 512], "float32")
+    return S
+
+
+def _pack(S):
+    real, virt, width = {}, {}, {}
+    for n, (where, sh, d) in S.items():
+        if where == "psum" or len(sh) > 2 or sh[1] > 400 or n in ("E0", "E1", "E2", "E3", "E4", "E5"):
+            real[n] = (where, sh, d)
+        else:
+            unit = 8 if d in ("float32", "int32") else 16
+            at = width.get(d, 0)
+            virt[n] = ("W" + d, at, sh[1])
+            width[d] = at + -(-sh[1] // unit) * unit
+    for d, w in width.items():
+        real["W" + d] = ("sbuf", [128, w], d)
+    return real, virt
+
+
+ALL = _scratch()
+SCRATCH, VIRT = _pack(ALL)
+ARR = ["ax0", "ax1", "ax2", "af0", "af1", "af2", "aff"] + ["ae%d" % k for k in range(6)]
+SEMAPHORES = ["pv", "pc", "pt", "pg"] + ARR + ["d%d" % k for k in range(70)]
+PSUM = ("ps0", "ps1", "ps2", "ps3", "PA", "PT", "PR", "PC")
+MASKS = {}
+
+
+def rank_program(g, core, T, topo):
+    rank = T.rank_of(core)
+    if rank is None:
+        return
+    eng = {"v": g.vector, "c": g.scalar, "t": g.tensor, "g": g, "y": g.sync}
+    psem = {"v": "pv", "c": "pc", "t": "pt", "g": "pg"}
+    cnt = {"v": 0, "c": 0, "t": 0, "g": 0}
+    know = {q: {} for q in eng}
+    W, R, X = {}, {}, {}
+    total = {}
+    nd = [0]
+
+    def r(name, *idx):
+        key = (name, str(idx))
+        if key not in MASKS:
+            if name in ALL and ALL[name][0] == "sbuf":
+                sh = ALL[name][1][1:]
+                n = int(np.prod(sh)); f = np.zeros(n, np.uint8)
+                f[np.arange(n).reshape(sh)[tuple(idx[1:])].reshape(-1)] = 1
+                MASKS[key] = int.from_bytes(np.packbits(f, bitorder="little").tobytes(), "little")
+            else:
+                MASKS[key] = 1
+        if name in VIRT:
+            arena, at, w = VIRT[name]
+            cs = idx[1] if len(idx) > 1 else slice(0, w)
+            lo, hi, st = cs.indices(w)
+            return (T[arena][idx[0] if idx else slice(None), at + lo:at + hi:st], ((name, MASKS[key]),))
+        t = T[name]
+        return (t[idx] if idx else t[:], ((name, MASKS[key]),))
+
+    def c(name, a, b):
+        return r(name, slice(None), slice(a, b))
+
+    def ind(w, o):
+        return (w[0].indirect(o[0]), w[1] + o[1], w[1])
+
+    def issue(q, fn, outs, ins, dma=None, rows=None, after=None):
+        need = []
+        rd = [x for o in ins for x in o[1]]
+        wt = [x for o in outs for x in (o[2] if len(o) > 2 else o[1])]
+        for o in outs:
+            if len(o) > 2:
+                rd += [x for x in o[1] if x not in o[2]]
+        for n, m in rd + (list(after[1]) if after else []):
+            if n in PSUM:
+                continue
+            for e in W.get(n, []):
+                if e[0] & m:
+                    need.append(e[1])
+        for n, m in wt:
+            if n in PSUM:
+                continue
+            for e in W.get(n, []):
+                if e[0] & m and not (rows and e[2] == rows):
+                    need.append(e[1])
+            for e in R.get(n, []):
+                if e[0] & m:
+                    need.append(e[1])
+        for n, m in rd + wt:
+            if n in PSUM:
+                need += [tk for q2, tk in X.get(n, {}).items() if q2 != q]
+        best = {}
+        for s, v, sn in need:
+            if s not in best or best[s][0] < v:
+                best[s] = (v, sn)
+        order = sorted(best.items(), key=lambda z: -len(z[1][1]))
+        for s, (v, sn) in order:
+            if know[q].get(s, 0) >= v:
+                continue
+            if any(s2 != s and sn2.get(s, 0) >= v and know[q].get(s2, 0) < v2 for s2, (v2, sn2) in order):
+                continue
+            eng[q].wait_ge(T.sem[s], v)
+            know[q][s] = max(know[q].get(s, 0), v)
+            for a, b in sn.items():
+                if know[q].get(a, 0) < b:
+                    know[q][a] = b
+        inst = fn()
+        if dma is None:
+            cnt[q] += 1
+            tok = (psem[q], cnt[q], dict(know[q]))
+            inst.then_inc(T.sem[psem[q]], 1)
+            total[psem[q]] = cnt[q]
+            mark = q
+        else:
+            tok = (dma[0], dma[1], dict(know[q])); total[dma[0]] = dma[1]; mark = "dma"
+            if dma[2]:
+                inst.then_inc(T.sem[dma[0]], 16)
+        for n, m in rd + wt:
+            if n in PSUM:
+                X.setdefault(n, {})[q] = tok
+        for n, m in wt:
+            if n not in PSUM:
+                W[n] = [(e[0] & ~m, e[1], e[2]) if not (rows and e[2] == rows) else e for e in W.get(n, []) if e[0] & ~m or (rows and e[2] == rows)] + [(m, tok, rows)]
+                R[n] = [(e[0] & ~m, e[1], e[2]) for e in R.get(n, []) if e[0] & ~m]
+        for n, m in rd:
+            if n not in PSUM:
+                R[n] = [e for e in R.get(n, []) if not (e[2] == mark and mark != "dma" and e[0] & ~m == 0)] + [(m, tok, mark)]
+        return tok
+
+    def dma(q, out, in_, accum=False, rows=None, after=None):
+        s = "d%d" % nd[0]; nd[0] += 1
+        if accum:
+            issue(q, lambda: eng[q].dma_start(out[0], in_[0], accum_op=O.add), [out], [in_], (s, 16, True), rows)
+        else:
+            issue(q, lambda: eng[q].dma_start(out[0], in_[0]), [out], [in_], (s, 16, True), rows, after)
+
+    def send(dst, out, in_, rsem, after=None):
+        s = "d%d" % nd[0]; nd[0] += 1
+        d = T.cores[dst % 4]
+        rid, pid, _ = topo.addr(d)
+        m = topo.mask(core, d)
+        issue("g", lambda: g.remote_dma(T[out[0]][:, 0:out[1]], in_[0], T.sem[rsem], T.sem[s], pid, rid, m), [], [in_], (s, len(topo.engines(core, d)), False), None, after)
+
+    def lands(out, rsem, src):
+        k = len(topo.engines(T.cores[src % 4], core))
+        total[rsem] = k
+        n, m = out[1][0]
+        W[n] = [(e[0] & ~m, e[1], e[2]) for e in W.get(n, []) if e[0] & ~m] + [(m, (rsem, k, {}), None)]
+
+    def ts(o, i, s1, op, s2=None, op2=None):
+        ins = [i] + [s for s in (s1, s2) if isinstance(s, tuple)]
+        a = s1[0] if isinstance(s1, tuple) else s1
+        b = s2[0] if isinstance(s2, tuple) else s2
+        if op2 is None:
+            issue("v", lambda: g.vector.tensor_scalar(o[0], i[0], a, None, op), [o], ins)
+        else:
+            issue("v", lambda: g.vector.tensor_scalar(o[0], i[0], a, b, op, op2), [o], ins)
+
+    def tt(o, a, b, op):
+        issue("v", lambda: g.vector.tensor_tensor(o[0], a[0], b[0], op), [o], [a, b])
+
+    def cp(o, i):
+        issue("v", lambda: g.vector.tensor_copy(o[0], i[0]), [o], [i])
+
+    def ms(o, x):
+        issue("v", lambda: g.vector.memset(o[0], x), [o], [])
+
+    def act(o, i, f=F.Identity, bias=0.0, scale=1.0, acc=None):
+        ins = [i] + ([bias] if isinstance(bias, tuple) else [])
+        b = bias[0] if isinstance(bias, tuple) else bias
+        if acc is None:
+            issue("c", lambda: g.scalar.activation(o[0], i[0], f, bias=b, scale=scale), [o], ins)
+        else:
+            issue("c", lambda: g.scalar.activation(o[0], i[0], f, bias=b, scale=scale, accum_out=acc[0]), [o, acc], ins)
+
+    def mm(o, l, x, start, stop):
+        issue("t", lambda: g.tensor.matmul(o[0], l[0], x[0], start, stop), [o], [l, x])
+
+    def iota(o, pat, base, cm, f=False):
+        if f:
+            issue("g", lambda: g.iota(o[0], pat, base, cm, allow_small_or_imprecise_dtypes=True), [o], [])
+        else:
+            issue("g", lambda: g.iota(o[0], pat, base, cm), [o], [])
+
+    def aff(o, i, pat, base, cm, op=O.is_ge):
+        issue("g", lambda: g.affine_select(o[0], i[0], pat, op, 0.0, base, cm), [o], [i])
+
+    def gat(q, o, w, l, add=None):
+        if q == "v":
+            if add is None:
+                cp(o, ind(w, l))
+            else:
+                ts(o, ind(w, l), add, O.add)
+        else:
+            act(o, ind(w, l), F.Identity, 0.0 if add is None else add)
+
+    def scan(o, d0, d1, init, o0, o1):
+        issue("v", lambda: g.vector.tensor_tensor_scan(o[0], d0[0], d1[0], init, o0, o1), [o], [d0, d1])
+
+    def trn(o, i):
+        issue("v", lambda: g.vector.transpose(o[0], i[0]), [o], [i])
+
+    def col(k):
+        return c("COL", k, k + 1)
+
+    def sel(z, a):
+        return c(z, 15 - a, 143 - a)
+
+    def stp(n, lo, hi, step):
+        return r(n, slice(None), slice(lo, hi, step))
+    A_ = slice(None)
+    SHR, AND = O.logical_shift_right, O.bitwise_and
+
+    dma("y", r("CI"), r("cx")); dma("c", r("TGL"), r("tg")); dma("y", c("V", 0, 4096), r("xr")); dma("g", c("YQ", 0, 256), r("qx"))
+    dma("y", r("XLH"), r("xl"))
+
+    iota(c("IP", 0, 1), [[1, 1]], 0, 1)
+    iota(r("NM"), [[1, 256]], 0, 256)
+    iota(r("J16"), [[1, 16]], 0, 0, True)
+    iota(r("I8"), [[16, 8]], 0, 0, True)
+    ms(r("ON128"), 1.0)
+    dma("y", r("LFH"), r("lf"), after=c("V", 0, 4096))
+    for j in range(4):
+        ts(c("DI", (5 + j) * 256, (6 + j) * 256), r("NM"), 3 * j, SHR, 7, AND)
+    ts(c("DG", 1280, 2304), c("DI", 1280, 2304), 0.0625, O.mult)
+    cp(r("CU"), r("CI"))
+    cp(c("CF", 0, 256), r("CI"))
+    ts(c("Q", 0, 256), c("YQ", 0, 256), 192.0, O.add)
+    for j in range(4):
+        ts(c("DI", j * 256, (j + 1) * 256), r("TGL"), 1 + 3 * j, SHR, 7, AND)
+    ts(c("DI", 1024, 1280), r("TGL"), 1, AND)
+    ts(c("DG", 0, 1280), c("DI", 0, 1280), 0.0625, O.mult)
+    aff(r("BO1"), r("ON128"), [[-16, 8], [0, 16]], 0, 1)
+    aff(r("BO"), r("BO1"), [[16, 8], [0, 16]], 15, -1)
+    aff(r("IDF"), r("ON128"), [[-1, 128]], 0, 1, O.is_equal)
+    aff(r("LTF"), r("BO"), [[1, 128]], -1, -1)
+    iota(r("NB"), [[1, 64]], 0, 64)
+    iota(r("PJ"), [[1, 8]], 0, 8)
+    iota(c("CB", 0, SUMV), [[16, SUMV]], 256, 0, True)
+    iota(c("CB", SUMV, 8), [[32, 8 - SUMV]], 32 * SUMV, 0, True)
+    for src, b, s in ((1, "XL0", "ax0"), (2, "XL1", "ax1"), (3, "XL2", "ax2"), (1, "U0", "af0"), (2, "U1", "af1"), (3, "U2", "af2"), (1, "LFF", "aff")):
+        lands(c(b, 0, 1024), s, rank + src)
+    for k, src in enumerate((1, 2, 1, 3, 2, 3)):
+        lands(r("E%d" % k), "ae%d" % k, rank + src)
+    iota(c("Q", 256, 384), [[0, 128]], 192, 0, True); iota(c("CF", 256, 384), [[0, 128]], 0, 0, True)
+    for k in range(3):
+        iota(c("LF%d" % k, 1024, 1152), [[0, 128]], 0, 0)
+        iota(c("XL%d" % k, 1024, 1152), [[0, 128]], 0, 0, True)
+    iota(c("DD", 256, 384), [[0, 128]], 0, 0, True)
+    iota(c("BA", 256, 384), [[0, 128]], 0, 0)
+    iota(r("DIG"), [[0, 1024]], 0, 0, True)
+    send(rank + 3, ("XL0", 1024), r("XLH"), "ax0")
+
+    def digits():
+        for f in (5, 6, 7, 8, 0, 1, 2, 3, 4):
+            dma("g", r("V", slice(f, None, 16), slice(0, 4096)), c("DG", f * 256, f * 256 + 256), True, rows="V")
+            if f == 0:
+                cp(r("HU"), r("LFH"))
+                send(rank + 3, ("U0", 1024), r("HU"), "af0")
+        send(rank + 2, ("U1", 1024), r("HU"), "af1", r("U0"))
+        send(rank + 2, ("XL1", 1024), r("XLH"), "ax1")
+    B24 = 16777216.0
+
+    def total_of(o, a, b):
+        tmp = c("TF4", 32, 32 + int(a[0].shape[1]))
+        tt(tmp, a, b, O.mult)
+        issue("v", lambda: g.vector.tensor_reduce(o[0], tmp[0], AxisListType.X, O.add), [o], [tmp])
+
+    def scaled(o, i, w):
+        if isinstance(w, tuple):
+            issue("c", lambda: g.scalar.activation(o[0], i[0], F.Copy, scale=w[0]), [o], [i, w])
+        else:
+            act(o, i, F.Copy, 0.0, float(w))
+
+    def zbuf(n, w):
+        scaled(stp(n, 15, 143, 16), stp("BO", 0, 128, 16), w)
+    ms(r("ZK"), 0.0)
+    scaled(r("ID"), r("IDF"), 1.0); scaled(r("NID"), r("IDF"), -1.0)
+    zbuf("ZK", 65536)
+
+    def consts():
+        ts(c("IP", 1, 2), c("IP", 0, 1), 15, AND)
+        ts(c("IP", 2, 3), c("IP", 0, 1), 4, SHR, 1, AND)
+        cp(col(0), c("IP", 1, 2)); cp(col(1), c("IP", 2, 3))
+        ts(col(20), col(1), B24, O.mult)
+        ts(col(21), col(1), -B24, O.mult, B24, O.add)
+        ts(col(24), col(0), 4096.0, O.mult)
+        tt(col(2), col(24), col(20), O.add); tt(col(3), col(24), col(21), O.add)
+        act(r("CE"), c("CF", 0, 256), F.Identity, col(2)); act(r("CO"), c("CF", 0, 256), F.Identity, col(3))
+        for n in ("ZKN", "ZT", "ZTN", "ZN", "Z1"):
+            ms(r(n), 0.0)
+        ts(c("TF4", 0, 16), r("J16"), col(0), O.is_equal)
+        ms(c("TF4", 16, 32), 0.5); ms(c("TF4", 64, 80), 0.0)
+        scan(c("POW", 0, 16), c("TF4", 16, 32), c("TF4", 64, 80), 65536.0, O.mult, O.add)
+        for j in range(4):
+            ms(c("POW", 16 + j, 17 + j), 16.0 * 8 ** j)
+        total_of(col(4), c("TF4", 0, 4), c("POW", 16, 20)); total_of(col(5), c("TF4", 5, 9), c("POW", 16, 20)); total_of(col(7), c("TF4", 0, 16), c("POW", 0, 16))
+        ts(col(6), c("TF4", 4, 5), -B24, O.mult)
+        ts(col(9), col(0), 5.0, O.is_ge); ts(col(10), col(0), 4.0, O.not_equal)
+        ts(c("COL", 11, 15), c("J16", 1, 5), c("TF4", 4, 5), O.mult, -0.0625, O.mult)
+        ts(c("COL", 15, 19), c("J16", 2, 6), c("TF4", 4, 5), O.mult, -0.0625, O.mult)
+        ts(col(19), col(4), -1.0, O.mult)
+        ms(r("RST"), 0.0); ms(stp("RST", 0, 512, 32), 67108864.0)
+        digits()
+        zbuf("ZN", col(5)); zbuf("ZT", col(4)); zbuf("ZTN", col(19)); zbuf("ZKN", -65536); zbuf("Z1", 0.0625)
+        for n, w in (("RN", col(5)), ("RE", col(6)), ("RL128", col(4)), ("RD", col(7)), ("RB", 65536.0)):
+            scaled(r(n), r("BO"), w)
+        scaled(r("KEEP"), r("IDF"), col(9)); scaled(r("K1"), r("IDF"), -16.0)
+        ts(c("CT2", 0, 16), c("POW", 0, 16), 2.0, O.mult)
+        for k in (16, 32, 64, 128):
+            cp(c("CT2", k, 2 * k), c("CT2", 0, k))
+        act(r("CT"), r("CT2"), F.Copy, -1048576.0)
+
+    def consts2():
+        ts(r("SW8"), r("I8"), col(0), O.add); ts(r("SC8"), r("SW8"), 0.5, O.add); ts(r("SW2"), r("SW8"), 2.0, O.mult)
+        ts(r("DSC"), r("SW8"), 4096.0, O.add); ts(r("DSM"), r("SW8"), 1152.0, O.add)
+        ms(r("ONE"), 1.0)
+
+    def pads():
+        for j in range(3):
+            ts(c("PJD", 8 * j, 8 * j + 8), r("PJ"), 3 * j, SHR, 7 if j < 2 else 1, AND)
+        ts(c("PD", 0, 24), r("PJD"), 0.0625, O.mult)
+        ms(c("PD", 24, 32), 0.125); ms(c("PD", 32, 40), 0.5)
+        for f, k in ((0, 0), (1, 1), (2, 2), (3, 3), (5, 0), (6, 1), (7, 2), (8, 4)):
+            dma("y", r("DD", slice(f, None, 16), slice(256, 384)), c("PD", 8 * k, 8 * k + 8), rows="DD")
+
+    def labels():
+        ts(r("NB"), r("NB"), 1023, AND)
+        for j in range(4):
+            ts(c("NBD", 64 * j, 64 * j + 64), r("NB"), 3 * j, SHR, 7, AND)
+        ts(c("NBB", 0, 256), r("NBD"), 0.0625, O.mult)
+        ms(c("NBB", 256, 320), 0.0625)
+        for f in range(5):
+            dma("y", r("DIG", slice(f, None, 16)), c("NBB", 64 * f, 64 * f + 64), rows="DIG")
+        act(c("V", 4096, 4224), c("DD", 256, 384))
+        tt(r("TRI"), r("LTF"), r("K1"), O.add)
+        for n in range(4):
+            scaled(r("TI%d" % n), r("IDF"), 32.0 * 8 ** n); scaled(r("TJ%d" % n), r("IDF"), -32.0 * 8 ** n)
+
+    pk = [0]
+
+    def sub(x, q, lo, u):
+        k = pk[0] % 4; pk[0] += 1
+        for ii in range(8):
+            o = c("ps%d" % k, ii * 64, ii * 64 + 64)
+            mm(o, r("NID"), c(q, lo, lo + 64), True, False)
+            mm(o, r("ID"), stp(x, 8 * u + ii, 1024, 16), False, True)
+        act(r("AB%d" % k), r("ps%d" % k), F.Abs)
+        return k
+
+    def sums(k, z, o, u, first, last):
+        for ii in range(8):
+            mm(o, sel(z, 8 * u + ii), c("AB%d" % k, ii * 64, ii * 64 + 64), first and u == 0 and ii == 0, last and u == 1 and ii == 7)
+
+    def tags(o, gx, xd):
+        for i in range(16):
+            mm(o, sel("ZT", i), stp(gx, i, 1024, 16), i == 0, False)
+            mm(o, sel("ZTN", i), stp(xd, i, 1024, 16), False, i == 15)
+
+    def earlier(eq, row, cols, nb, n):
+        for b in range(nb):
+            ts(r(eq, A_, b, slice(0, n - 16 * b)), c(row, 16 * b, n), c(cols, b, b + 1), O.is_equal)
+
+    def dup_compare(row, cols):
+        earlier("EQ2", row, cols, 8, 128)
+
+    def dup_count():
+        mm(c("PC", 0, 128), r("RD"), r("EQ2", A_, A_, slice(0, 16)), True, False)
+        for b in range(7):
+            mm(c("PC", 16 * b + 16, 128), r("RB"), r("EQ2", A_, b, slice(16, 128 - 16 * b)), False, b == 6)
+
+    def dup_flag(o):
+        tt(o, c("PC", 0, 128), c("CT2", 0, 128), O.is_ge)
+
+    def wrap(o, z, x):
+        for a in range(16):
+            mm(o, sel(z, a), stp(x, a, 128, 16), a == 0, a == 15)
+
+    def choice(t):
+        win = c("V", 0, 4096)
+
+        def take(k, a=0, b=64):
+            gat("v" if CHOICE[k] == "v" or k == late and a == 0 else "c", c("XG%d" % k, 16 * a, 16 * b), win, c("CU", 64 * k + a, 64 * k + b), 192.0)
+        order = [k for k in range(4) if CHOICE[k] == "v"] + [k for k in range(4) if CHOICE[k] != "v"]
+        late = order[-1]
+        for k in order:
+            if k != late:
+                take(k)
+        half = HALF if t else 64
+        take(late, 0, half)
+        if t:
+            claims1(t - 1)
+            disk_write(t - 1)
+            claims2(t - 1)
+        lag = None
+        for n, k in enumerate(order):
+            for u in range(2):
+                b = sub("XG%d" % k, "Q", 64 * k, u)
+                if n == 0 and u == 1 and half < 64:
+                    take(late, half)
+                if t and n == CEAT and u == 1:
+                    act(r("CE"), c("CF", 0, 256), F.Identity, col(2)); act(r("CO"), c("CF", 0, 256), F.Identity, col(3))
+                if lag:
+                    sums(*lag)
+                lag = (b, "ZK", c("PA", 64 * k, 64 * k + 64), u, True, True)
+                if t and n == CL2 and u == CU2:
+                    claims4(t - 1)
+            if t and n == CL1:
+                claims3(t - 1)
+        sums(*lag)
+        if t == 0:
+            consts()
+            consts2()
+        if t:
+            wrap(c("PC", 272, 280), "Z1", "FL")
+
+    def pick(t):
+        tt(r("KEY", A_, A_, slice(0, 16)), c("PA", 0, 256), r("CE"), O.add)
+        tt(r("KEY", A_, A_, slice(16, 32)), c("PA", 0, 256), r("CO"), O.add)
+        trn(r("KT"), r("KEY"))
+        scan(r("SCN"), r("RST"), r("KT"), 67108864.0, O.max, O.min)
+        cp(r("OI"), stp("SCN", 31, 512, 32))
+        ts(r("OI"), r("OI"), 4095, AND)
+        cp(r("OU"), r("OI"))
+        cp(r("OF"), r("OI"))
+        if t:
+            claims5(t - 1)
+        else:
+            pads()
+            dma("y", r("FD"), r("fd"), after=c("V", 0, 4096))
+        gat("c", r("VO"), c("V", 0, 4096), r("OU"), 192.0)
+        gat("v", r("XO"), c("V", 0, 4096), r("OU"), 192.0)
+        tt(c("DD", 0, 256), r("VO"), r("XO"), O.subtract)
+        mm(c("PR", 0, 256), r("RN"), c("DD", 0, 256), True, True)
+        mm(c("PC", 0, 256), r("RE"), c("DD", 0, 256), True, False)
+        for a in range(16):
+            mm(c("PT", 0, 16), sel("ZT", a), stp("DD", a, 256, 16), a == 0, a == 15)
+        cp(r("OR"), c("PR", 0, 256))
+        for b in range(16):
+            ts(r("EQ", A_, b, slice(0, 256 - 16 * b)), c("OR", 16 * b, 256), c("OF", b, b + 1), O.is_equal)
+            if b < 15:
+                mm(c("PC", 16 * b + 16, 256), r("RB"), r("EQ", A_, b, slice(16, 256 - 16 * b)), False, False)
+        mm(c("PC", 0, 256), r("RD"), r("EQ", A_, A_, slice(0, 16)), False, True)
+        tt(r("CA"), c("PC", 0, 256), r("CT"), O.is_lt)
+        scan(r("PX"), r("ONE"), r("CA"), 0.0, O.mult, O.add)
+        for b in range(SUMV):
+            act(c("JS", 0, 256 - 16 * b), c("PX", 16 * b, 256), F.Sign, c("SC8", b, b + 1), -1.0, c("LS", b, b + 1))
+        ts(r("T2"), c("PX", 255, 256), 2.0, O.mult)
+        for b in range(SUMV, 8):
+            ts(c("JV", 0, 256 - 16 * b), c("PX", 16 * b, 256), c("SC8", b, b + 1), O.is_le, 2.0, O.mult)
+            o, i = c("LS", b, b + 1), c("JV", 0, 256 - 16 * b)
+            issue("v", lambda: g.vector.tensor_reduce(o[0], i[0], AxisListType.X, O.add), [o], [i])
+        ts(r("RL"), r("SW2"), r("T2"), O.subtract, 0.0, O.max)
+        tt(r("CBP"), r("CB"), r("RL"), O.add)
+        ts(r("INV"), r("SW2"), r("T2"), O.is_ge, 8192.0, O.mult)
+        if t:
+            apply(2 * (t - 1), "LF%d" % (t % 3))
+        else:
+            cp(c("LF0", 0, 1024), r("U0"))
+        cp(r("NA"), c("PT", 0, 16))
+        gat("v", c("BA", 0, 256), c("LF%d" % (t % 3), 0, 1152), r("NA"))
+        tt(r("H8"), r("LS"), r("CBP"), O.add)
+        ts(r("LU"), r("H8"), 0.5, O.mult)
+        gat("v", r("BI"), r("BA"), r("LU"))
+        gat("c", r("CR"), r("CF"), r("LU"))
+        gat("c", r("QR"), r("Q"), r("LU"))
+        tt(r("SQ"), r("BI"), r("BI"), O.mult)
+        cp(r("CRU"), r("CR"))
+        gat("v", r("DDR"), r("DD"), r("LU"))
+        wrap(c("PR", 256, 264), "ZT", "DDR")
+
+    def translate(t):
+        LF, XL = "LF%d" % (t % 3), "XL%d" % (t % 3)
+        wrap(c("PC", 264, 272), "ZN", "DDR")
+        mm(c("PC", 0, 128), r("RL128"), r("DDR"), True, True)
+        ts(c("H", 0, 128), r("SQ"), 3, SHR)
+        ts(r("S5"), r("SQ"), 5, SHR)
+        ts(c("H", 128, 256), r("BI"), 37.0, O.mult, 1.0, O.add)
+        tt(c("H", 0, 128), c("H", 0, 128), r("BI"), O.add)
+        tt(c("H", 128, 256), c("H", 128, 256), r("S5"), O.add)
+        ts(r("H"), r("H"), 4095, AND)
+        cp(r("CCU"), r("H"))
+        for k in range(2):
+            gat("c", r("GS%d" % k), c("V", 0, 4096), c("CRU", 64 * k, 64 * k + 64))
+        blk = [(0, 0), (0, 1), (1, 0), (1, 1)]
+
+        def take(k):
+            lo = 128 * blk[k][1] + 64 * blk[k][0]
+            gat("v" if TRANS[k] == "v" else "c", r("XG%d" % k), c("V", 0, 4096), c("CCU", lo, lo + 64))
+
+        def plain(k):
+            ts(r("XD%d" % k), r("XG%d" % k), 192.0, O.add)
+
+        def subs(k):
+            return [sub("XD%d" % k, "QR", 64 * blk[k][0], u) for u in range(2)]
+        bank = [("PC", 128, "PR", 384), ("PT", 0, "PA", 256)]
+
+        def flush(x):
+            k, bs, pos = x
+            hs, w = blk[k]
+            bt, t0, ba, a0 = bank[hs]
+            tags(c(bt, t0 + 64 * w, t0 + 64 * w + 64), "XG%d" % k, "XD%d" % k)
+            for u in range(2):
+                sums(bs[u], "ZK" if w else "ZKN", c(ba, a0, a0 + 64), u, pos == 0, pos == 1)
+
+        def decide(hs):
+            bt, t0, ba, a0 = bank[hs]
+            lo, hi = 64 * hs, 64 * hs + 64
+            for w in range(2):
+                tt(c("IN", 128 * w + lo, 128 * w + hi), c(bt, t0 + 64 * w, t0 + 64 * w + 64), c("BS", lo, hi), O.is_equal)
+            ts(c("INB", lo, hi), c("IN", lo, hi), 33554432.0, O.mult)
+            tt(c("M2", lo, hi), c(ba, a0, a0 + 64), c("IN", 128 + lo, 128 + hi), O.max)
+            tt(c("SEL", lo, hi), c("M2", lo, hi), c("INB", lo, hi), O.is_gt)
+            tt(c("SEL", lo, hi), c("SEL", lo, hi), c("D12", lo, hi), O.mult)
+            tt(c("SS", lo, hi), c("SEL", lo, hi), c("H", lo, hi), O.add)
+            if hs == 0:
+                claim_keys(lo, hi)
+            cp(ind(r("FW"), c("OUR", 4 * hs, 4 * hs + 4)), c("SS", lo, hi))
+        take(0); plain(0)
+        cp(r("NU"), c("PR", 256, 264))
+        cp(r("OUR"), c("PC", 264, 272))
+        cp(r("NR"), c("PC", 0, 128))
+        take(1)
+        b0 = subs(0)
+        plain(1)
+        take(2); take(3)
+        b1 = subs(1)
+        gat("c", r("A"), r(XL), r("NU"))
+        flush((0, b0, 0))
+        plain(2)
+        b2 = subs(2)
+        flush((1, b1, 1))
+        plain(3)
+        lag = [(3, subs(3), 1)]
+        flush((2, b2, 0))
+        cp(r("WNF"), r("NU"))
+        tt(r("D12"), c("H", 128, 256), c("H", 0, 128), O.subtract)
+        ts(r("BS"), r("BI"), -1797120.0, O.add)
+        for k in range(2):
+            ts(r("SX%d" % k), r("GS%d" % k), 192.0, O.add)
+        if t == 0:
+            labels()
+            ts(c("FW", 0, 2048), r("FD"), 4095, AND)
+            ts(c("FW", 2048, 4096), r("FD"), 12, SHR)
+        ts(r("DDM"), r("DDR"), col(10), O.mult, col(11 + t), O.add)
+        tt(r("VL"), r("A"), r("DDM"), O.add)
+        cp(ind(r("V"), r("OUR")), r("VL"))
+        tt(r("QF"), ind(c("V", 0, 4096), r("OU")), c("Q", 0, 256), O.add)
+        ts(c("Q", 0, 256), r("QF"), 0.5, O.mult, 95.75, O.add)
+        cp(r("NI"), r("NU"))
+        ts(r("N1"), r("NI"), 1, AND)
+        ts(r("N1"), r("N1"), -2.0, O.mult, 1.0, O.add)
+        tt(r("NI"), r("NI"), r("N1"), O.add)
+        decide(0)
+        if t == 1:
+            cp(c("LF2", 0, 1024), r("U2"))
+            apply(1, "LF2")
+        if t == 2:
+            apply(3, "LF0")
+        dup_compare("NR", "WNF")
+        flush(lag.pop())
+        dup_count()
+        decide(1)
+        if t == STEPS - 1:
+            dup_flag(r("FL"))
+            wrap(c("PC", 272, 280), "Z1", "FL")
+            claim_order()
+        for k in range(2):
+            tags(c("PT", 256 + 64 * k, 320 + 64 * k), "GS%d" % k, "SX%d" % k)
+        cp(c("CF", 0, 256), ind(c("FW", 0, 4096), r("OU")))
+        if t < STEPS - 1:
+            cp(r("CU"), c("CF", 0, 256))
+
+    def claim_keys(lo, hi):
+        tt(c("N12", lo, hi), c("IN", lo, hi), c("IN", 128 + lo, 128 + hi), O.max)
+        ts(c("NEW", lo, hi), c("N12", lo, hi), -1.0, O.mult, 1.0, O.add)
+        ts(c("K1", lo, hi), c("SS", lo, hi), 1024.0, O.mult)
+        tt(c("KK", lo, hi), c("K1", lo, hi), c("BI", lo, hi), O.add)
+
+    def disk_write(t):
+        act(c("SF", 0, 128), c("PT", 256, 384), F.Identity, 1797120.0)
+        tt(r("MF"), c("PC", 272, 280), r("DSM"), O.mult)
+        tt(c("SF", 128, 136), r("MF"), r("NI"), O.max)
+        for dst, k in (((3, 0), (2, 1)), ((3, 2), (1, 3)), ((2, 4),), ((1, 5),))[t]:
+            send(rank + dst, ("E%d" % k, 136), r("SF"), "ae%d" % k)
+        if t == 0:
+            send(rank + 1, ("U2", 1024), r("HU"), "af2")
+            send(rank + 1, ("XL2", 1024), r("XLH"), "ax2")
+        if t in (0, 2):
+            cp(r("MU"), c("SF", 128, 136))
+            cp(ind(r("LF%d" % t), r("MU")), c("SF", 0, 128))
+        if t == 2:
+            send(rank + 3, ("LFF", 1024), c("LF2", 0, 1024), "aff")
+
+    def apply(k, n):
+        cp(r("MX"), c("E%d" % k, 128, 136))
+        cp(ind(r(n), r("MX")), c("E%d" % k, 0, 128))
+
+    def claims1(t):
+        if t < STEPS - 1:
+            dup_flag(r("FL"))
+            wrap(c("PC", 272, 280), "Z1", "FL")
+            claim_order()
+
+    def claim_order():
+        claim_keys(64, 128)
+        mm(c("PC", 384, 512), r("TRI"), r("NEW"), True, True)
+        act(r("KKE"), r("KK"), F.Identity, col(20)); act(r("KKO"), r("KK"), F.Identity, col(21))
+
+    def claims2(t):
+        ts(r("PEN"), c("PC", 384, 512), -16.0, O.is_gt, B24, O.mult)
+        tt(r("KEC", A_, A_, slice(0, 16)), r("PEN"), r("KKE"), O.add)
+        tt(r("KEC", A_, A_, slice(16, 32)), r("PEN"), r("KKO"), O.add)
+        trn(r("KTC"), r("KEC"))
+        scan(r("SNC"), c("RST", 0, 256), r("KTC"), 67108864.0, O.max, O.min)
+        cp(r("KI"), stp("SNC", 31, 256, 32))
+        ts(r("PI"), r("KI"), 10, SHR)
+        ts(r("BW"), r("KI"), 1023, AND)
+        tt(r("PF"), r("PI"), r("INV"), O.max)
+        tt(r("PF"), r("PF"), r("DSC"), O.min)
+        cp(r("PU"), r("PF"))
+        cp(r("BU"), r("BW"))
+        gat("v", r("GP"), r("V"), r("PU"), 192.0)
+        gat("v", r("XP"), r("V"), r("PU"), 192.0)
+        gat("v", r("DB"), r("DIG"), r("BU"))
+        tt(r("DP"), r("GP"), r("XP"), O.subtract)
+        ts(r("ZC"), r("DP"), -(t + 1) / 16.0, O.is_equal, col(15 + t), O.mult)
+
+    def claims3(t):
+        mm(c("PR", 0, 128), r("RN"), r("DP"), True, True)
+        o = c("PT", 384, 512)
+        mm(o, r("ID"), r("XP"), True, False); mm(o, r("KEEP"), r("DP"), False, False)
+        mm(o, r("ID"), r("DB"), False, False); mm(o, r("ID"), r("ZC"), False, True)
+        if t == 0:
+            cp(c("LF1", 0, 1024), r("U1"))
+        cp(r("PLR"), c("PR", 0, 128))
+        dup_compare("PLR", "PF")
+        ts(r("NV"), o, -192.0, O.add)
+
+    def claims4(t):
+        dup_count()
+        dup_flag(r("FL"))
+
+    def claims5(t):
+        tt(r("FS"), c("PC", 272, 280), r("DSC"), O.mult)
+        tt(r("P2"), r("FS"), r("PF"), O.max)
+        cp(r("PU2"), r("P2"))
+        cp(ind(r("V"), r("PU2")), r("NV"))
+
+    for t in range(STEPS):
+        choice(t)
+        pick(t)
+        translate(t)
+    claims1(STEPS - 1)
+    dma("y", r("yc"), c("CF", 0, 256))
+    disk_write(STEPS - 1)
+    claims2(STEPS - 1)
+    ts(r("YQ"), c("Q", 0, 256), -192.0, O.add)
+    dma("y", r("yq"), r("YQ"))
+    claims3(STEPS - 1); claims4(STEPS - 1)
+    wrap(c("PC", 272, 280), "Z1", "FL")
+    claims5(STEPS - 1)
+    for n in range(5):
+        dma("y" if n % 2 else "c", c("TX", 256 * n, 256 * n + 256), r("V", slice(n, None, 16), slice(0, 4096)))
+    cp(c("YL", 0, 1024), c("LFF", 0, 1024))
+    apply(5, "YL")
+    dma("y", r("yl"), c("YL", 0, 1024))
+    ts(r("TD"), r("TX"), 192.0, O.add)
+    for n in range(4):
+        mm(c("PT", 0, 256), r("TI%d" % n), c("TX", 256 * n, 256 * n + 256), n == 0, False)
+        mm(c("PT", 0, 256), r("TJ%d" % n), c("TD", 256 * n, 256 * n + 256), False, n == 3)
+    act(r("TE"), c("TX", 1024, 1280), F.Identity, 192.0625)
+    tt(r("TE2"), r("TE"), c("TD", 1024, 1280), O.subtract)
+    ts(r("TE2"), r("TE2"), 0.125, O.is_equal, 3594240.0, O.add)
+    tt(r("TY"), c("PT", 0, 256), r("TE2"), O.add)
+    dma("c", r("yt"), r("TY"))
+    for s in sorted(total):
+        g.wait_ge(T.sem[s], total[s])

@@ -2,12 +2,13 @@ import numpy as np
 from concourse.mybir import AluOpType as O, AxisListType, ActivationFunctionType as F
 
 STEPS = 4
-CHOICE = "svss"
-CL1, CL2, CU2 = 2, 3, 1
-TRANS = "vsvs"
-CEAT = 1
-HALF = 32
-SUMV = 7
+CHOICE0 = ((192, 256, "c"), (128, 192, "v"), (64, 128, "v"), (32, 64, "c"), (0, 32, "v"))
+CHOICE = ((192, 256, "c"), (128, 192, "v"), (64, 128, "c"), (32, 64, "c"), (0, 32, "v"))
+TRANS = ((0, 0, 64, "v"), (0, 64, 128, "c"), (1, 0, 64, "v"), (1, 64, 96, "c"), (1, 96, 128, "v"))
+PARTS = ((64, 256), (0, 64))
+POOLS = {"s": 3, "x": 5}
+SLACK, ROUNDS = 100, 6
+CYC, PE, WAKE, GAT, SCA, DMA0, DMAB, REM0, REMB = 0.83, 0.417, 190, 1.56, 3.8, 1200, 0.004, 1500, 0.02
 
 
 def _scratch():
@@ -16,54 +17,42 @@ def _scratch():
     def sb(n, w, d="float32"):
         S[n] = ("sbuf", [128] + (w if isinstance(w, list) else [w]), d)
     B, I, U = "bfloat16", "int32", "uint16"
-    sb("V", 4224, B); sb("FW", 4224, I); sb("FD", 2048, I)
-    for k in range(6):
+    sb("V", 4224, B); sb("DG", 4224, B); sb("FW", 4224, I); sb("FD", 2048, I); sb("NAME", 4096)
+    for k in (0, 2, 3, 4, 5):
         sb("E%d" % k, 136)
-    sb("LFF", 1280, I); sb("LFH", 1024, I); sb("YL", 1280); sb("MX", 8, U)
+    sb("LFH", 1024, I); sb("LFS", 1024); sb("YL", 1152); sb("XLH", 1024, B)
     for k in range(3):
-        sb("LF%d" % k, 1280, I); sb("U%d" % k, 1024, U)
-        sb("XL%d" % k, 1152, B)
-    sb("XLH", 1024, B); sb("HU", 1024, U)
-    sb("CI", 256, I); sb("CF", 384); sb("CU", 256, U); sb("Q", 384, B); sb("CE", [16, 16]); sb("CO", [16, 16])
-    for k in range(4):
-        sb("XG%d" % k, 1024, B); sb("XD%d" % k, 1024, B); sb("AB%d" % k, 512, B)
-    for k in range(2):
-        sb("GS%d" % k, 1024, B); sb("SX%d" % k, 1024, B)
+        sb("LF%d" % k, 1152); sb("XL%d" % k, 1024, B)
+    sb("CI", 256, I); sb("CF", 272); sb("CU", 256, U); sb("Q", 272, B); sb("CE", [16, 16]); sb("CO", [16, 16])
+    sb("XG", 4096, B); sb("XD", 4096, B); sb("AB", [32, 128], B); sb("GS", 2048, B)
     sb("KEY", [16, 32]); sb("KT", 512); sb("SCN", 512); sb("RST", 512)
-    sb("OI", 16, I); sb("OF", 16); sb("OU", 16, U)
-    sb("VO", 256); sb("XO", 256, B); sb("DD", 384, B); sb("OR", 256, U); sb("EQ", [16, 272], B); sb("CA", 256); sb("PX", 256)
-    sb("ONE", 256); sb("JS", 256, B); sb("JV", 256, B); sb("LS", 8); sb("T2", 1); sb("RL", 8); sb("CBP", 8); sb("INV", 8); sb("H8", 8); sb("LU", 8, U)
-    sb("DDR", 128, B); sb("CR", 128); sb("CRU", 128, U); sb("QR", 128, B)
-    sb("WNF", 8); sb("NU", 8, U); sb("OUR", 8, U); sb("NR", 128, U); sb("A", 128, B); sb("BI", 128, I); sb("BS", 128)
-    sb("SQ", 128, I); sb("S5", 128, I); sb("H", 256, I); sb("CCU", 256, U); sb("D12", 128)
-    sb("IN", 256, B); sb("INB", 128); sb("M2", 128); sb("SEL", 128); sb("SS", 128, I); sb("N12", 128, B); sb("NEW", 128, B)
-    sb("K1", 128); sb("KK", 128); sb("KKE", [8, 16]); sb("KKO", [8, 16]); sb("PEN", [8, 16]); sb("KEC", [8, 32]); sb("KTC", 256); sb("SNC", 256)
+    sb("OI", 16, I); sb("OF", 16); sb("OU", 16, U); sb("DD", 272, B); sb("OR", 256, U); sb("EQ", [16, 256], B)
+    sb("NA", 16, U); sb("Y", 512); sb("HI", 512, I); sb("H1", 272, I); sb("H2", 272, I)
+    sb("CA", 256, B); sb("PX", 304, B); sb("ONE", 256, B); sb("JS", [4, 304], B); sb("JV", 768, B); sb("SV", 768, B); sb("RS2", 768, B)
+    sb("LS", 4); sb("LU", 8, U); sb("CCU", 256, U); sb("QR", 128, B); sb("DDR", 128, B); sb("DDM", 128, B); sb("DDE", 128, B); sb("CRU", 128, U)
+    sb("NU", 8, U); sb("OUF", 8); sb("OUR", 8, U); sb("A", 128, B); sb("BF", 128); sb("CC", 256); sb("D12", 128)
+    sb("IN", 256, B); sb("SEL", 128, B); sb("SD", 128); sb("SS", 128); sb("NEW", 128, B); sb("XO", 256, B)
+    sb("KE", [8, 16]); sb("KO", [8, 16]); sb("KEC", [8, 32]); sb("KTC", 256); sb("SNC", 256)
     sb("KI", 8, I); sb("PI", 8, I); sb("BW", 8, I); sb("BU", 8, U); sb("PF", 8); sb("PU", 8, U); sb("P2", 8); sb("PU2", 8, U)
-    sb("GP", 128); sb("XP", 128, B); sb("DP", 128, B); sb("DB", 128, B); sb("ZC", 128, B); sb("NV", 128, B); sb("PLR", 128, U)
-    sb("EQ2", [8, 144], B); sb("FL", 128, B); sb("FS", 8)
-    sb("VL", 128, B); sb("QF", 256); sb("SF", 136); sb("BA", 384, I); sb("NA", 16, U)
-    sb("NI", 8, I); sb("N1", 8, I); sb("MF", 8); sb("MU", 8, U)
-    sb("YQ", 256, B); sb("TX", 5 * 256, B); sb("TD", 5 * 256, B); sb("TE", 256); sb("TE2", 256); sb("TY", 256); sb("TW", 256)
-    sb("COL", 64); sb("IP", 4, I); sb("BO", 128); sb("BO1", 128); sb("TF4", 80)
-    for n in ("ZK", "ZKN", "ZT", "ZTN", "ZN", "Z1"):
-        sb(n, 144, B)
-    for n in ("ID", "NID", "RN", "RE", "RL128", "RD", "RB", "KEEP", "TRI"):
+    sb("NMP", 128, B); sb("XP", 128, B); sb("DB", 128, B); sb("NV", 128, B); sb("EQ2", [8, 128], B); sb("EQ3", [8, 128], B); sb("FL", 128, B); sb("FM", 128, B)
+    sb("SF", 136); sb("MU", 8, U); sb("MX", 8, U); sb("YQ", 256, B); sb("QX", 256, B); sb("TY", 256)
+    sb("COL", 48); sb("IP", 4, I); sb("BO", 128); sb("BO1", 128); sb("OH", 16); sb("TF", 48); sb("POW", 16)
+    sb("ZZ", 6 * 144, B); sb("WN", 16, B)
+    for n in ("ID", "NID", "HID", "DB1", "DB2", "RN", "RE", "RL", "RD", "RB", "RI", "TRI", "ONB", "KP", "ZR"):
         sb(n, 128, B)
-    for n in range(5):
-        sb("TI%d" % n, 128, B); sb("TJ%d" % n, 128, B)
-    sb("ON128", 128); sb("IDF", 128); sb("LTF", 128); sb("J16", 16); sb("POW", 20); sb("DDM", 128, B); sb("CT", 256); sb("CT2", 256)
-    sb("SC8", 8); sb("SW8", 8); sb("SW2", 8); sb("DSC", 8); sb("DSM", 8); sb("CB", 8); sb("I8", 8)
-    sb("TGL", 256, I); sb("NM", 256, I); sb("DI", 9 * 256, I); sb("DG", 9 * 256, B)
-    sb("NB", 64, I); sb("NBD", 256, I); sb("NBB", 320, B); sb("DIG", 1024, B); sb("PJ", 8, I); sb("PJD", 24, I); sb("PD", 40, B)
-    for n in ("ps0", "ps1", "ps2", "ps3", "PA", "PT", "PR", "PC"):
-        S[n] = ("psum", [128, 512], "float32")
+    sb("ON128", 128); sb("IDF", 128); sb("NIF", 128); sb("LTF", 128); sb("J16", 16); sb("CT", 256); sb("CT2", 256)
+    sb("SC8", 8); sb("DSC", 8); sb("DSM", 8); sb("I8", 8)
+    sb("TGL", 256, I); sb("DI", 1280, I); sb("DS", 7 * 256, B)
+    sb("NB", 64, I); sb("NBD", 256, I); sb("NBB", 320, B); sb("DIG", 1024, B); sb("J128", 128, B)
+    for n in range(8):
+        S["ps%d" % n] = ("psum", [128, 512], "float32")
     return S
 
 
 def _pack(S):
     real, virt, width = {}, {}, {}
     for n, (where, sh, d) in S.items():
-        if where == "psum" or len(sh) > 2 or sh[1] > 400 or n in ("E0", "E1", "E2", "E3", "E4", "E5"):
+        if where == "psum" or len(sh) > 2 or sh[1] > 400 or n[0] == "E" and n[1:].isdigit():
             real[n] = (where, sh, d)
         else:
             unit = 8 if d in ("float32", "int32") else 16
@@ -77,10 +66,136 @@ def _pack(S):
 
 ALL = _scratch()
 SCRATCH, VIRT = _pack(ALL)
-ARR = ["ax0", "ax1", "ax2", "af0", "af1", "af2", "aff"] + ["ae%d" % k for k in range(6)]
-SEMAPHORES = ["pv", "pc", "pt", "pg"] + ARR + ["d%d" % k for k in range(70)]
-PSUM = ("ps0", "ps1", "ps2", "ps3", "PA", "PT", "PR", "PC")
+ARR = ["ax0", "ax1", "ax2", "af0", "af1", "af2", "aff", "ae0", "ae2", "ae3", "ae4", "ae5"]
+SEMAPHORES = ["pv", "pc", "pt", "pg"] + ARR + ["d%d" % k for k in range(60)]
 MASKS = {}
+PLAN = []
+ZK, ZT, ZN, ZM, ZY, Z1 = range(6)
+
+
+def first_order(ops, tiles):
+    n = len(ops)
+    succ = [[] for _ in ops]
+    for k, o in enumerate(ops):
+        for p, w in o["pre"].items():
+            succ[p].append((k, w))
+    tail = [0.0] * n
+    for k in range(n - 1, -1, -1):
+        tail[k] = ops[k]["lat"] + max([tail[s] + (WAKE if w else 0) for s, w in succ[k]] + [0])
+    left = [len(o["pre"]) for o in ops]
+    ready = [0.0] * n
+    avail = {q: [] for q in "vctgyn"}
+    for k in range(n):
+        if not left[k]:
+            avail[ops[k]["q"]].append(k)
+    free = {q: 0.0 for q in avail}
+    begin, end = [0.0] * n, [0.0] * n
+    banks, at = {}, 0
+    for p, m in POOLS.items():
+        banks[p] = [[at + j, None] for j in range(m)]; at += m
+    nxt = {p: 0 for p in POOLS}
+    todo = [len(t["ops"]) for t in tiles]
+    bank, after, order = {}, {}, []
+
+    def start(k):
+        s = max(free[ops[k]["q"]], ready[k]) if ops[k]["q"] != "n" else ready[k]
+        tl = ops[k].get("opens")
+        if tl is None:
+            return s, None
+        t = tiles[tl]
+        if t["pool"] == "s" and t["nth"] != nxt["s"]:
+            return None, None
+        best = None
+        for b in banks[t["pool"]]:
+            if b[1] is None or todo[b[1]] == 0:
+                e = 0.0 if b[1] is None else max(end[x] for x in tiles[b[1]]["ops"]) + WAKE
+                if best is None or e < best[0]:
+                    best = (e, b)
+        return (None, None) if best is None else (max(s, best[0]), best[1])
+    while len(order) < n:
+        pick = None
+        for q in avail:
+            cand = [(k,) + start(k) for k in avail[q]]
+            cand = [x for x in cand if x[1] is not None]
+            if not cand:
+                continue
+            cand.sort(key=lambda x: (-tail[x[0]], x[0]))
+            best = cand[0]
+            for x in cand[1:]:
+                if x[1] < best[1]:
+                    first = max(x[1] + tail[x[0]], max(best[1], x[1] + ops[x[0]]["busy"]) + tail[best[0]])
+                    second = max(best[1] + tail[best[0]], best[1] + ops[best[0]]["busy"] + tail[x[0]])
+                    if first <= second + SLACK:
+                        best = x
+            if pick is None or best[1] < pick[1]:
+                pick = best
+        k, s, b = pick
+        o = ops[k]
+        if b is not None:
+            tl = o["opens"]
+            if b[1] is not None:
+                after[k] = list(tiles[b[1]]["ops"])
+            b[1] = tl; bank[tl] = b[0]; nxt[tiles[tl]["pool"]] += 1
+        for tl in o["tiles"]:
+            todo[tl] -= 1
+        avail[o["q"]].remove(k)
+        free[o["q"]] = s + o["busy"]; begin[k] = s; end[k] = s + o["lat"]
+        if "wire" in o:
+            end[k] = free[o["wire"][0]] = max(end[k], free.get(o["wire"][0], 0.0) + o["wire"][1])
+        order.append(k)
+        for x, w in succ[k]:
+            ready[x] = max(ready[x], end[k] + WAKE if w else s + o["busy"])
+            left[x] -= 1
+            if not left[x]:
+                avail[ops[x]["q"]].append(x)
+    return order, bank, after, max(end)
+
+
+def gap(line, t, d):
+    j = len(line)
+    while j and line[j - 1][1] > t:
+        j -= 1
+    while j < len(line) and line[j][0] < t + d:
+        t = max(t, line[j][1]); j += 1
+    line.insert(j, (t, t + d))
+    return t
+
+
+def plan(ops, tiles):
+    order, bank, after, span = first_order(ops, tiles)
+    pre = [dict(o["pre"]) for o in ops]
+    for k, l in after.items():
+        for x in l:
+            pre[k][x] = pre[k].get(x, False) or ops[x]["q"] != "t"
+    succ = [{} for _ in ops]
+    for k, d in enumerate(pre):
+        for x, w in d.items():
+            succ[x][k] = w
+    best, now = (span, order), order
+    for _ in range(ROUNDS):
+        lines, late = {}, {}
+        for k in reversed(now):
+            o = ops[k]
+            e = max([late[x] + WAKE for x, w in succ[k].items() if w] + [0.0])
+            if "wire" in o:
+                e = gap(lines.setdefault(o["wire"][0], []), e, o["wire"][1])
+            e = max([e + o["lat"] - o["busy"]] + [late[x] for x, w in succ[k].items() if not w])
+            late[k] = (gap(lines.setdefault(o["q"], []), e, o["busy"]) if o["busy"] else e) + o["busy"]
+        pos = {k: j for j, k in enumerate(now)}
+        now = sorted(now, key=lambda k: (-late[k], pos[k]))
+        lines, begin, end = {}, {}, {}
+        for k in now:
+            o = ops[k]
+            s = max([end[x] + WAKE if w else begin[x] + ops[x]["busy"] for x, w in pre[k].items()] + [0.0])
+            begin[k] = gap(lines.setdefault(o["q"], []), s, o["busy"]) if o["busy"] else s
+            end[k] = begin[k] + o["lat"]
+            if "wire" in o:
+                end[k] = gap(lines.setdefault(o["wire"][0], []), end[k] - o["wire"][1], o["wire"][1]) + o["wire"][1]
+        pos = {k: j for j, k in enumerate(now)}
+        now = sorted(now, key=lambda k: (begin[k], pos[k]))
+        if max(end.values()) < best[0]:
+            best = (max(end.values()), now)
+    return best[1], bank, after
 
 
 def rank_program(g, core, T, topo):
@@ -89,645 +204,477 @@ def rank_program(g, core, T, topo):
         return
     eng = {"v": g.vector, "c": g.scalar, "t": g.tensor, "g": g, "y": g.sync}
     psem = {"v": "pv", "c": "pc", "t": "pt", "g": "pg"}
-    cnt = {"v": 0, "c": 0, "t": 0, "g": 0}
-    know = {q: {} for q in eng}
-    W, R, X = {}, {}, {}
-    total = {}
+    ops, tiles, bank = [], [], {}
+    W, R = {}, {}
     nd = [0]
+    A_ = slice(None)
 
     def r(name, *idx):
         key = (name, str(idx))
         if key not in MASKS:
-            if name in ALL and ALL[name][0] == "sbuf":
+            if name in ALL:
                 sh = ALL[name][1][1:]
                 n = int(np.prod(sh)); f = np.zeros(n, np.uint8)
                 f[np.arange(n).reshape(sh)[tuple(idx[1:])].reshape(-1)] = 1
-                MASKS[key] = int.from_bytes(np.packbits(f, bitorder="little").tobytes(), "little")
+                MASKS[key] = (int.from_bytes(np.packbits(f, bitorder="little").tobytes(), "little"), int(f.sum()))
             else:
-                MASKS[key] = 1
+                MASKS[key] = (1, int(np.prod(T[name].shape)) // 128)
+        m, n = MASKS[key]
         if name in VIRT:
             arena, at, w = VIRT[name]
             cs = idx[1] if len(idx) > 1 else slice(0, w)
             lo, hi, st = cs.indices(w)
-            return (T[arena][idx[0] if idx else slice(None), at + lo:at + hi:st], ((name, MASKS[key]),))
-        t = T[name]
-        return (t[idx] if idx else t[:], ((name, MASKS[key]),))
+            ap = T[arena][idx[0] if idx else A_, at + lo:at + hi:st]
+        else:
+            ap = T[name][idx] if idx else T[name][:]
+        size = 2 if (ALL[name][2] if name in ALL else name) in ("bfloat16", "uint16", "xr", "xl", "qx", "yq") else 4
+        return dict(ap=lambda: ap, n=n, size=size, use=[(name, m)], tile=None, ind=False)
 
-    def c(name, a, b):
-        return r(name, slice(None), slice(a, b))
+    def c(name, a, b, step=1):
+        return r(name, A_, slice(a, b, step))
+
+    def tile(pool="x"):
+        tiles.append(dict(pool=pool, ops=[], phase=[], nth=None))
+        return len(tiles) - 1
+
+    def p(tl, a, b, step=1):
+        return dict(ap=lambda: T["ps%d" % bank[tl]][:, a:b:step], n=len(range(a, b, step)), size=4, use=[], tile=tl, ind=False)
 
     def ind(w, o):
-        return (w[0].indirect(o[0]), w[1] + o[1], w[1])
+        return dict(ap=lambda: w["ap"]().indirect(o["ap"]()), n=16 * o["n"], size=w["size"], use=w["use"], off=o["use"], tile=None, ind=True)
 
-    def issue(q, fn, outs, ins, dma=None, rows=None, after=None):
-        need = []
-        rd = [x for o in ins for x in o[1]]
-        wt = [x for o in outs for x in (o[2] if len(o) > 2 else o[1])]
-        for o in outs:
-            if len(o) > 2:
-                rd += [x for x in o[1] if x not in o[2]]
-        for n, m in rd + (list(after[1]) if after else []):
-            if n in PSUM:
-                continue
+    def record(q, fns, outs, ins, busy, lat=None, dma=None, rows=None, after=()):
+        k = len(ops)
+        pre = {x: True for x in after}
+        rd = [x for o in ins for x in o["use"]] + [x for o in ins + outs for x in o.get("off", [])]
+        wt = [x for o in outs for x in o["use"]]
+        for n, m in rd:
             for e in W.get(n, []):
                 if e[0] & m:
-                    need.append(e[1])
+                    pre[e[1]] = True
         for n, m in wt:
-            if n in PSUM:
-                continue
             for e in W.get(n, []):
                 if e[0] & m and not (rows and e[2] == rows):
-                    need.append(e[1])
+                    pre[e[1]] = True
             for e in R.get(n, []):
                 if e[0] & m:
-                    need.append(e[1])
-        for n, m in rd + wt:
-            if n in PSUM:
-                need += [tk for q2, tk in X.get(n, {}).items() if q2 != q]
-        best = {}
-        for s, v, sn in need:
-            if s not in best or best[s][0] < v:
-                best[s] = (v, sn)
-        order = sorted(best.items(), key=lambda z: -len(z[1][1]))
-        for s, (v, sn) in order:
-            if know[q].get(s, 0) >= v:
-                continue
-            if any(s2 != s and sn2.get(s, 0) >= v and know[q].get(s2, 0) < v2 for s2, (v2, sn2) in order):
-                continue
-            eng[q].wait_ge(T.sem[s], v)
-            know[q][s] = max(know[q].get(s, 0), v)
-            for a, b in sn.items():
-                if know[q].get(a, 0) < b:
-                    know[q][a] = b
-        inst = fn()
-        if dma is None:
-            cnt[q] += 1
-            tok = (psem[q], cnt[q], dict(know[q]))
-            inst.then_inc(T.sem[psem[q]], 1)
-            total[psem[q]] = cnt[q]
-            mark = q
-        else:
-            tok = (dma[0], dma[1], dict(know[q])); total[dma[0]] = dma[1]; mark = "dma"
-            if dma[2]:
-                inst.then_inc(T.sem[dma[0]], 16)
-        for n, m in rd + wt:
-            if n in PSUM:
-                X.setdefault(n, {})[q] = tok
+                    pre[e[1]] = True
+        op = dict(q=q, fns=fns, pre=pre, busy=busy, lat=busy if lat is None else lat, dma=dma, tiles=sorted({o["tile"] for o in ins + outs if o["tile"] is not None}))
+        for tl in op["tiles"]:
+            t = tiles[tl]
+            if not t["ops"]:
+                op["opens"] = tl
+                t["nth"] = sum(1 for x in tiles if x["pool"] == t["pool"] and x["nth"] is not None)
+            if t["phase"] and ops[t["phase"][0]]["q"] != q:
+                t["before"] = t["phase"]; t["phase"] = []
+            for x in t.get("before", []):
+                pre[x] = True
+            if q == "t" and t["phase"]:
+                pre.setdefault(t["phase"][-1], False)
+            t["phase"].append(k); t["ops"].append(k)
         for n, m in wt:
-            if n not in PSUM:
-                W[n] = [(e[0] & ~m, e[1], e[2]) if not (rows and e[2] == rows) else e for e in W.get(n, []) if e[0] & ~m or (rows and e[2] == rows)] + [(m, tok, rows)]
-                R[n] = [(e[0] & ~m, e[1], e[2]) for e in R.get(n, []) if e[0] & ~m]
+            if rows:
+                W[n] = W.get(n, []) + [(m, k, rows)]
+            else:
+                W[n] = [(e[0] & ~m, e[1], e[2]) for e in W.get(n, []) if e[0] & ~m] + [(m, k, rows)]
+                R[n] = [(e[0] & ~m, e[1]) for e in R.get(n, []) if e[0] & ~m]
         for n, m in rd:
-            if n not in PSUM:
-                R[n] = [e for e in R.get(n, []) if not (e[2] == mark and mark != "dma" and e[0] & ~m == 0)] + [(m, tok, mark)]
-        return tok
+            R.setdefault(n, []).append((m, k))
+        ops.append(op)
+        return k
 
-    def dma(q, out, in_, accum=False, rows=None, after=None):
-        s = "d%d" % nd[0]; nd[0] += 1
-        if accum:
-            issue(q, lambda: eng[q].dma_start(out[0], in_[0], accum_op=O.add), [out], [in_], (s, 16, True), rows)
-        else:
-            issue(q, lambda: eng[q].dma_start(out[0], in_[0]), [out], [in_], (s, 16, True), rows, after)
+    def cost(o, ins, rate, fix):
+        if o["ind"]:
+            return fix + o["n"] * SCA * CYC
+        if ins[0]["ind"]:
+            return fix + o["n"] * GAT * CYC
+        return max(64, max(o["n"], ins[0]["n"]) * rate) * CYC
 
-    def send(dst, out, in_, rsem, after=None):
+    def half(*x):
+        return 0.5 if all(y["size"] == 2 for y in x) else 1
+
+    def val(x):
+        return x["ap"]() if isinstance(x, dict) else x
+
+    def dma(q, out, in_, accum=False, rows=None, after=()):
         s = "d%d" % nd[0]; nd[0] += 1
-        d = T.cores[dst % 4]
+        kw = dict(accum_op=O.add) if accum else {}
+        d = 300 + 128 * min(out["n"], in_["n"]) * out["size"] * DMAB
+        k = record(q, [lambda: eng[q].dma_start(val(out), val(in_), **kw)], [out], [in_], 1000 if q == "g" else 60, DMA0 + d, (s, 16, True), rows)
+        ops[k]["wire"] = ("dma", d)
+        for x in after:
+            ops[k]["pre"].setdefault(x, False)
+        return k
+
+    def send(dst, name, n, in_, rsem, after=()):
+        s = "d%d" % nd[0]; nd[0] += 1
+        d = T.cores[(rank + dst) % 4]
         rid, pid, _ = topo.addr(d)
-        m = topo.mask(core, d)
-        issue("g", lambda: g.remote_dma(T[out[0]][:, 0:out[1]], in_[0], T.sem[rsem], T.sem[s], pid, rid, m), [], [in_], (s, len(topo.engines(core, d)), False), None, after)
-
-    def lands(out, rsem, src):
-        k = len(topo.engines(T.cores[src % 4], core))
-        total[rsem] = k
-        n, m = out[1][0]
-        W[n] = [(e[0] & ~m, e[1], e[2]) for e in W.get(n, []) if e[0] & ~m] + [(m, (rsem, k, {}), None)]
+        k = record("g", [lambda: g.remote_dma(T[name][:, 0:n], val(in_), T.sem[rsem], T.sem[s], pid, rid, topo.mask(core, d))], [], [in_], 500,
+                   REM0 + 128 * n * in_["size"] * REMB, (s, len(topo.engines(core, d)), False), None, after)
+        ops[k]["wire"] = ("port", ops[k]["lat"] - REM0)
+        ops.append(dict(q="n", fns=[], pre={k: True}, busy=0, lat=0, dma=(rsem, len(topo.engines(T.cores[(rank - dst) % 4], core)), False), tiles=[]))
+        nm, m = c(name, 0, n)["use"][0]
+        W[nm] = [(e[0] & ~m, e[1], e[2]) for e in W.get(nm, []) if e[0] & ~m] + [(m, k + 1, None)]
+        return k + 1
 
     def ts(o, i, s1, op, s2=None, op2=None):
-        ins = [i] + [s for s in (s1, s2) if isinstance(s, tuple)]
-        a = s1[0] if isinstance(s1, tuple) else s1
-        b = s2[0] if isinstance(s2, tuple) else s2
+        ins = [i] + [s for s in (s1, s2) if isinstance(s, dict)]
         if op2 is None:
-            issue("v", lambda: g.vector.tensor_scalar(o[0], i[0], a, None, op), [o], ins)
+            record("v", [lambda: g.vector.tensor_scalar(val(o), val(i), val(s1), None, op)], [o], ins, cost(o, ins, half(o, i), 50))
         else:
-            issue("v", lambda: g.vector.tensor_scalar(o[0], i[0], a, b, op, op2), [o], ins)
+            record("v", [lambda: g.vector.tensor_scalar(val(o), val(i), val(s1), val(s2), op, op2)], [o], ins, cost(o, ins, half(o, i), 50))
 
     def tt(o, a, b, op):
-        issue("v", lambda: g.vector.tensor_tensor(o[0], a[0], b[0], op), [o], [a, b])
+        record("v", [lambda: g.vector.tensor_tensor(val(o), val(a), val(b), op)], [o], [a, b], cost(o, [a], 1 if a["tile"] is not None else 2 * half(o, a, b), 50))
 
     def cp(o, i):
-        issue("v", lambda: g.vector.tensor_copy(o[0], i[0]), [o], [i])
+        record("v", [lambda: g.vector.tensor_copy(val(o), val(i))], [o], [i], cost(o, [i], half(o, i), 50))
 
     def ms(o, x):
-        issue("v", lambda: g.vector.memset(o[0], x), [o], [])
+        record("v", [lambda: g.vector.memset(val(o), x)], [o], [], cost(o, [o], half(o), 0))
 
     def act(o, i, f=F.Identity, bias=0.0, scale=1.0, acc=None):
-        ins = [i] + ([bias] if isinstance(bias, tuple) else [])
-        b = bias[0] if isinstance(bias, tuple) else bias
-        if acc is None:
-            issue("c", lambda: g.scalar.activation(o[0], i[0], f, bias=b, scale=scale), [o], ins)
-        else:
-            issue("c", lambda: g.scalar.activation(o[0], i[0], f, bias=b, scale=scale, accum_out=acc[0]), [o, acc], ins)
+        ins = [i] + [s for s in (bias, scale) if isinstance(s, dict)]
+        kw = {} if acc is None else dict(accum_out=val(acc))
+        record("c", [lambda: g.scalar.activation(val(o), val(i), f, bias=val(bias), scale=val(scale), **kw)], [o] + ([acc] if acc else []), ins, cost(o, ins, 1, 65))
 
-    def mm(o, l, x, start, stop):
-        issue("t", lambda: g.tensor.matmul(o[0], l[0], x[0], start, stop), [o], [l, x])
+    def mm(*l, start=True, stop=True):
+        def one(j, x):
+            return lambda: g.tensor.matmul(val(x[0]), val(x[1]), val(x[2]), start and j == 0, stop and j == len(l) - 1)
+        record("t", [one(j, x) for j, x in enumerate(l)], [x[0] for x in l], [y for x in l for y in x[1:]], sum(max(64, x[2]["n"]) * (4 if x[2]["size"] == 4 else 1) * PE for x in l))
 
     def iota(o, pat, base, cm, f=False):
-        if f:
-            issue("g", lambda: g.iota(o[0], pat, base, cm, allow_small_or_imprecise_dtypes=True), [o], [])
-        else:
-            issue("g", lambda: g.iota(o[0], pat, base, cm), [o], [])
+        kw = dict(allow_small_or_imprecise_dtypes=True) if f else {}
+        record("g", [lambda: g.iota(val(o), pat, base, cm, **kw)], [o], [], 130 + 2 * o["n"] * CYC)
 
     def aff(o, i, pat, base, cm, op=O.is_ge):
-        issue("g", lambda: g.affine_select(o[0], i[0], pat, op, 0.0, base, cm), [o], [i])
+        record("g", [lambda: g.affine_select(val(o), val(i), pat, op, 0.0, base, cm)], [o], [i], 170 + 2 * o["n"] * CYC)
 
     def gat(q, o, w, l, add=None):
-        if q == "v":
-            if add is None:
-                cp(o, ind(w, l))
-            else:
-                ts(o, ind(w, l), add, O.add)
-        else:
+        if q == "c":
             act(o, ind(w, l), F.Identity, 0.0 if add is None else add)
+        elif add is None:
+            cp(o, ind(w, l))
+        else:
+            ts(o, ind(w, l), add, O.add)
 
     def scan(o, d0, d1, init, o0, o1):
-        issue("v", lambda: g.vector.tensor_tensor_scan(o[0], d0[0], d1[0], init, o0, o1), [o], [d0, d1])
+        record("v", [lambda: g.vector.tensor_tensor_scan(val(o), val(d0), val(d1), init, o0, o1)], [o], [d0, d1], cost(o, [d0], half(o, d0, d1), 0))
 
     def trn(o, i):
-        issue("v", lambda: g.vector.transpose(o[0], i[0]), [o], [i])
+        record("v", [lambda: g.vector.transpose(val(o), val(i))], [o], [i], cost(o, [i], half(o, i), 0))
 
     def col(k):
         return c("COL", k, k + 1)
 
     def sel(z, a):
-        return c(z, 15 - a, 143 - a)
+        return c("ZZ", 144 * z + 15 - a, 144 * z + 143 - a)
 
-    def stp(n, lo, hi, step):
-        return r(n, slice(None), slice(lo, hi, step))
-    A_ = slice(None)
+    def zcols(z):
+        return c("ZZ", 144 * z + 15, 144 * z + 143, 16)
+
+    def scaled(o, i, w):
+        act(o, i, F.Copy, 0.0, w if isinstance(w, dict) else float(w))
+
+    def wrap(o, z, x, lo, hi):
+        return [(o, sel(z, a), c(x, lo + a, hi, 16)) for a in range(16)]
     SHR, AND = O.logical_shift_right, O.bitwise_and
+    B23, B24, B26, BIG, ROUND = 2.0 ** 23, 2.0 ** 24, 2.0 ** 26, 2.0 ** 30, 1.5 * 2.0 ** 23
+    VW, DW = c("V", 0, 4096), c("DG", 0, 4096)
 
-    dma("y", r("CI"), r("cx")); dma("c", r("TGL"), r("tg")); dma("y", c("V", 0, 4096), r("xr")); dma("g", c("YQ", 0, 256), r("qx"))
-    dma("y", r("XLH"), r("xl"))
+    k = []
+    for o, i in ((r("CI"), "cx"), (r("TGL"), "tg"), (VW, "xr"), (r("QX"), "qx"), (r("LFH"), "lf")):
+        k = [dma("y", o, r(i), after=k)]
+    dma("y", r("XLH"), r("xl"), after=k)
+    cp(r("CU"), r("CI")); cp(c("CF", 0, 256), r("CI"))
+    act(c("Q", 0, 256), r("QX"), F.Identity, 192.0)
+    cp(r("LFS"), r("LFH"))
+    first = send(3, "LF0", 1024, r("LFS"), "af0")
+    second = send(3, "XL0", 1024, r("XLH"), "ax0", [first - 1])
+    send(2, "LF1", 1024, r("LFS"), "af1", [second]); send(2, "XL1", 1024, r("XLH"), "ax1", [second]); send(1, "XL2", 1024, r("XLH"), "ax2", [second])
 
     iota(c("IP", 0, 1), [[1, 1]], 0, 1)
-    iota(r("NM"), [[1, 256]], 0, 256)
     iota(r("J16"), [[1, 16]], 0, 0, True)
     iota(r("I8"), [[16, 8]], 0, 0, True)
     ms(r("ON128"), 1.0)
-    dma("y", r("LFH"), r("lf"), after=c("V", 0, 4096))
-    for j in range(4):
-        ts(c("DI", (5 + j) * 256, (6 + j) * 256), r("NM"), 3 * j, SHR, 7, AND)
-    ts(c("DG", 1280, 2304), c("DI", 1280, 2304), 0.0625, O.mult)
-    cp(r("CU"), r("CI"))
-    cp(c("CF", 0, 256), r("CI"))
-    ts(c("Q", 0, 256), c("YQ", 0, 256), 192.0, O.add)
-    for j in range(4):
-        ts(c("DI", j * 256, (j + 1) * 256), r("TGL"), 1 + 3 * j, SHR, 7, AND)
-    ts(c("DI", 1024, 1280), r("TGL"), 1, AND)
-    ts(c("DG", 0, 1280), c("DI", 0, 1280), 0.0625, O.mult)
+    aff(r("IDF"), r("ON128"), [[-1, 128]], 0, 1, O.is_equal)
     aff(r("BO1"), r("ON128"), [[-16, 8], [0, 16]], 0, 1)
     aff(r("BO"), r("BO1"), [[16, 8], [0, 16]], 15, -1)
-    aff(r("IDF"), r("ON128"), [[-1, 128]], 0, 1, O.is_equal)
     aff(r("LTF"), r("BO"), [[1, 128]], -1, -1)
+    iota(c("DS", 1280, 1536), [[1, 256]], 0, 0, True)
     iota(r("NB"), [[1, 64]], 0, 64)
-    iota(r("PJ"), [[1, 8]], 0, 8)
-    iota(c("CB", 0, SUMV), [[16, SUMV]], 256, 0, True)
-    iota(c("CB", SUMV, 8), [[32, 8 - SUMV]], 32 * SUMV, 0, True)
-    for src, b, s in ((1, "XL0", "ax0"), (2, "XL1", "ax1"), (3, "XL2", "ax2"), (1, "U0", "af0"), (2, "U1", "af1"), (3, "U2", "af2"), (1, "LFF", "aff")):
-        lands(c(b, 0, 1024), s, rank + src)
-    for k, src in enumerate((1, 2, 1, 3, 2, 3)):
-        lands(r("E%d" % k), "ae%d" % k, rank + src)
-    iota(c("Q", 256, 384), [[0, 128]], 192, 0, True); iota(c("CF", 256, 384), [[0, 128]], 0, 0, True)
-    for k in range(3):
-        iota(c("LF%d" % k, 1024, 1152), [[0, 128]], 0, 0)
-        iota(c("XL%d" % k, 1024, 1152), [[0, 128]], 0, 0, True)
-    iota(c("DD", 256, 384), [[0, 128]], 0, 0, True)
-    iota(c("BA", 256, 384), [[0, 128]], 0, 0)
-    iota(r("DIG"), [[0, 1024]], 0, 0, True)
-    send(rank + 3, ("XL0", 1024), r("XLH"), "ax0")
+    iota(r("J128"), [[1, 128]], 0, 0, True)
+    for k in range(2):
+        iota(c("NAME", 1024 * k, 1024 * k + 1024), [[1, 1024]], 1024 * k, 0, True)
+        act(c("NAME", 2048 + 1024 * k, 3072 + 1024 * k), c("NAME", 1024 * k, 1024 * k + 1024), F.Identity, 2048.0)
+    ts(c("IP", 1, 2), c("IP", 0, 1), 15, AND); ts(c("IP", 2, 3), c("IP", 0, 1), 4, SHR, 1, AND)
+    cp(col(0), c("IP", 1, 2)); cp(col(1), c("IP", 2, 3))
+    ts(r("OH"), r("J16"), col(0), O.is_equal)
 
-    def digits():
-        for f in (5, 6, 7, 8, 0, 1, 2, 3, 4):
-            dma("g", r("V", slice(f, None, 16), slice(0, 4096)), c("DG", f * 256, f * 256 + 256), True, rows="V")
-            if f == 0:
-                cp(r("HU"), r("LFH"))
-                send(rank + 3, ("U0", 1024), r("HU"), "af0")
-        send(rank + 2, ("U1", 1024), r("HU"), "af1", r("U0"))
-        send(rank + 2, ("XL1", 1024), r("XLH"), "ax1")
-    B24 = 16777216.0
+    def oh(f):
+        return c("OH", f, f + 1)
+    ts(col(24), col(0), 4096.0, O.mult)
+    ts(col(2), col(1), B24, O.mult, col(24), O.add); ts(col(25), col(24), B24, O.add); ts(col(3), col(1), -B24, O.mult, col(25), O.add)
+    ts(col(20), col(1), B26, O.mult, B23, O.add); ts(col(21), col(1), -B26, O.mult, B26 + B23, O.add)
+    ts(col(26), oh(1), 32.0, O.mult); ts(col(27), oh(2), 256.0, O.mult, col(26), O.add); ts(col(28), oh(3), 2048.0, O.mult, col(27), O.add)
+    ts(col(4), oh(0), 16.0, O.mult, col(28), O.add)
+    ts(col(29), oh(0), -16.0, O.mult, col(28), O.add); ts(col(8), oh(9), 4096.0, O.mult, col(29), O.add)
+    ts(col(30), oh(4), 16.0, O.mult); ts(col(11), col(4), 2.0, O.mult, col(30), O.add)
+    ts(col(5), oh(6), 256.0, O.mult, oh(5), O.add); ts(col(12), oh(9), 8192.0, O.mult, col(5), O.add)
+    ts(col(6), oh(4), -B24, O.mult); ts(col(13), oh(9), B23, O.mult)
+    ts(col(9), col(0), 5.0, O.is_lt); tt(col(14), oh(5), oh(6), O.add)
+    ts(col(19), col(4), -1.0, O.mult); ts(col(15), oh(6), 16.0, O.mult)
+    ts(col(10), col(0), 10.0, O.is_ge, -0.0625, O.mult); ts(col(31), oh(4), -0.0625, O.mult)
+    ts(c("COL", 32, 36), c("OH", 10, 14), col(14), O.add); ts(c("COL", 36, 40), c("OH", 10, 14), col(31), O.add)
+    ms(c("TF", 0, 16), 0.5); ms(c("TF", 16, 32), 0.0)
+    scan(r("POW"), c("TF", 0, 16), c("TF", 16, 32), 65536.0, O.mult, O.add)
+    tt(c("TF", 32, 48), r("OH"), r("POW"), O.mult)
+    record("v", [lambda: g.vector.tensor_reduce(val(col(7)), val(c("TF", 32, 48)), AxisListType.X, O.add)], [col(7)], [c("TF", 32, 48)], 64 * CYC)
+    ms(r("ZZ"), 0.0)
+    for z, w in ((ZK, 65536.0), (ZT, col(4)), (ZN, col(12)), (ZM, col(8)), (ZY, col(11)), (Z1, 512.0)):
+        scaled(zcols(z), c("BO", 0, 128, 16), w)
+    scaled(c("WN", 0, 8), c("BO", 0, 128, 16), col(19)); scaled(c("WN", 8, 16), c("BO", 0, 128, 16), -65536.0)
+    for n, w in (("ID", 1.0), ("NID", -1.0), ("HID", 0.5), ("DB1", -2.0 ** 28), ("DB2", B26), ("NIF", -1.0), ("KP", col(14))):
+        scaled(r(n), r("IDF"), w)
+    scaled(c("KP", 4, 128, 16), c("BO", 0, 128, 16), col(10))
+    for n, w in (("RN", col(5)), ("RE", col(6)), ("RL", col(4)), ("RD", col(7)), ("RB", 65536.0), ("RI", col(13))):
+        scaled(r(n), r("BO"), w)
+    tt(r("BO1"), r("LTF"), r("IDF"), O.subtract); scaled(r("TRI"), r("BO1"), B23)
+    ms(r("ONB"), 1.0); ms(r("ZR"), 0.0)
+    ts(c("CT2", 0, 16), r("POW"), 2.0, O.mult)
+    for k in (16, 32, 64, 128):
+        act(c("CT2", k, 2 * k), c("CT2", 0, k))
+    act(r("CT"), r("CT2"), F.Copy, -1048576.0)
+    ms(r("RST"), 0.0); ms(c("RST", 0, 512, 32), BIG)
+    ms(r("RS2"), 1.0); ms(c("RS2", 0, 768, 192), 0.0); ms(r("ONE"), 1.0); ms(c("PX", 256, 304), 1024.0)
+    ts(r("SC8"), r("I8"), col(0), O.add, 0.5, O.add); ts(r("DSC"), r("I8"), col(0), O.add, 4096.0, O.add); ts(r("DSM"), r("I8"), col(0), O.add, 1023.0, O.add)
+    ms(c("Q", 256, 272), 192.0); ms(c("CF", 256, 272), 0.0); ms(c("H1", 256, 272), 0); ms(c("H2", 256, 272), 0); ms(c("V", 4096, 4224), 0.0)
+    scaled(c("DD", 256, 272), c("ON128", 0, 16), oh(9))
+    for h in range(2):
+        ms(c("DG", 2048 * h, 2048 * h + 2048), 0.0)
+    act(c("DG", 4096, 4224), r("J128"), F.Identity, col(15), oh(5))
+    for j, (s, m) in enumerate(((1, 1), (2, 7), (5, 7), (8, 7), (0, 1))):
+        ts(c("DI", j * 256, (j + 1) * 256), r("TGL"), s, SHR, m, AND)
+    ts(c("DS", 0, 1280), r("DI"), 0.0625, O.mult)
+    act(c("DS", 1536, 1792), c("DS", 1280, 1536), F.Identity, col(0), 0.0)
+    k = [dma("y", r("DG", slice(f, None, 16), slice(0, 4096)), c("DS", f * 256, f * 256 + 256), rows="DG") for f in range(7)]
+    dma("y", r("FD"), r("fd"), after=k)
+    for j, (s, m) in enumerate(((0, 1), (1, 7), (4, 7), (7, 7))):
+        ts(c("NBD", 64 * j, 64 * j + 64), r("NB"), s, SHR, m, AND)
+    ts(c("NBB", 0, 256), r("NBD"), 0.0625, O.mult); ms(c("NBB", 256, 320), 0.0625); ms(r("DIG"), 0.0)
+    for f in range(5):
+        dma("y", r("DIG", slice(f, None, 16)), c("NBB", 64 * f, 64 * f + 64), rows="DIG")
+    for h in range(2):
+        ts(c("FW", 1024 * h, 1024 * h + 1024), c("FD", 1024 * h, 1024 * h + 1024), 4095, AND)
+        ts(c("FW", 2048 + 1024 * h, 3072 + 1024 * h), c("FD", 1024 * h, 1024 * h + 1024), 12, SHR)
 
-    def total_of(o, a, b):
-        tmp = c("TF4", 32, 32 + int(a[0].shape[1]))
-        tt(tmp, a, b, O.mult)
-        issue("v", lambda: g.vector.tensor_reduce(o[0], tmp[0], AxisListType.X, O.add), [o], [tmp])
+    def sub(x0, q, lo, u, out):
+        b = tile("s")
+        mm(*[(p(b, ii * 64, ii * 64 + 64), r("NID"), c(q, lo, lo + 64)) for ii in range(8)], stop=False)
+        mm(*[(p(b, ii * 64, ii * 64 + 64), r("ID"), c("XD", x0 + 8 * u + ii, x0 + 1024, 16)) for ii in range(8)], start=False)
+        act(out, p(b, 0, 512), F.Abs)
 
-    def scaled(o, i, w):
-        if isinstance(w, tuple):
-            issue("c", lambda: g.scalar.activation(o[0], i[0], F.Copy, scale=w[0]), [o], [i, w])
-        else:
-            act(o, i, F.Copy, 0.0, float(w))
-
-    def zbuf(n, w):
-        scaled(stp(n, 15, 143, 16), stp("BO", 0, 128, 16), w)
-    ms(r("ZK"), 0.0)
-    scaled(r("ID"), r("IDF"), 1.0); scaled(r("NID"), r("IDF"), -1.0)
-    zbuf("ZK", 65536)
-
-    def consts():
-        ts(c("IP", 1, 2), c("IP", 0, 1), 15, AND)
-        ts(c("IP", 2, 3), c("IP", 0, 1), 4, SHR, 1, AND)
-        cp(col(0), c("IP", 1, 2)); cp(col(1), c("IP", 2, 3))
-        ts(col(20), col(1), B24, O.mult)
-        ts(col(21), col(1), -B24, O.mult, B24, O.add)
-        ts(col(24), col(0), 4096.0, O.mult)
-        tt(col(2), col(24), col(20), O.add); tt(col(3), col(24), col(21), O.add)
+    def keys():
         act(r("CE"), c("CF", 0, 256), F.Identity, col(2)); act(r("CO"), c("CF", 0, 256), F.Identity, col(3))
-        for n in ("ZKN", "ZT", "ZTN", "ZN", "Z1"):
-            ms(r(n), 0.0)
-        ts(c("TF4", 0, 16), r("J16"), col(0), O.is_equal)
-        ms(c("TF4", 16, 32), 0.5); ms(c("TF4", 64, 80), 0.0)
-        scan(c("POW", 0, 16), c("TF4", 16, 32), c("TF4", 64, 80), 65536.0, O.mult, O.add)
-        for j in range(4):
-            ms(c("POW", 16 + j, 17 + j), 16.0 * 8 ** j)
-        total_of(col(4), c("TF4", 0, 4), c("POW", 16, 20)); total_of(col(5), c("TF4", 5, 9), c("POW", 16, 20)); total_of(col(7), c("TF4", 0, 16), c("POW", 0, 16))
-        ts(col(6), c("TF4", 4, 5), -B24, O.mult)
-        ts(col(9), col(0), 5.0, O.is_ge); ts(col(10), col(0), 4.0, O.not_equal)
-        ts(c("COL", 11, 15), c("J16", 1, 5), c("TF4", 4, 5), O.mult, -0.0625, O.mult)
-        ts(c("COL", 15, 19), c("J16", 2, 6), c("TF4", 4, 5), O.mult, -0.0625, O.mult)
-        ts(col(19), col(4), -1.0, O.mult)
-        ms(r("RST"), 0.0); ms(stp("RST", 0, 512, 32), 67108864.0)
-        digits()
-        zbuf("ZN", col(5)); zbuf("ZT", col(4)); zbuf("ZTN", col(19)); zbuf("ZKN", -65536); zbuf("Z1", 0.0625)
-        for n, w in (("RN", col(5)), ("RE", col(6)), ("RL128", col(4)), ("RD", col(7)), ("RB", 65536.0)):
-            scaled(r(n), r("BO"), w)
-        scaled(r("KEEP"), r("IDF"), col(9)); scaled(r("K1"), r("IDF"), -16.0)
-        ts(c("CT2", 0, 16), c("POW", 0, 16), 2.0, O.mult)
-        for k in (16, 32, 64, 128):
-            cp(c("CT2", k, 2 * k), c("CT2", 0, k))
-        act(r("CT"), r("CT2"), F.Copy, -1048576.0)
-
-    def consts2():
-        ts(r("SW8"), r("I8"), col(0), O.add); ts(r("SC8"), r("SW8"), 0.5, O.add); ts(r("SW2"), r("SW8"), 2.0, O.mult)
-        ts(r("DSC"), r("SW8"), 4096.0, O.add); ts(r("DSM"), r("SW8"), 1152.0, O.add)
-        ms(r("ONE"), 1.0)
-
-    def pads():
-        for j in range(3):
-            ts(c("PJD", 8 * j, 8 * j + 8), r("PJ"), 3 * j, SHR, 7 if j < 2 else 1, AND)
-        ts(c("PD", 0, 24), r("PJD"), 0.0625, O.mult)
-        ms(c("PD", 24, 32), 0.125); ms(c("PD", 32, 40), 0.5)
-        for f, k in ((0, 0), (1, 1), (2, 2), (3, 3), (5, 0), (6, 1), (7, 2), (8, 4)):
-            dma("y", r("DD", slice(f, None, 16), slice(256, 384)), c("PD", 8 * k, 8 * k + 8), rows="DD")
-
-    def labels():
-        ts(r("NB"), r("NB"), 1023, AND)
-        for j in range(4):
-            ts(c("NBD", 64 * j, 64 * j + 64), r("NB"), 3 * j, SHR, 7, AND)
-        ts(c("NBB", 0, 256), r("NBD"), 0.0625, O.mult)
-        ms(c("NBB", 256, 320), 0.0625)
-        for f in range(5):
-            dma("y", r("DIG", slice(f, None, 16)), c("NBB", 64 * f, 64 * f + 64), rows="DIG")
-        act(c("V", 4096, 4224), c("DD", 256, 384))
-        tt(r("TRI"), r("LTF"), r("K1"), O.add)
-        for n in range(4):
-            scaled(r("TI%d" % n), r("IDF"), 32.0 * 8 ** n); scaled(r("TJ%d" % n), r("IDF"), -32.0 * 8 ** n)
-
-    pk = [0]
-
-    def sub(x, q, lo, u):
-        k = pk[0] % 4; pk[0] += 1
-        for ii in range(8):
-            o = c("ps%d" % k, ii * 64, ii * 64 + 64)
-            mm(o, r("NID"), c(q, lo, lo + 64), True, False)
-            mm(o, r("ID"), stp(x, 8 * u + ii, 1024, 16), False, True)
-        act(r("AB%d" % k), r("ps%d" % k), F.Abs)
-        return k
-
-    def sums(k, z, o, u, first, last):
-        for ii in range(8):
-            mm(o, sel(z, 8 * u + ii), c("AB%d" % k, ii * 64, ii * 64 + 64), first and u == 0 and ii == 0, last and u == 1 and ii == 7)
-
-    def tags(o, gx, xd):
-        for i in range(16):
-            mm(o, sel("ZT", i), stp(gx, i, 1024, 16), i == 0, False)
-            mm(o, sel("ZTN", i), stp(xd, i, 1024, 16), False, i == 15)
-
-    def earlier(eq, row, cols, nb, n):
-        for b in range(nb):
-            ts(r(eq, A_, b, slice(0, n - 16 * b)), c(row, 16 * b, n), c(cols, b, b + 1), O.is_equal)
-
-    def dup_compare(row, cols):
-        earlier("EQ2", row, cols, 8, 128)
-
-    def dup_count():
-        mm(c("PC", 0, 128), r("RD"), r("EQ2", A_, A_, slice(0, 16)), True, False)
-        for b in range(7):
-            mm(c("PC", 16 * b + 16, 128), r("RB"), r("EQ2", A_, b, slice(16, 128 - 16 * b)), False, b == 6)
-
-    def dup_flag(o):
-        tt(o, c("PC", 0, 128), c("CT2", 0, 128), O.is_ge)
-
-    def wrap(o, z, x):
-        for a in range(16):
-            mm(o, sel(z, a), stp(x, a, 128, 16), a == 0, a == 15)
 
     def choice(t):
-        win = c("V", 0, 4096)
-
-        def take(k, a=0, b=64):
-            gat("v" if CHOICE[k] == "v" or k == late and a == 0 else "c", c("XG%d" % k, 16 * a, 16 * b), win, c("CU", 64 * k + a, 64 * k + b), 192.0)
-        order = [k for k in range(4) if CHOICE[k] == "v"] + [k for k in range(4) if CHOICE[k] != "v"]
-        late = order[-1]
-        for k in order:
-            if k != late:
-                take(k)
-        half = HALF if t else 64
-        take(late, 0, half)
-        if t:
-            claims1(t - 1)
-            disk_write(t - 1)
-            claims2(t - 1)
-        lag = None
-        for n, k in enumerate(order):
-            for u in range(2):
-                b = sub("XG%d" % k, "Q", 64 * k, u)
-                if n == 0 and u == 1 and half < 64:
-                    take(late, half)
-                if t and n == CEAT and u == 1:
-                    act(r("CE"), c("CF", 0, 256), F.Identity, col(2)); act(r("CO"), c("CF", 0, 256), F.Identity, col(3))
-                if lag:
-                    sums(*lag)
-                lag = (b, "ZK", c("PA", 64 * k, 64 * k + 64), u, True, True)
-                if t and n == CL2 and u == CU2:
-                    claims4(t - 1)
-            if t and n == CL1:
-                claims3(t - 1)
-        sums(*lag)
+        LF = c("LF%d" % (t % 3), 0, 1024)
+        for lo, hi, q in (CHOICE if t else CHOICE0):
+            gat(q, c("XD", 16 * lo, 16 * hi), VW, c("CU", lo, hi), 192.0)
         if t == 0:
-            consts()
-            consts2()
-        if t:
-            wrap(c("PC", 272, 280), "Z1", "FL")
-
-    def pick(t):
-        tt(r("KEY", A_, A_, slice(0, 16)), c("PA", 0, 256), r("CE"), O.add)
-        tt(r("KEY", A_, A_, slice(16, 32)), c("PA", 0, 256), r("CO"), O.add)
-        trn(r("KT"), r("KEY"))
-        scan(r("SCN"), r("RST"), r("KT"), 67108864.0, O.max, O.min)
-        cp(r("OI"), stp("SCN", 31, 512, 32))
-        ts(r("OI"), r("OI"), 4095, AND)
-        cp(r("OU"), r("OI"))
-        cp(r("OF"), r("OI"))
-        if t:
-            claims5(t - 1)
+            for f in range(4):
+                dma("g", r("V", slice(f, None, 16), slice(0, 4096)), c("DS", f * 256, f * 256 + 256), True, rows="V")
         else:
-            pads()
-            dma("y", r("FD"), r("fd"), after=c("V", 0, 4096))
-        gat("c", r("VO"), c("V", 0, 4096), r("OU"), 192.0)
-        gat("v", r("XO"), c("V", 0, 4096), r("OU"), 192.0)
-        tt(c("DD", 0, 256), r("VO"), r("XO"), O.subtract)
-        mm(c("PR", 0, 256), r("RN"), c("DD", 0, 256), True, True)
-        mm(c("PC", 0, 256), r("RE"), c("DD", 0, 256), True, False)
-        for a in range(16):
-            mm(c("PT", 0, 16), sel("ZT", a), stp("DD", a, 256, 16), a == 0, a == 15)
-        cp(r("OR"), c("PR", 0, 256))
-        for b in range(16):
-            ts(r("EQ", A_, b, slice(0, 256 - 16 * b)), c("OR", 16 * b, 256), c("OF", b, b + 1), O.is_equal)
-            if b < 15:
-                mm(c("PC", 16 * b + 16, 256), r("RB"), r("EQ", A_, b, slice(16, 256 - 16 * b)), False, False)
-        mm(c("PC", 0, 256), r("RD"), r("EQ", A_, A_, slice(0, 16)), False, True)
-        tt(r("CA"), c("PC", 0, 256), r("CT"), O.is_lt)
-        scan(r("PX"), r("ONE"), r("CA"), 0.0, O.mult, O.add)
-        for b in range(SUMV):
-            act(c("JS", 0, 256 - 16 * b), c("PX", 16 * b, 256), F.Sign, c("SC8", b, b + 1), -1.0, c("LS", b, b + 1))
-        ts(r("T2"), c("PX", 255, 256), 2.0, O.mult)
-        for b in range(SUMV, 8):
-            ts(c("JV", 0, 256 - 16 * b), c("PX", 16 * b, 256), c("SC8", b, b + 1), O.is_le, 2.0, O.mult)
-            o, i = c("LS", b, b + 1), c("JV", 0, 256 - 16 * b)
-            issue("v", lambda: g.vector.tensor_reduce(o[0], i[0], AxisListType.X, O.add), [o], [i])
-        ts(r("RL"), r("SW2"), r("T2"), O.subtract, 0.0, O.max)
-        tt(r("CBP"), r("CB"), r("RL"), O.add)
-        ts(r("INV"), r("SW2"), r("T2"), O.is_ge, 8192.0, O.mult)
-        if t:
-            apply(2 * (t - 1), "LF%d" % (t % 3))
-        else:
-            cp(c("LF0", 0, 1024), r("U0"))
-        cp(r("NA"), c("PT", 0, 16))
-        gat("v", c("BA", 0, 256), c("LF%d" % (t % 3), 0, 1152), r("NA"))
-        tt(r("H8"), r("LS"), r("CBP"), O.add)
-        ts(r("LU"), r("H8"), 0.5, O.mult)
-        gat("v", r("BI"), r("BA"), r("LU"))
-        gat("c", r("CR"), r("CF"), r("LU"))
-        gat("c", r("QR"), r("Q"), r("LU"))
-        tt(r("SQ"), r("BI"), r("BI"), O.mult)
-        cp(r("CRU"), r("CR"))
-        gat("v", r("DDR"), r("DD"), r("LU"))
-        wrap(c("PR", 256, 264), "ZT", "DDR")
+            claims(t - 1); disk_write(t - 1)
+        PC = tile()
+        for lo, hi in PARTS:
+            PA, PN = tile(), tile()
+            b0, b1 = lo // 16, hi // 16
+            for k in range(hi // 64 - 1, lo // 64 - 1, -1):
+                for u in range(2):
+                    j = 8 * k + 4 * u
+                    sub(1024 * k, "Q", 64 * k, u, r("AB", A_, slice(j, j + 4)))
+                    mm(*[(p(PA, 64 * k, 64 * k + 64), sel(ZK, 8 * u + ii), r("AB", A_, j + ii // 2, slice(64 * (ii % 2), 64 * (ii % 2) + 64))) for ii in range(8)], start=u == 0, stop=u == 1)
+            tt(r("KEY", A_, slice(b0, b1), slice(0, 16)), p(PA, lo, hi), r("CE", A_, slice(b0, b1)), O.add)
+            tt(r("KEY", A_, slice(b0, b1), slice(16, 32)), p(PA, lo, hi), r("CO", A_, slice(b0, b1)), O.add)
+            trn(c("KT", 2 * lo, 2 * hi), r("KEY", A_, slice(b0, b1)))
+            scan(c("SCN", 2 * lo, 2 * hi), c("RST", 2 * lo, 2 * hi), c("KT", 2 * lo, 2 * hi), BIG, O.max, O.min)
+            cp(c("OI", b0, b1), c("SCN", 2 * lo + 31, 2 * hi, 32))
+            ts(c("OI", b0, b1), c("OI", b0, b1), 4095, AND)
+            cp(c("OU", b0, b1), c("OI", b0, b1)); cp(c("OF", b0, b1), c("OI", b0, b1))
+            gat("v", c("OR", lo, hi), r("NAME"), c("OU", b0, b1))
+            gat("c", c("DD", lo, hi), DW, c("OU", b0, b1))
+            for b in range(b0, b1):
+                ts(r("EQ", A_, b, slice(0, 256 - 16 * b)), c("OR", 16 * b, 256), c("OF", b, b + 1), O.is_equal)
+                if b < 15:
+                    opens = b == PARTS[0][0] // 16
+                    mm(*[(p(PC, 0, 256), r("ZR"), r("ONE"))] * opens, (p(PC, 16 * b + 16, 256), r("RB"), r("EQ", A_, b, slice(16, 256 - 16 * b))), start=opens, stop=False)
+            mm((p(PC, lo, hi), r("RD"), r("EQ", A_, slice(b0, b1), slice(0, 16))), start=False, stop=False)
+            mm(*wrap(p(PN, b0, b1), ZT, "DD", lo, hi))
+            cp(c("NA", b0, b1), p(PN, b0, b1))
+            for w, (add, less, sh) in enumerate(((4.0, 16.0, 3), (592.0, 592.0 ** 2 - 32, 5))):
+                act(c("Y", 256 * w + lo, 256 * w + hi), ind(LF, c("NA", b0, b1)), F.Square, add)
+                ts(c("HI", 256 * w + lo, 256 * w + hi), c("Y", 256 * w + lo, 256 * w + hi), less, O.subtract)
+                ts(c("H%d" % (w + 1), lo, hi), c("HI", 256 * w + lo, 256 * w + hi), sh, SHR, 4095, AND)
+        mm((p(PC, 0, 256), r("RE"), c("DD", 0, 256)), start=False)
+        tt(r("CA"), p(PC, 0, 256), r("CT"), O.is_lt)
+        scan(c("PX", 0, 256), r("ONE"), r("CA"), 0.0, O.mult, O.add)
+        for b in range(4):
+            act(r("JS", A_, b, slice(0, 304 - 32 * b)), c("PX", 16 * b, 304 - 16 * b), F.Sign, c("SC8", b, b + 1), -1.0, c("LS", b, b + 1))
+            ts(c("JV", 192 * b, 192 * b + 192), c("PX", 64, 256), c("SC8", 4 + b, 5 + b), O.is_le)
+        scan(r("SV"), r("RS2"), r("JV"), 0.0, O.mult, O.add)
+        ts(c("LU", 4, 8), c("SV", 191, 768, 192), 64.0, O.add)
+        ts(c("LU", 0, 4), r("LS"), 0.5, O.mult, 152.0, O.add)
 
     def translate(t):
-        LF, XL = "LF%d" % (t % 3), "XL%d" % (t % 3)
-        wrap(c("PC", 264, 272), "ZN", "DDR")
-        mm(c("PC", 0, 128), r("RL128"), r("DDR"), True, True)
-        ts(c("H", 0, 128), r("SQ"), 3, SHR)
-        ts(r("S5"), r("SQ"), 5, SHR)
-        ts(c("H", 128, 256), r("BI"), 37.0, O.mult, 1.0, O.add)
-        tt(c("H", 0, 128), c("H", 0, 128), r("BI"), O.add)
-        tt(c("H", 128, 256), c("H", 128, 256), r("S5"), O.add)
-        ts(r("H"), r("H"), 4095, AND)
-        cp(r("CCU"), r("H"))
-        for k in range(2):
-            gat("c", r("GS%d" % k), c("V", 0, 4096), c("CRU", 64 * k, 64 * k + 64))
-        blk = [(0, 0), (0, 1), (1, 0), (1, 1)]
-
-        def take(k):
-            lo = 128 * blk[k][1] + 64 * blk[k][0]
-            gat("v" if TRANS[k] == "v" else "c", r("XG%d" % k), c("V", 0, 4096), c("CCU", lo, lo + 64))
-
-        def plain(k):
-            ts(r("XD%d" % k), r("XG%d" % k), 192.0, O.add)
-
-        def subs(k):
-            return [sub("XD%d" % k, "QR", 64 * blk[k][0], u) for u in range(2)]
-        bank = [("PC", 128, "PR", 384), ("PT", 0, "PA", 256)]
-
-        def flush(x):
-            k, bs, pos = x
-            hs, w = blk[k]
-            bt, t0, ba, a0 = bank[hs]
-            tags(c(bt, t0 + 64 * w, t0 + 64 * w + 64), "XG%d" % k, "XD%d" % k)
+        LF, XL = c("LF%d" % (t % 3), 0, 1024), r("XL%d" % (t % 3))
+        gat("v", c("CCU", 0, 128), r("H1"), r("LU")); gat("v", c("CCU", 128, 256), r("H2"), r("LU"))
+        gat("c", r("QR"), r("Q"), r("LU")); gat("c", r("DDR"), r("DD"), r("LU")); gat("v", r("CRU"), r("CF"), r("LU"))
+        for w, lo, hi, q in TRANS:
+            gat(q, c("XG", 2048 * w + 16 * lo, 2048 * w + 16 * hi), VW, c("CCU", 128 * w + lo, 128 * w + hi))
+        PL, PT, PD, PS, PQ = tile(), tile(), tile(), tile(), tile()
+        mm(*wrap(p(PL, 0, 8), ZT, "DDR", 0, 128)); mm(*wrap(p(PL, 8, 16), ZN, "DDR", 0, 128)); mm((p(PL, 128, 256), r("RL"), r("DDR")))
+        cp(r("NU"), p(PL, 0, 8)); tt(r("OUF"), p(PL, 8, 16), r("DSC"), O.min); cp(r("OUR"), r("OUF"))
+        gat("c", r("BF"), LF, r("NU")); gat("c", r("A"), XL, r("NU")); scaled(r("DDM"), r("DDR"), col(9))
+        for b in range(8):
+            ts(r("EQ3", A_, b, slice(0, 128 - 16 * b)), p(PL, 128 + 16 * b, 256), p(PL, b, b + 1), O.is_equal)
+        cp(r("CC"), r("CCU")); tt(r("D12"), c("CC", 128, 256), c("CC", 0, 128), O.subtract)
+        for w in range(2):
+            for h in range(2):
+                x0 = 2048 * w + 1024 * h
+                ts(c("XD", x0, x0 + 1024), c("XG", x0, x0 + 1024), 192.0, O.add)
+                for u in range(2):
+                    sub(x0, "QR", 64 * h, u, r("AB", A_, slice(16 * w + 8 * u, 16 * w + 8 * u + 8), slice(64 * h, 64 * h + 64)))
+            for x, z in (("XG", zcols(ZT)), ("XD", c("WN", 0, 8))):
+                mm(*[(p(PT, 128 * w + i, 128 * w + 128, 16), c(x, 2048 * w + i, 2048 * w + 2048, 16), z) for i in range(16)], start=w == 0 and x == "XG", stop=False)
+            mm((p(PT, 128 * w, 128 * w + 128), r("BF"), r("NIF")), start=False, stop=w == 1)
+        ts(r("IN"), p(PT, 0, 256), -451584.0, O.is_equal)
+        for w in range(2):
             for u in range(2):
-                sums(bs[u], "ZK" if w else "ZKN", c(ba, a0, a0 + 64), u, pos == 0, pos == 1)
-
-        def decide(hs):
-            bt, t0, ba, a0 = bank[hs]
-            lo, hi = 64 * hs, 64 * hs + 64
-            for w in range(2):
-                tt(c("IN", 128 * w + lo, 128 * w + hi), c(bt, t0 + 64 * w, t0 + 64 * w + 64), c("BS", lo, hi), O.is_equal)
-            ts(c("INB", lo, hi), c("IN", lo, hi), 33554432.0, O.mult)
-            tt(c("M2", lo, hi), c(ba, a0, a0 + 64), c("IN", 128 + lo, 128 + hi), O.max)
-            tt(c("SEL", lo, hi), c("M2", lo, hi), c("INB", lo, hi), O.is_gt)
-            tt(c("SEL", lo, hi), c("SEL", lo, hi), c("D12", lo, hi), O.mult)
-            tt(c("SS", lo, hi), c("SEL", lo, hi), c("H", lo, hi), O.add)
-            if hs == 0:
-                claim_keys(lo, hi)
-            cp(ind(r("FW"), c("OUR", 4 * hs, 4 * hs + 4)), c("SS", lo, hi))
-        take(0); plain(0)
-        cp(r("NU"), c("PR", 256, 264))
-        cp(r("OUR"), c("PC", 264, 272))
-        cp(r("NR"), c("PC", 0, 128))
-        take(1)
-        b0 = subs(0)
-        plain(1)
-        take(2); take(3)
-        b1 = subs(1)
-        gat("c", r("A"), r(XL), r("NU"))
-        flush((0, b0, 0))
-        plain(2)
-        b2 = subs(2)
-        flush((1, b1, 1))
-        plain(3)
-        lag = [(3, subs(3), 1)]
-        flush((2, b2, 0))
-        cp(r("WNF"), r("NU"))
-        tt(r("D12"), c("H", 128, 256), c("H", 0, 128), O.subtract)
-        ts(r("BS"), r("BI"), -1797120.0, O.add)
-        for k in range(2):
-            ts(r("SX%d" % k), r("GS%d" % k), 192.0, O.add)
-        if t == 0:
-            labels()
-            ts(c("FW", 0, 2048), r("FD"), 4095, AND)
-            ts(c("FW", 2048, 4096), r("FD"), 12, SHR)
-        ts(r("DDM"), r("DDR"), col(10), O.mult, col(11 + t), O.add)
-        tt(r("VL"), r("A"), r("DDM"), O.add)
-        cp(ind(r("V"), r("OUR")), r("VL"))
-        tt(r("QF"), ind(c("V", 0, 4096), r("OU")), c("Q", 0, 256), O.add)
-        ts(c("Q", 0, 256), r("QF"), 0.5, O.mult, 95.75, O.add)
-        cp(r("NI"), r("NU"))
-        ts(r("N1"), r("NI"), 1, AND)
-        ts(r("N1"), r("N1"), -2.0, O.mult, 1.0, O.add)
-        tt(r("NI"), r("NI"), r("N1"), O.add)
-        decide(0)
-        if t == 1:
-            cp(c("LF2", 0, 1024), r("U2"))
-            apply(1, "LF2")
-        if t == 2:
-            apply(3, "LF0")
-        dup_compare("NR", "WNF")
-        flush(lag.pop())
-        dup_count()
-        decide(1)
-        if t == STEPS - 1:
-            dup_flag(r("FL"))
-            wrap(c("PC", 272, 280), "Z1", "FL")
-            claim_order()
-        for k in range(2):
-            tags(c("PT", 256 + 64 * k, 320 + 64 * k), "GS%d" % k, "SX%d" % k)
-        cp(c("CF", 0, 256), ind(c("FW", 0, 4096), r("OU")))
+                if w == 1 and u == 1:
+                    mm((p(PD, 0, 128), r("DB1"), c("IN", 0, 128)), (p(PD, 0, 128), r("DB2"), c("IN", 128, 256)), start=False, stop=False)
+                mm(*[(p(PD, i, 128, 16), r("AB", A_, 16 * w + i), zcols(ZK) if w else c("WN", 8, 16)) for i in range(8 * u, 8 * u + 8)], start=w + u == 0, stop=w + u == 2)
+        act(r("SEL"), p(PD, 0, 128), F.Sign, -0.5)
+        mm((p(PS, 0, 128), r("ONB"), r("HID")), (p(PS, 0, 128), r("SEL"), r("HID")))
+        tt(r("SD"), p(PS, 0, 128), r("D12"), O.mult)
+        tt(r("SS"), r("SD"), c("CC", 0, 128), O.add)
+        cp(ind(r("FW"), r("OUR")), r("SS"))
         if t < STEPS - 1:
-            cp(r("CU"), c("CF", 0, 256))
+            gat("v", r("CU"), c("FW", 0, 4096), r("OU"))
+        tt(ind(r("V"), r("OUR")), r("A"), r("DDM"), O.add)
+        gat("c", r("XO"), VW, r("OU"), 192.0)
+        mm((p(PQ, 0, 256), r("HID"), c("Q", 0, 256)), (p(PQ, 0, 256), r("HID"), r("XO")))
+        act(c("Q", 0, 256), p(PQ, 0, 256), F.Identity, -0.25)
+        act(r("DDE"), r("DDR"), F.Identity, col(36 + t))
+        cp(ind(r("DG"), r("OUR")), r("DDE"))
+        for h in range(2):
+            gat("c", c("GS", 1024 * h, 1024 * h + 1024), DW, c("CRU", 64 * h, 64 * h + 64))
+        gat("v", c("CF", 0, 256), c("FW", 0, 4096), r("OU"))
+        if t < STEPS - 1:
+            keys()
 
-    def claim_keys(lo, hi):
-        tt(c("N12", lo, hi), c("IN", lo, hi), c("IN", 128 + lo, 128 + hi), O.max)
-        ts(c("NEW", lo, hi), c("N12", lo, hi), -1.0, O.mult, 1.0, O.add)
-        ts(c("K1", lo, hi), c("SS", lo, hi), 1024.0, O.mult)
-        tt(c("KK", lo, hi), c("K1", lo, hi), c("BI", lo, hi), O.add)
+    def lower(b, eq, fl):
+        mm((p(b, 0, 128), r("RD"), r(eq, A_, A_, slice(0, 16))), *[(p(b, 16 * j + 16, 128), r("RB"), r(eq, A_, j, slice(16, 128 - 16 * j))) for j in range(7)])
+        tt(r(fl), p(b, 0, 128), c("CT2", 0, 128), O.is_ge)
+
+    def apply(lst, x, n, u):
+        ts(r(u), lst, 1.0, O.add)
+        cp(ind(r(n), r(u)), x)
 
     def disk_write(t):
-        act(c("SF", 0, 128), c("PT", 256, 384), F.Identity, 1797120.0)
-        tt(r("MF"), c("PC", 272, 280), r("DSM"), O.mult)
-        tt(c("SF", 128, 136), r("MF"), r("NI"), O.max)
-        for dst, k in (((3, 0), (2, 1)), ((3, 2), (1, 3)), ((2, 4),), ((1, 5),))[t]:
-            send(rank + dst, ("E%d" % k, 136), r("SF"), "ae%d" % k)
-        if t == 0:
-            send(rank + 1, ("U2", 1024), r("HU"), "af2")
-            send(rank + 1, ("XL2", 1024), r("XLH"), "ax2")
+        a, b, s = tile(), tile(), tile()
+        lower(a, "EQ3", "FM")
+        mm(*wrap(p(b, 0, 8), ZM, "DDR", 0, 128), *wrap(p(b, 0, 8), Z1, "FM", 0, 128))
+        tt(c("SF", 128, 136), p(b, 0, 8), r("DSM"), O.min)
+        mm(*[(p(s, 0, 128), sel(ZT, i), c("GS", i, 2048, 16)) for i in range(16)])
+        act(c("SF", 0, 128), p(s, 0, 128))
+        to = (((3, 0, "LF1"),), ((3, 2, "LF2"), (1, 3, "LF0")), ((2, 4, "LF0"),), ((1, 5, "YL"),))[t]
+        for dst, k, n in to:
+            send(dst, "E%d" % k, 136, r("SF"), "ae%d" % k)
         if t in (0, 2):
-            cp(r("MU"), c("SF", 128, 136))
-            cp(ind(r("LF%d" % t), r("MU")), c("SF", 0, 128))
-        if t == 2:
-            send(rank + 3, ("LFF", 1024), c("LF2", 0, 1024), "aff")
+            apply(c("SF", 128, 136), c("SF", 0, 128), "LF%d" % t, "MU")
+            send(*((2, "LF2", 1024, c("LF0", 0, 1024), "af2"), (3, "YL", 1024, c("LF2", 0, 1024), "aff"))[t // 2])
+        for dst, k, n in to:
+            apply(c("E%d" % k, 128, 136), c("E%d" % k, 0, 128), n, "MX")
 
-    def apply(k, n):
-        cp(r("MX"), c("E%d" % k, 128, 136))
-        cp(ind(r(n), r("MX")), c("E%d" % k, 0, 128))
-
-    def claims1(t):
-        if t < STEPS - 1:
-            dup_flag(r("FL"))
-            wrap(c("PC", 272, 280), "Z1", "FL")
-            claim_order()
-
-    def claim_order():
-        claim_keys(64, 128)
-        mm(c("PC", 384, 512), r("TRI"), r("NEW"), True, True)
-        act(r("KKE"), r("KK"), F.Identity, col(20)); act(r("KKO"), r("KK"), F.Identity, col(21))
-
-    def claims2(t):
-        ts(r("PEN"), c("PC", 384, 512), -16.0, O.is_gt, B24, O.mult)
-        tt(r("KEC", A_, A_, slice(0, 16)), r("PEN"), r("KKE"), O.add)
-        tt(r("KEC", A_, A_, slice(16, 32)), r("PEN"), r("KKO"), O.add)
+    def claims(t):
+        a, b, n, v, e, w = tile(), tile(), tile(), tile(), tile(), tile()
+        mm((p(a, 0, 128), c("IN", 0, 128), r("ID")), (p(a, 0, 128), c("IN", 128, 256), r("ID")))
+        act(r("NEW"), p(a, 0, 128), F.Relu, 1.0, -1.0)
+        mm((p(b, 0, 128), r("TRI"), r("NEW")), (p(b, 0, 128), r("IDF"), r("BF")), (p(b, 0, 128), r("RI"), r("DDR")))
+        act(r("KE"), r("SS"), F.Identity, col(20), 1024.0); act(r("KO"), r("SS"), F.Identity, col(21), 1024.0)
+        tt(r("KEC", A_, A_, slice(0, 16)), p(b, 0, 128), r("KE"), O.add); tt(r("KEC", A_, A_, slice(16, 32)), p(b, 0, 128), r("KO"), O.add)
         trn(r("KTC"), r("KEC"))
-        scan(r("SNC"), c("RST", 0, 256), r("KTC"), 67108864.0, O.max, O.min)
-        cp(r("KI"), stp("SNC", 31, 256, 32))
-        ts(r("PI"), r("KI"), 10, SHR)
-        ts(r("BW"), r("KI"), 1023, AND)
-        tt(r("PF"), r("PI"), r("INV"), O.max)
-        tt(r("PF"), r("PF"), r("DSC"), O.min)
-        cp(r("PU"), r("PF"))
-        cp(r("BU"), r("BW"))
-        gat("v", r("GP"), r("V"), r("PU"), 192.0)
-        gat("v", r("XP"), r("V"), r("PU"), 192.0)
-        gat("v", r("DB"), r("DIG"), r("BU"))
-        tt(r("DP"), r("GP"), r("XP"), O.subtract)
-        ts(r("ZC"), r("DP"), -(t + 1) / 16.0, O.is_equal, col(15 + t), O.mult)
-
-    def claims3(t):
-        mm(c("PR", 0, 128), r("RN"), r("DP"), True, True)
-        o = c("PT", 384, 512)
-        mm(o, r("ID"), r("XP"), True, False); mm(o, r("KEEP"), r("DP"), False, False)
-        mm(o, r("ID"), r("DB"), False, False); mm(o, r("ID"), r("ZC"), False, True)
-        if t == 0:
-            cp(c("LF1", 0, 1024), r("U1"))
-        cp(r("PLR"), c("PR", 0, 128))
-        dup_compare("PLR", "PF")
-        ts(r("NV"), o, -192.0, O.add)
-
-    def claims4(t):
-        dup_count()
-        dup_flag(r("FL"))
-
-    def claims5(t):
-        tt(r("FS"), c("PC", 272, 280), r("DSC"), O.mult)
-        tt(r("P2"), r("FS"), r("PF"), O.max)
+        scan(r("SNC"), c("RST", 0, 256), r("KTC"), BIG, O.max, O.min)
+        cp(r("KI"), c("SNC", 31, 256, 32))
+        ts(r("PI"), r("KI"), 10, SHR); ts(r("BW"), r("KI"), 1023, AND)
+        tt(r("PF"), r("PI"), r("DSC"), O.min)
+        cp(r("PU"), r("PF")); cp(r("BU"), r("BW"))
+        act(r("NMP"), ind(r("DG"), r("PU")), F.Copy, 0.0, col(32 + t))
+        gat("c", r("DB"), r("DIG"), r("BU"))
+        mm((p(n, 0, 128), r("RN"), r("NMP")))
+        mm((p(v, 0, 128), r("KP"), r("NMP")), (p(v, 0, 128), r("ID"), r("DB")))
+        act(r("NV"), p(v, 0, 128))
+        for j in range(8):
+            ts(r("EQ2", A_, j, slice(0, 128 - 16 * j)), p(n, 16 * j, 128), c("PF", j, j + 1), O.is_equal)
+        lower(e, "EQ2", "FL")
+        mm((p(w, 0, 8), r("IDF"), r("PF")), *wrap(p(w, 0, 8), Z1, "FL", 0, 128))
+        tt(r("P2"), p(w, 0, 8), r("DSC"), O.min)
         cp(r("PU2"), r("P2"))
-        cp(ind(r("V"), r("PU2")), r("NV"))
+        cp(ind(r("DG"), r("PU2")), r("NV"))
+        if t < STEPS - 1:
+            ts(r("XP"), ind(r("V"), r("PU")), ROUND, O.add, ROUND, O.subtract)
+            tt(ind(r("V"), r("PU2")), r("XP"), r("DB"), O.add)
 
+    keys()
     for t in range(STEPS):
         choice(t)
-        pick(t)
         translate(t)
-    claims1(STEPS - 1)
     dma("y", r("yc"), c("CF", 0, 256))
-    disk_write(STEPS - 1)
-    claims2(STEPS - 1)
-    ts(r("YQ"), c("Q", 0, 256), -192.0, O.add)
+    act(r("YQ"), c("Q", 0, 256), F.Identity, -192.0)
     dma("y", r("yq"), r("YQ"))
-    claims3(STEPS - 1); claims4(STEPS - 1)
-    wrap(c("PC", 272, 280), "Z1", "FL")
-    claims5(STEPS - 1)
-    for n in range(5):
-        dma("y" if n % 2 else "c", c("TX", 256 * n, 256 * n + 256), r("V", slice(n, None, 16), slice(0, 4096)))
-    cp(c("YL", 0, 1024), c("LFF", 0, 1024))
-    apply(5, "YL")
+    claims(STEPS - 1); disk_write(STEPS - 1)
     dma("y", r("yl"), c("YL", 0, 1024))
-    ts(r("TD"), r("TX"), 192.0, O.add)
-    for n in range(4):
-        mm(c("PT", 0, 256), r("TI%d" % n), c("TX", 256 * n, 256 * n + 256), n == 0, False)
-        mm(c("PT", 0, 256), r("TJ%d" % n), c("TD", 256 * n, 256 * n + 256), False, n == 3)
-    act(r("TE"), c("TX", 1024, 1280), F.Identity, 192.0625)
-    tt(r("TE2"), r("TE"), c("TD", 1024, 1280), O.subtract)
-    ts(r("TE2"), r("TE2"), 0.125, O.is_equal, 3594240.0, O.add)
-    tt(r("TY"), c("PT", 0, 256), r("TE2"), O.add)
-    dma("c", r("yt"), r("TY"))
+    b = tile()
+    mm(*[(p(b, 0, 256), sel(ZY, j), c("DG", 256 * j, 256 * j + 256)) for j in range(16)])
+    act(r("TY"), p(b, 0, 256))
+    dma("y", r("yt"), r("TY"))
+
+    if not PLAN:
+        PLAN.append(plan(ops, tiles))
+    order, banks, after = PLAN[0]
+    bank.update(banks)
+    cnt = {q: 0 for q in psem}
+    know = {q: {} for q in eng}
+    tok, total = {}, {}
+    for k in order:
+        o = ops[k]; q = o["q"]
+        if q == "n":
+            tok[k] = (o["dma"][0], o["dma"][1], {}); total[o["dma"][0]] = o["dma"][1]
+            continue
+        best = {}
+        for x in [x for x, w in o["pre"].items() if w] + [x for x in after.get(k, []) if ops[x]["q"] != "t"]:
+            s, v, sn = tok[x]
+            if s not in best or best[s][0] < v:
+                best[s] = (v, sn)
+        need = sorted(best.items(), key=lambda z: -len(z[1][1]))
+        for s, (v, sn) in need:
+            if know[q].get(s, 0) >= v or any(s2 != s and sn2.get(s, 0) >= v and know[q].get(s2, 0) < v2 for s2, (v2, sn2) in need):
+                continue
+            eng[q].wait_ge(T.sem[s], v)
+            know[q][s] = v
+            for a, b in sn.items():
+                if know[q].get(a, 0) < b:
+                    know[q][a] = b
+        for fn in o["fns"]:
+            inst = fn()
+            if o["dma"] is None:
+                cnt[q] += 1
+                inst.then_inc(T.sem[psem[q]], 1)
+            elif o["dma"][2]:
+                inst.then_inc(T.sem[o["dma"][0]], 16)
+        s, v = (psem[q], cnt[q]) if o["dma"] is None else o["dma"][:2]
+        tok[k] = (s, v, dict(know[q])); total[s] = v
     for s in sorted(total):
         g.wait_ge(T.sem[s], total[s])

@@ -3,11 +3,19 @@ from concourse.mybir import AluOpType as O, AxisListType, ActivationFunctionType
 
 STEPS = 4
 CHOICE0 = ((192, 256, "c"), (128, 192, "v"), (64, 128, "v"), (32, 64, "c"), (0, 32, "v"))
-CHOICE = ((192, 256, "c"), (128, 192, "v"), (64, 128, "c"), (32, 64, "c"), (0, 32, "v"))
-TRANS = ((0, 0, 64, "v"), (0, 64, 128, "c"), (1, 0, 64, "v"), (1, 64, 96, "c"), (1, 96, 128, "v"))
+CHOICE = ((192, 256, "c"), (128, 192, "v"), (64, 128, "c"), (0, 64, "v"))
+TRANS = ((0, 0, 64, "v"), (0, 64, 128, "c"), (1, 0, 64, "v"), (1, 64, 128, "c"))
+NAMES = ((0, 64, "v"), (64, 128, "c"))
+NAMES3 = ((0, 64, "v"), (64, 128, "c"))
+LOADS = ("cx", "tg", "xr", "qx", "lf")
+WHICH, SWAPS, TABU = 0, 300, 12
+HASHES = ((0, 256),)
+BLOCKS0, BLOCKS = (3, 2, 1, 0), (3, 1, 2, 0)
+FIXED = ("kKTC0 cXD2048 kSNC0 " + " ".join("kEQ2%d" % (128 * j) for j in range(8)) + " cXD0",
+         "tXG0 tROW0 tROW128 tROW256 tXD0 tXD1024 tXG2048 tXD2048 tXD3072 tA0 tV0 tBT0 tGS0 tIN0", "tXG1024 tXG3072 tAB0 tAB3136 tSEL0 tGS1024")
 PARTS = ((64, 256), (0, 64))
-POOLS = {"s": 3, "x": 5}
-SLACK, ROUNDS = 100, 6
+POOLS = {"s": 4, "x": 4}
+SLACK, ROUNDS, PASSES, JIT, WIN = 100, 1, 20, 1000, 5000
 CYC, PE, WAKE, GAT, SCA, DMA0, DMAB, REM0, REMB = 0.83, 0.417, 190, 1.56, 3.8, 1200, 0.004, 1500, 0.02
 
 
@@ -17,33 +25,33 @@ def _scratch():
     def sb(n, w, d="float32"):
         S[n] = ("sbuf", [128] + (w if isinstance(w, list) else [w]), d)
     B, I, U = "bfloat16", "int32", "uint16"
-    sb("V", 4224, B); sb("DG", 4224, B); sb("FW", 4224, I); sb("FD", 2048, I); sb("NAME", 4096)
+    sb("V", 4224, B); sb("DG", 4224, B); sb("FW", 4224, I); sb("FD", 2048, I); sb("NAME", 4224); sb("YT", 4224)
     for k in (0, 2, 3, 4, 5):
         sb("E%d" % k, 136)
-    sb("LFH", 1024, I); sb("LFS", 1024); sb("YL", 1152); sb("XLH", 1024, B)
+    sb("HU", 1024, U); sb("U0", 1024, U); sb("PLR", 128, U); sb("NY", 128); sb("LFH", 1024, I); sb("LFS", 1024); sb("YL", 1152); sb("XLH", 1024, B)
     for k in range(3):
         sb("LF%d" % k, 1152); sb("XL%d" % k, 1024, B)
-    sb("CI", 256, I); sb("CF", 272); sb("CU", 256, U); sb("Q", 272, B); sb("CE", [16, 16]); sb("CO", [16, 16])
+    sb("CI", 256, I); sb("CF", 272); sb("CU", 256, U); sb("Q", 272, B)
     sb("XG", 4096, B); sb("XD", 4096, B); sb("AB", [32, 128], B); sb("GS", 2048, B)
     sb("KEY", [16, 32]); sb("KT", 512); sb("SCN", 512); sb("RST", 512)
     sb("OI", 16, I); sb("OF", 16); sb("OU", 16, U); sb("DD", 272, B); sb("OR", 256, U); sb("EQ", [16, 256], B)
     sb("NA", 16, U); sb("Y", 512); sb("HI", 512, I); sb("H1", 272, I); sb("H2", 272, I)
     sb("CA", 256, B); sb("PX", 304, B); sb("ONE", 256, B); sb("JS", [4, 304], B); sb("JV", 768, B); sb("SV", 768, B); sb("RS2", 768, B)
-    sb("LS", 4); sb("LU", 8, U); sb("CCU", 256, U); sb("QR", 128, B); sb("DDR", 128, B); sb("DDM", 128, B); sb("DDE", 128, B); sb("CRU", 128, U)
+    sb("LS", 4); sb("LU", 8, U); sb("CCU", 256, U); sb("QR", 128, B); sb("DDR", 128, B); sb("ROW", [3, 128], B); sb("MF", 8); sb("BT", 128); sb("DDE", 128, B); sb("CRU", 128, U)
     sb("NU", 8, U); sb("OUF", 8); sb("OUR", 8, U); sb("A", 128, B); sb("BF", 128); sb("CC", 256); sb("D12", 128)
     sb("IN", 256, B); sb("SEL", 128, B); sb("SD", 128); sb("SS", 128); sb("NEW", 128, B); sb("XO", 256, B)
-    sb("KE", [8, 16]); sb("KO", [8, 16]); sb("KEC", [8, 32]); sb("KTC", 256); sb("SNC", 256)
+    sb("KEC", [8, 32]); sb("KTC", 256); sb("SNC", 256)
     sb("KI", 8, I); sb("PI", 8, I); sb("BW", 8, I); sb("BU", 8, U); sb("PF", 8); sb("PU", 8, U); sb("P2", 8); sb("PU2", 8, U)
     sb("NMP", 128, B); sb("XP", 128, B); sb("DB", 128, B); sb("NV", 128, B); sb("EQ2", [8, 128], B); sb("EQ3", [8, 128], B); sb("FL", 128, B); sb("FM", 128, B)
     sb("SF", 136); sb("MU", 8, U); sb("MX", 8, U); sb("YQ", 256, B); sb("QX", 256, B); sb("TY", 256)
-    sb("COL", 48); sb("IP", 4, I); sb("BO", 128); sb("BO1", 128); sb("OH", 16); sb("TF", 48); sb("POW", 16)
-    sb("ZZ", 6 * 144, B); sb("WN", 16, B)
-    for n in ("ID", "NID", "HID", "DB1", "DB2", "RN", "RE", "RL", "RD", "RB", "RI", "TRI", "ONB", "KP", "ZR"):
+    sb("COL", 48); sb("IP", 4, I); sb("BO", 128); sb("BO1", 128); sb("OH", 16); sb("TF", 64); sb("POW", 16)
+    sb("ZZ", 4 * 144, B); sb("WN", 16, B)
+    for n in ("ID", "NID", "HID", "DB1", "DB2", "RY", "RE", "RL", "RD", "RB", "RI", "TRI", "ONB", "KP", "KD"):
         sb(n, 128, B)
-    sb("ON128", 128); sb("IDF", 128); sb("NIF", 128); sb("LTF", 128); sb("J16", 16); sb("CT", 256); sb("CT2", 256)
-    sb("SC8", 8); sb("DSC", 8); sb("DSM", 8); sb("I8", 8)
-    sb("TGL", 256, I); sb("DI", 1280, I); sb("DS", 7 * 256, B)
-    sb("NB", 64, I); sb("NBD", 256, I); sb("NBB", 320, B); sb("DIG", 1024, B); sb("J128", 128, B)
+    sb("ON128", 128); sb("IDF", 128); sb("NIF", 128); sb("LTF", 128); sb("J16", 16); sb("CT", 256, B); sb("KID", 128)
+    sb("SC8", 8); sb("DSC", 8); sb("DSM", 8); sb("DSP", 8); sb("I8", 8)
+    sb("TGL", 256, I); sb("DI", 1280, I); sb("DS", 5 * 256, B)
+    sb("NB", 64, I); sb("NBD", 256, I); sb("NBB", 320, B); sb("DIG", 1024, B); sb("J256", 256, B)
     for n in range(8):
         S["ps%d" % n] = ("psum", [128, 512], "float32")
     return S
@@ -70,18 +78,24 @@ ARR = ["ax0", "ax1", "ax2", "af0", "af1", "af2", "aff", "ae0", "ae2", "ae3", "ae
 SEMAPHORES = ["pv", "pc", "pt", "pg"] + ARR + ["d%d" % k for k in range(60)]
 MASKS = {}
 PLAN = []
-ZK, ZT, ZN, ZM, ZY, Z1 = range(6)
+ZK, ZT, ZN, Z1 = range(4)
 
 
-def first_order(ops, tiles):
+def first_order(ops, tiles, tail):
     n = len(ops)
     succ = [[] for _ in ops]
     for k, o in enumerate(ops):
         for p, w in o["pre"].items():
             succ[p].append((k, w))
-    tail = [0.0] * n
-    for k in range(n - 1, -1, -1):
-        tail[k] = ops[k]["lat"] + max([tail[s] + (WAKE if w else 0) for s, w in succ[k]] + [0])
+    if tail is None:
+        tail, left = [0.0] * n, [len(s) for s in succ]
+        todo = [k for k in range(n) if not left[k]]
+        for k in todo:
+            tail[k] = max([ops[k]["lat"]] + [tail[s] + (WAKE + ops[k]["lat"] if w else ops[k]["busy"]) for s, w in succ[k]])
+            for x in ops[k]["pre"]:
+                left[x] -= 1
+                if not left[x]:
+                    todo.append(x)
     left = [len(o["pre"]) for o in ops]
     ready = [0.0] * n
     avail = {q: [] for q in "vctgyn"}
@@ -162,7 +176,17 @@ def gap(line, t, d):
 
 
 def plan(ops, tiles):
-    order, bank, after, span = first_order(ops, tiles)
+    best, late, rng = None, None, np.random.default_rng(0)
+    for _ in range(PASSES):
+        x = settle(ops, *first_order(ops, tiles, late))
+        if best is None or x[0] < best[0]:
+            best = x
+        at = best[0] * rng.random()
+        late = {k: v + (JIT * float(z) if abs(v - at) < WIN else JIT / 2) for (k, v), z in zip(best[4].items(), rng.random(len(ops)))}
+    return best[1:4] + best[:1]
+
+
+def settle(ops, order, bank, after, span):
     pre = [dict(o["pre"]) for o in ops]
     for k, l in after.items():
         for x in l:
@@ -195,7 +219,177 @@ def plan(ops, tiles):
         now = sorted(now, key=lambda k: (begin[k], pos[k]))
         if max(end.values()) < best[0]:
             best = (max(end.values()), now)
-    return best[1], bank, after
+    return best + (bank, after, late)
+
+
+def early(ops, pre, late):
+    left = [len(d) for d in pre]
+    succ = [[] for _ in ops]
+    for k, d in enumerate(pre):
+        for x in d:
+            succ[x].append(k)
+    avail = [k for k in range(len(ops)) if not left[k]]
+    lines, begin, end, seq = {}, {}, {}, []
+    while avail:
+        k = max(avail, key=lambda x: (late[x], -x))
+        avail.remove(k); seq.append(k)
+        o = ops[k]
+        s = max([end[x] + WAKE if w else begin[x] + ops[x]["busy"] for x, w in pre[k].items()] + [0.0])
+        begin[k] = gap(lines.setdefault(o["q"], []), s, o["busy"]) if o["busy"] else s
+        end[k] = begin[k] + o["lat"]
+        if "wire" in o:
+            end[k] = gap(lines.setdefault(o["wire"][0], []), end[k] - o["wire"][1], o["wire"][1]) + o["wire"][1]
+        for x in succ[k]:
+            left[x] -= 1
+            if not left[x]:
+                avail.append(x)
+    if len(seq) < len(ops):
+        return None
+    pos = {k: j for j, k in enumerate(seq)}
+    return sorted(seq, key=lambda k: (begin[k], pos[k])), begin, end
+
+
+def latest(ops, pre, order):
+    succ = [{} for _ in ops]
+    for k, d in enumerate(pre):
+        for x, w in d.items():
+            succ[x][k] = w
+    lines, late = {}, {}
+    for k in reversed(order):
+        o = ops[k]
+        e = max([late[x] + WAKE for x, w in succ[k].items() if w] + [0.0])
+        if "wire" in o:
+            e = gap(lines.setdefault(o["wire"][0], []), e, o["wire"][1])
+        e = max([e + o["lat"] - o["busy"]] + [late[x] for x, w in succ[k].items() if not w])
+        late[k] = (gap(lines.setdefault(o["q"], []), e, o["busy"]) if o["busy"] else e) + o["busy"]
+    return late
+
+
+def plan2(ops, tiles):
+    def behind(pre, after, a, b):
+        k = tiles[b]["ops"][0]
+        after[k] = tiles[a]["ops"]
+        pre[k] = dict(pre[k])
+        for x in after[k]:
+            pre[k][x] = pre[k].get(x, False) or ops[x]["q"] != "t"
+    base, after0, bank0 = [o["pre"] for o in ops], {}, {}
+    turn = sorted((t["nth"], j) for j, t in enumerate(tiles) if t["pool"] == "s")
+    for n, j in turn:
+        bank0[j] = n % POOLS["s"]
+        if n >= POOLS["s"]:
+            behind(base, after0, turn[n - POOLS["s"]][1], j)
+    late = [0.0] * len(ops)
+    for k in range(len(ops) - 1, -1, -1):
+        late[k] += ops[k]["lat"]
+        for x, w in base[k].items():
+            late[x] = max(late[x], late[k] + (WAKE if w else 0))
+    best, rng = None, np.random.default_rng(0)
+    for n in range(PASSES):
+        order, begin, end = early(ops, base, late)
+        pre, after, bank = list(base), dict(after0), dict(bank0)
+        last = [None] * POOLS["x"]
+        for s, j in sorted((begin[t["ops"][0]], j) for j, t in enumerate(tiles) if t["pool"] == "x" and t["ops"]):
+            b = min(range(len(last)), key=lambda b: -1 if last[b] is None else max(end[x] for x in tiles[last[b]]["ops"]))
+            if last[b] is not None:
+                behind(pre, after, last[b], j)
+            last[b] = j; bank[j] = POOLS["s"] + b
+        x = early(ops, pre, late)
+        if x is not None:
+            x = early(ops, pre, latest(ops, pre, x[0]))
+            span = max(x[2].values())
+            if best is None or span < best[3]:
+                best = (x[0], bank, after, span, latest(ops, base, x[0]))
+        if best is None:
+            late = latest(ops, base, order)
+        else:
+            at = best[3] * rng.random()
+            late = {k: v + (JIT * float(z) if abs(v - at) < WIN else JIT / 2) for (k, v), z in zip(best[4].items(), rng.random(len(ops)))}
+    return best
+
+
+def polish(ops, order, after):
+    n = len(ops)
+    pre = [dict(o["pre"]) for o in ops]
+    for k, l in after.items():
+        for x in l:
+            pre[k][x] = pre[k].get(x, False) or ops[x]["q"] != "t"
+    busy = [o["busy"] for o in ops]; lat = [o["lat"] for o in ops]; wire = [o["wire"][1] if "wire" in o else 0 for o in ops]
+    pw = [[x for x, w in d.items() if w] for d in pre]; po = [[x for x, w in d.items() if not w] for d in pre]
+    sw, so = [[] for _ in ops], [[] for _ in ops]
+    for k in range(n):
+        for x in pw[k]:
+            sw[x].append(k)
+        for x in po[k]:
+            so[x].append(k)
+    mp, mn, wp, wn, last = [-1] * n, [-1] * n, [-1] * n, [-1] * n, {}
+    for k in order:
+        for key, a, b in [(ops[k]["q"], mp, mn)] * (ops[k]["q"] != "n") + ([(ops[k]["wire"][0], wp, wn)] if wire[k] else []):
+            if key in last:
+                a[k] = last[key]; b[last[key]] = k
+            last[key] = k
+    best, tabu, order = None, {}, list(order)
+    for it in range(SWAPS):
+        hb, jb, he, tb, jt, te = [0.0] * n, [0.0] * n, [0.0] * n, [0.0] * n, [0.0] * n, [0.0] * n
+        for k in order:
+            s = 0.0
+            for x in pw[k]:
+                if he[x] + WAKE > s:
+                    s = he[x] + WAKE
+            for x in po[k]:
+                if hb[x] + busy[x] > s:
+                    s = hb[x] + busy[x]
+            jb[k] = s
+            x = mp[k]
+            if x >= 0 and hb[x] + busy[x] > s:
+                s = hb[x] + busy[x]
+            hb[k] = s; he[k] = s + lat[k]
+            if wp[k] >= 0 and he[wp[k]] + wire[k] > he[k]:
+                he[k] = he[wp[k]] + wire[k]
+        span = max(he)
+        if best is None or span < best[0] - 1e-6:
+            best = (span, sorted(range(n), key=lambda j: (hb[order[j]], j)), list(order))
+        for k in reversed(order):
+            e = 0.0
+            for x in sw[k]:
+                if tb[x] + WAKE > e:
+                    e = tb[x] + WAKE
+            if wn[k] >= 0 and te[wn[k]] + wire[wn[k]] > e:
+                e = te[wn[k]] + wire[wn[k]]
+            te[k] = e; e += lat[k]
+            for x in so[k]:
+                if tb[x] + busy[k] > e:
+                    e = tb[x] + busy[k]
+            jt[k] = e
+            if mn[k] >= 0 and tb[mn[k]] + busy[k] > e:
+                e = tb[mn[k]] + busy[k]
+            tb[k] = e
+        pick = None
+        for a in order:
+            b = mn[a]
+            if b < 0 or wire[a] or wire[b] or a in pre[b] or hb[a] + busy[a] + tb[b] < span - 1e-6:
+                continue
+            rb = max(jb[b], hb[mp[a]] + busy[mp[a]] if mp[a] >= 0 else 0.0); ra = max(jb[a], rb + busy[b])
+            qa = max(jt[a], busy[a] + tb[mn[b]] if mn[b] >= 0 else 0.0); qb = max(jt[b], busy[b] + qa)
+            est = max(rb + qb, ra + qa)
+            if (tabu.get((a, b), -1) < it or est < best[0] - 1e-6) and (pick is None or est < pick[0]):
+                pick = (est, a, b)
+        if pick is None:
+            break
+        _, a, b = pick
+        tabu[(b, a)] = it + TABU + (it * 7) % 11
+        x, y = mp[a], mn[b]
+        mp[b], mn[b], mp[a], mn[a] = x, a, b, y
+        if x >= 0:
+            mn[x] = b
+        if y >= 0:
+            mp[y] = a
+        i, j = order.index(a), order.index(b)
+        need, up = {b}, []
+        for k in reversed(order[i + 1:j + 1]):
+            if k in need:
+                up.append(k); need.update(pre[k]); need.update((mp[k], wp[k]))
+        order[i:j + 1] = up[::-1] + [k for k in order[i:j + 1] if k not in need or k == a]
+    return [best[2][j] for j in best[1]], best[0]
 
 
 def rank_program(g, core, T, topo):
@@ -205,7 +399,7 @@ def rank_program(g, core, T, topo):
     eng = {"v": g.vector, "c": g.scalar, "t": g.tensor, "g": g, "y": g.sync}
     psem = {"v": "pv", "c": "pc", "t": "pt", "g": "pg"}
     ops, tiles, bank = [], [], {}
-    W, R = {}, {}
+    W, R, named, part = {}, {}, {}, ["", 0]
     nd = [0]
     A_ = slice(None)
 
@@ -260,6 +454,8 @@ def rank_program(g, core, T, topo):
                 if e[0] & m:
                     pre[e[1]] = True
         op = dict(q=q, fns=fns, pre=pre, busy=busy, lat=busy if lat is None else lat, dma=dma, tiles=sorted({o["tile"] for o in ins + outs if o["tile"] is not None}))
+        if wt:
+            named.setdefault(("%s%s%d" % (part[0], wt[0][0], (wt[0][1] & -wt[0][1]).bit_length() - 1), part[1]), k)
         for tl in op["tiles"]:
             t = tiles[tl]
             if not t["ops"]:
@@ -299,8 +495,8 @@ def rank_program(g, core, T, topo):
     def dma(q, out, in_, accum=False, rows=None, after=()):
         s = "d%d" % nd[0]; nd[0] += 1
         kw = dict(accum_op=O.add) if accum else {}
-        d = 300 + 128 * min(out["n"], in_["n"]) * out["size"] * DMAB
-        k = record(q, [lambda: eng[q].dma_start(val(out), val(in_), **kw)], [out], [in_], 1000 if q == "g" else 60, DMA0 + d, (s, 16, True), rows)
+        d = 500 + 128 * min(out["n"], in_["n"]) * out["size"] * DMAB * (2 if accum else 1)
+        k = record(q, [lambda: eng[q].dma_start(val(out), val(in_), **kw)], [out], [in_], 600 if q == "g" else 50, DMA0 + d, (s, 16, True), rows)
         ops[k]["wire"] = ("dma", d)
         for x in after:
             ops[k]["pre"].setdefault(x, False)
@@ -384,15 +580,13 @@ def rank_program(g, core, T, topo):
     VW, DW = c("V", 0, 4096), c("DG", 0, 4096)
 
     k = []
-    for o, i in ((r("CI"), "cx"), (r("TGL"), "tg"), (VW, "xr"), (r("QX"), "qx"), (r("LFH"), "lf")):
-        k = [dma("y", o, r(i), after=k)]
-    dma("y", r("XLH"), r("xl"), after=k)
+    for n in LOADS:
+        k = [dma("y", {"cx": r("CI"), "tg": r("TGL"), "xr": VW, "qx": r("QX"), "lf": r("LFH")}[n], r(n), after=k)]
     cp(r("CU"), r("CI")); cp(c("CF", 0, 256), r("CI"))
     act(c("Q", 0, 256), r("QX"), F.Identity, 192.0)
-    cp(r("LFS"), r("LFH"))
-    first = send(3, "LF0", 1024, r("LFS"), "af0")
-    second = send(3, "XL0", 1024, r("XLH"), "ax0", [first - 1])
-    send(2, "LF1", 1024, r("LFS"), "af1", [second]); send(2, "XL1", 1024, r("XLH"), "ax1", [second]); send(1, "XL2", 1024, r("XLH"), "ax2", [second])
+    cp(r("HU"), r("LFH")); cp(r("LFS"), r("LFH"))
+    first = send(3, "U0", 1024, r("HU"), "af0")
+    cp(c("LF0", 0, 1024), r("U0"))
 
     iota(c("IP", 0, 1), [[1, 1]], 0, 1)
     iota(r("J16"), [[1, 16]], 0, 0, True)
@@ -402,12 +596,12 @@ def rank_program(g, core, T, topo):
     aff(r("BO1"), r("ON128"), [[-16, 8], [0, 16]], 0, 1)
     aff(r("BO"), r("BO1"), [[16, 8], [0, 16]], 15, -1)
     aff(r("LTF"), r("BO"), [[1, 128]], -1, -1)
-    iota(c("DS", 1280, 1536), [[1, 256]], 0, 0, True)
+    iota(r("J256"), [[1, 256]], 0, 0, True)
     iota(r("NB"), [[1, 64]], 0, 64)
-    iota(r("J128"), [[1, 128]], 0, 0, True)
     for k in range(2):
         iota(c("NAME", 1024 * k, 1024 * k + 1024), [[1, 1024]], 1024 * k, 0, True)
         act(c("NAME", 2048 + 1024 * k, 3072 + 1024 * k), c("NAME", 1024 * k, 1024 * k + 1024), F.Identity, 2048.0)
+    act(c("NAME", 4096, 4224), c("NAME", 0, 128), F.Identity, 4096.0)
     ts(c("IP", 1, 2), c("IP", 0, 1), 15, AND); ts(c("IP", 2, 3), c("IP", 0, 1), 4, SHR, 1, AND)
     cp(col(0), c("IP", 1, 2)); cp(col(1), c("IP", 2, 3))
     ts(r("OH"), r("J16"), col(0), O.is_equal)
@@ -419,9 +613,11 @@ def rank_program(g, core, T, topo):
     ts(col(20), col(1), B26, O.mult, B23, O.add); ts(col(21), col(1), -B26, O.mult, B26 + B23, O.add)
     ts(col(26), oh(1), 32.0, O.mult); ts(col(27), oh(2), 256.0, O.mult, col(26), O.add); ts(col(28), oh(3), 2048.0, O.mult, col(27), O.add)
     ts(col(4), oh(0), 16.0, O.mult, col(28), O.add)
-    ts(col(29), oh(0), -16.0, O.mult, col(28), O.add); ts(col(8), oh(9), 4096.0, O.mult, col(29), O.add)
+    ts(col(29), col(0), 4.0, O.is_lt, oh(9), O.add); ts(col(8), oh(0), -2.0, O.mult, col(29), O.add)
+    ts(col(16), col(0), 5.0, O.is_ge)
     ts(col(30), oh(4), 16.0, O.mult); ts(col(11), col(4), 2.0, O.mult, col(30), O.add)
-    ts(col(5), oh(6), 256.0, O.mult, oh(5), O.add); ts(col(12), oh(9), 8192.0, O.mult, col(5), O.add)
+    ts(col(5), oh(6), 256.0, O.mult, oh(5), O.add); ts(col(17), oh(9), 8192.0, O.mult, col(5), O.add)
+    tt(col(12), col(17), col(4), O.add)
     ts(col(6), oh(4), -B24, O.mult); ts(col(13), oh(9), B23, O.mult)
     ts(col(9), col(0), 5.0, O.is_lt); tt(col(14), oh(5), oh(6), O.add)
     ts(col(19), col(4), -1.0, O.mult); ts(col(15), oh(6), 16.0, O.mult)
@@ -432,39 +628,45 @@ def rank_program(g, core, T, topo):
     tt(c("TF", 32, 48), r("OH"), r("POW"), O.mult)
     record("v", [lambda: g.vector.tensor_reduce(val(col(7)), val(c("TF", 32, 48)), AxisListType.X, O.add)], [col(7)], [c("TF", 32, 48)], 64 * CYC)
     ms(r("ZZ"), 0.0)
-    for z, w in ((ZK, 65536.0), (ZT, col(4)), (ZN, col(12)), (ZM, col(8)), (ZY, col(11)), (Z1, 512.0)):
+    for z, w in ((ZK, 65536.0), (ZT, col(4)), (ZN, col(12)), (Z1, 512.0)):
         scaled(zcols(z), c("BO", 0, 128, 16), w)
     scaled(c("WN", 0, 8), c("BO", 0, 128, 16), col(19)); scaled(c("WN", 8, 16), c("BO", 0, 128, 16), -65536.0)
-    for n, w in (("ID", 1.0), ("NID", -1.0), ("HID", 0.5), ("DB1", -2.0 ** 28), ("DB2", B26), ("NIF", -1.0), ("KP", col(14))):
+    for n, w in (("ID", 1.0), ("NID", -1.0), ("HID", 0.5), ("DB1", -2.0 ** 28), ("DB2", B26), ("KP", col(14)), ("KD", col(9))):
         scaled(r(n), r("IDF"), w)
     scaled(c("KP", 4, 128, 16), c("BO", 0, 128, 16), col(10))
-    for n, w in (("RN", col(5)), ("RE", col(6)), ("RL", col(4)), ("RD", col(7)), ("RB", 65536.0), ("RI", col(13))):
+    for n, w in (("RY", col(11)), ("RE", col(6)), ("RL", col(4)), ("RD", col(7)), ("RB", 65536.0), ("RI", col(13))):
         scaled(r(n), r("BO"), w)
     tt(r("BO1"), r("LTF"), r("IDF"), O.subtract); scaled(r("TRI"), r("BO1"), B23)
-    ms(r("ONB"), 1.0); ms(r("ZR"), 0.0)
-    ts(c("CT2", 0, 16), r("POW"), 2.0, O.mult)
+    ms(r("ONB"), 1.0); scaled(r("KID"), r("IDF"), 1024.0)
+    ts(c("CT", 0, 16), r("POW"), 2.0, O.mult)
     for k in (16, 32, 64, 128):
-        act(c("CT2", k, 2 * k), c("CT2", 0, k))
-    act(r("CT"), r("CT2"), F.Copy, -1048576.0)
+        act(c("CT", k, 2 * k), c("CT", 0, k))
     ms(r("RST"), 0.0); ms(c("RST", 0, 512, 32), BIG)
     ms(r("RS2"), 1.0); ms(c("RS2", 0, 768, 192), 0.0); ms(r("ONE"), 1.0); ms(c("PX", 256, 304), 1024.0)
-    ts(r("SC8"), r("I8"), col(0), O.add, 0.5, O.add); ts(r("DSC"), r("I8"), col(0), O.add, 4096.0, O.add); ts(r("DSM"), r("I8"), col(0), O.add, 1023.0, O.add)
+    ts(r("DSC"), r("I8"), col(0), O.add, 4096.0, O.add); ts(r("SC8"), r("DSC"), 2.0, O.mult, -8191.0, O.add)
+    ts(r("DSM"), r("DSC"), -3073.0 - 8192, O.add); ts(r("DSP"), r("DSC"), -8192.0, O.add)
     ms(c("Q", 256, 272), 192.0); ms(c("CF", 256, 272), 0.0); ms(c("H1", 256, 272), 0); ms(c("H2", 256, 272), 0); ms(c("V", 4096, 4224), 0.0)
     scaled(c("DD", 256, 272), c("ON128", 0, 16), oh(9))
-    for h in range(2):
-        ms(c("DG", 2048 * h, 2048 * h + 2048), 0.0)
-    act(c("DG", 4096, 4224), r("J128"), F.Identity, col(15), oh(5))
+    ts(c("TF", 48, 64), r("J16"), oh(6), O.mult)
+    for j in range(16):
+        if j % 2:
+            act(c("DG", 256 * j, 256 * j + 256), r("J256"), F.Identity, c("TF", 48 + j, 49 + j), oh(5))
+        else:
+            ts(c("DG", 256 * j, 256 * j + 256), r("J256"), oh(5), O.mult, c("TF", 48 + j, 49 + j), O.add)
+    act(c("DG", 4096, 4224), c("J256", 0, 128), F.Identity, col(15), oh(5))
     for j, (s, m) in enumerate(((1, 1), (2, 7), (5, 7), (8, 7), (0, 1))):
         ts(c("DI", j * 256, (j + 1) * 256), r("TGL"), s, SHR, m, AND)
     ts(c("DS", 0, 1280), r("DI"), 0.0625, O.mult)
-    act(c("DS", 1536, 1792), c("DS", 1280, 1536), F.Identity, col(0), 0.0)
-    k = [dma("y", r("DG", slice(f, None, 16), slice(0, 4096)), c("DS", f * 256, f * 256 + 256), rows="DG") for f in range(7)]
-    dma("y", r("FD"), r("fd"), after=k)
+    k = [dma("y", r("DG", slice(f, None, 16), slice(0, 4096)), c("DS", f * 256, f * 256 + 256), rows="DG") for f in range(5)]
+    k = [dma("y", r("XLH"), r("xl"), after=k)]
+    k = [dma("y", r("FD"), r("fd"), after=k)]
+    second = send(3, "XL0", 1024, r("XLH"), "ax0", [first - 1])
+    send(2, "LF1", 1024, r("LFS"), "af1", [second])
     for j, (s, m) in enumerate(((0, 1), (1, 7), (4, 7), (7, 7))):
         ts(c("NBD", 64 * j, 64 * j + 64), r("NB"), s, SHR, m, AND)
     ts(c("NBB", 0, 256), r("NBD"), 0.0625, O.mult); ms(c("NBB", 256, 320), 0.0625); ms(r("DIG"), 0.0)
     for f in range(5):
-        dma("y", r("DIG", slice(f, None, 16)), c("NBB", 64 * f, 64 * f + 64), rows="DIG")
+        dma("y", r("DIG", slice(f, None, 16)), c("NBB", 64 * f, 64 * f + 64), rows="DIG", after=k)
     for h in range(2):
         ts(c("FW", 1024 * h, 1024 * h + 1024), c("FD", 1024 * h, 1024 * h + 1024), 4095, AND)
         ts(c("FW", 2048 + 1024 * h, 3072 + 1024 * h), c("FD", 1024 * h, 1024 * h + 1024), 12, SHR)
@@ -475,42 +677,49 @@ def rank_program(g, core, T, topo):
         mm(*[(p(b, ii * 64, ii * 64 + 64), r("ID"), c("XD", x0 + 8 * u + ii, x0 + 1024, 16)) for ii in range(8)], start=False)
         act(out, p(b, 0, 512), F.Abs)
 
-    def keys():
-        act(r("CE"), c("CF", 0, 256), F.Identity, col(2)); act(r("CO"), c("CF", 0, 256), F.Identity, col(3))
-
     def choice(t):
         LF = c("LF%d" % (t % 3), 0, 1024)
+        part[:] = "c", t
         for lo, hi, q in (CHOICE if t else CHOICE0):
             gat(q, c("XD", 16 * lo, 16 * hi), VW, c("CU", lo, hi), 192.0)
         if t == 0:
-            for f in range(4):
-                dma("g", r("V", slice(f, None, 16), slice(0, 4096)), c("DS", f * 256, f * 256 + 256), True, rows="V")
+            for j in range(8):
+                b = tile()
+                mm((p(b, 0, 512), r("ID"), c("V", 512 * j, 512 * j + 512)), (p(b, 0, 512), r("KD"), c("DG", 512 * j, 512 * j + 512)))
+                act(c("V", 512 * j, 512 * j + 512), p(b, 0, 512))
         else:
             claims(t - 1); disk_write(t - 1)
+        part[:] = "c", t
         PC = tile()
         for lo, hi in PARTS:
-            PA, PN = tile(), tile()
+            PA = tile()
             b0, b1 = lo // 16, hi // 16
-            for k in range(hi // 64 - 1, lo // 64 - 1, -1):
+            mm((p(PA, lo, hi), r("IDF"), c("CF", lo, hi)), stop=False)
+            blocks = [k for k in (BLOCKS if t else BLOCKS0) if lo <= 64 * k < hi]
+            for k in blocks:
                 for u in range(2):
                     j = 8 * k + 4 * u
                     sub(1024 * k, "Q", 64 * k, u, r("AB", A_, slice(j, j + 4)))
-                    mm(*[(p(PA, 64 * k, 64 * k + 64), sel(ZK, 8 * u + ii), r("AB", A_, j + ii // 2, slice(64 * (ii % 2), 64 * (ii % 2) + 64))) for ii in range(8)], start=u == 0, stop=u == 1)
-            tt(r("KEY", A_, slice(b0, b1), slice(0, 16)), p(PA, lo, hi), r("CE", A_, slice(b0, b1)), O.add)
-            tt(r("KEY", A_, slice(b0, b1), slice(16, 32)), p(PA, lo, hi), r("CO", A_, slice(b0, b1)), O.add)
+                    mm(*[(p(PA, 64 * k, 64 * k + 64), sel(ZK, 8 * u + ii), r("AB", A_, j + ii // 2, slice(64 * (ii % 2), 64 * (ii % 2) + 64))) for ii in range(8)],
+                       start=False, stop=u == 1 and k == blocks[-1])
+            act(r("KEY", A_, slice(b0, b1), slice(0, 16)), p(PA, lo, hi), F.Identity, col(2))
+            act(r("KEY", A_, slice(b0, b1), slice(16, 32)), p(PA, lo, hi), F.Identity, col(3))
             trn(c("KT", 2 * lo, 2 * hi), r("KEY", A_, slice(b0, b1)))
             scan(c("SCN", 2 * lo, 2 * hi), c("RST", 2 * lo, 2 * hi), c("KT", 2 * lo, 2 * hi), BIG, O.max, O.min)
             cp(c("OI", b0, b1), c("SCN", 2 * lo + 31, 2 * hi, 32))
             ts(c("OI", b0, b1), c("OI", b0, b1), 4095, AND)
             cp(c("OU", b0, b1), c("OI", b0, b1)); cp(c("OF", b0, b1), c("OI", b0, b1))
-            gat("v", c("OR", lo, hi), r("NAME"), c("OU", b0, b1))
-            gat("c", c("DD", lo, hi), DW, c("OU", b0, b1))
+            gat("v", c("OR", lo, hi), c("NAME", 0, 4096), c("OU", b0, b1))
             for b in range(b0, b1):
                 ts(r("EQ", A_, b, slice(0, 256 - 16 * b)), c("OR", 16 * b, 256), c("OF", b, b + 1), O.is_equal)
                 if b < 15:
                     opens = b == PARTS[0][0] // 16
-                    mm(*[(p(PC, 0, 256), r("ZR"), r("ONE"))] * opens, (p(PC, 16 * b + 16, 256), r("RB"), r("EQ", A_, b, slice(16, 256 - 16 * b))), start=opens, stop=False)
+                    mm(*[(p(PC, 0, 256), r("NID"), r("CT"))] * opens, (p(PC, 16 * b + 16, 256), r("RB"), r("EQ", A_, b, slice(16, 256 - 16 * b))), start=opens, stop=False)
             mm((p(PC, lo, hi), r("RD"), r("EQ", A_, slice(b0, b1), slice(0, 16))), start=False, stop=False)
+        for lo, hi in HASHES:
+            PN = tile()
+            b0, b1 = lo // 16, hi // 16
+            gat("c", c("DD", lo, hi), DW, c("OU", b0, b1))
             mm(*wrap(p(PN, b0, b1), ZT, "DD", lo, hi))
             cp(c("NA", b0, b1), p(PN, b0, b1))
             for w, (add, less, sh) in enumerate(((4.0, 16.0, 3), (592.0, 592.0 ** 2 - 32, 5))):
@@ -518,8 +727,8 @@ def rank_program(g, core, T, topo):
                 ts(c("HI", 256 * w + lo, 256 * w + hi), c("Y", 256 * w + lo, 256 * w + hi), less, O.subtract)
                 ts(c("H%d" % (w + 1), lo, hi), c("HI", 256 * w + lo, 256 * w + hi), sh, SHR, 4095, AND)
         mm((p(PC, 0, 256), r("RE"), c("DD", 0, 256)), start=False)
-        tt(r("CA"), p(PC, 0, 256), r("CT"), O.is_lt)
-        scan(c("PX", 0, 256), r("ONE"), r("CA"), 0.0, O.mult, O.add)
+        act(r("CA"), p(PC, 0, 256), F.Sign, -1048576.5, -1.0)
+        scan(c("PX", 0, 256), r("ONE"), r("CA"), 0.0, O.add, O.add)
         for b in range(4):
             act(r("JS", A_, b, slice(0, 304 - 32 * b)), c("PX", 16 * b, 304 - 16 * b), F.Sign, c("SC8", b, b + 1), -1.0, c("LS", b, b + 1))
             ts(c("JV", 192 * b, 192 * b + 192), c("PX", 64, 256), c("SC8", 4 + b, 5 + b), O.is_le)
@@ -528,15 +737,20 @@ def rank_program(g, core, T, topo):
         ts(c("LU", 0, 4), r("LS"), 0.5, O.mult, 152.0, O.add)
 
     def translate(t):
+        part[:] = "t", t
         LF, XL = c("LF%d" % (t % 3), 0, 1024), r("XL%d" % (t % 3))
         gat("v", c("CCU", 0, 128), r("H1"), r("LU")); gat("v", c("CCU", 128, 256), r("H2"), r("LU"))
         gat("c", r("QR"), r("Q"), r("LU")); gat("c", r("DDR"), r("DD"), r("LU")); gat("v", r("CRU"), r("CF"), r("LU"))
         for w, lo, hi, q in TRANS:
             gat(q, c("XG", 2048 * w + 16 * lo, 2048 * w + 16 * hi), VW, c("CCU", 128 * w + lo, 128 * w + hi))
         PL, PT, PD, PS, PQ = tile(), tile(), tile(), tile(), tile()
-        mm(*wrap(p(PL, 0, 8), ZT, "DDR", 0, 128)); mm(*wrap(p(PL, 8, 16), ZN, "DDR", 0, 128)); mm((p(PL, 128, 256), r("RL"), r("DDR")))
-        cp(r("NU"), p(PL, 0, 8)); tt(r("OUF"), p(PL, 8, 16), r("DSC"), O.min); cp(r("OUR"), r("OUF"))
-        gat("c", r("BF"), LF, r("NU")); gat("c", r("A"), XL, r("NU")); scaled(r("DDM"), r("DDR"), col(9))
+        for j, w in enumerate((9, 16, 8)):
+            ts(r("ROW", A_, j), r("DDR"), col(w), O.mult)
+        mm(*[(p(PL, 0, 24), sel(ZN, a), r("ROW", A_, A_, slice(a, 128, 16))) for a in range(16)]); mm((p(PL, 128, 256), r("RL"), r("DDR")))
+        cp(r("NU"), p(PL, 0, 8)); tt(r("OUF"), p(PL, 8, 16), r("DSC"), O.min); cp(r("OUR"), r("OUF")); cp(r("MF"), p(PL, 16, 24))
+        gat("v", r("BF"), LF, r("NU")); gat("v", r("A"), XL, r("NU"))
+        PB = tile()
+        mm((p(PB, 0, 128), r("BF"), r("IDF"))); ts(r("BT"), p(PB, 0, 128), -451584.0, O.add)
         for b in range(8):
             ts(r("EQ3", A_, b, slice(0, 128 - 16 * b)), p(PL, 128 + 16 * b, 256), p(PL, b, b + 1), O.is_equal)
         cp(r("CC"), r("CCU")); tt(r("D12"), c("CC", 128, 256), c("CC", 0, 128), O.subtract)
@@ -547,9 +761,9 @@ def rank_program(g, core, T, topo):
                 for u in range(2):
                     sub(x0, "QR", 64 * h, u, r("AB", A_, slice(16 * w + 8 * u, 16 * w + 8 * u + 8), slice(64 * h, 64 * h + 64)))
             for x, z in (("XG", zcols(ZT)), ("XD", c("WN", 0, 8))):
-                mm(*[(p(PT, 128 * w + i, 128 * w + 128, 16), c(x, 2048 * w + i, 2048 * w + 2048, 16), z) for i in range(16)], start=w == 0 and x == "XG", stop=False)
-            mm((p(PT, 128 * w, 128 * w + 128), r("BF"), r("NIF")), start=False, stop=w == 1)
-        ts(r("IN"), p(PT, 0, 256), -451584.0, O.is_equal)
+                mm(*[(p(PT, 128 * w + i, 128 * w + 128, 16), c(x, 2048 * w + i, 2048 * w + 2048, 16), z) for i in range(16)], start=w == 0 and x == "XG", stop=w == 1 and x == "XD")
+        for w in range(2):
+            tt(c("IN", 128 * w, 128 * w + 128), p(PT, 128 * w, 128 * w + 128), r("BT"), O.is_equal)
         for w in range(2):
             for u in range(2):
                 if w == 1 and u == 1:
@@ -562,49 +776,57 @@ def rank_program(g, core, T, topo):
         cp(ind(r("FW"), r("OUR")), r("SS"))
         if t < STEPS - 1:
             gat("v", r("CU"), c("FW", 0, 4096), r("OU"))
-        tt(ind(r("V"), r("OUR")), r("A"), r("DDM"), O.add)
+        tt(ind(r("V"), r("OUR")), r("A"), r("ROW", A_, 0), O.add)
         gat("c", r("XO"), VW, r("OU"), 192.0)
         mm((p(PQ, 0, 256), r("HID"), c("Q", 0, 256)), (p(PQ, 0, 256), r("HID"), r("XO")))
         act(c("Q", 0, 256), p(PQ, 0, 256), F.Identity, -0.25)
-        act(r("DDE"), r("DDR"), F.Identity, col(36 + t))
+        ts(r("DDE"), r("DDR"), col(36 + t), O.add)
         cp(ind(r("DG"), r("OUR")), r("DDE"))
-        for h in range(2):
-            gat("c", c("GS", 1024 * h, 1024 * h + 1024), DW, c("CRU", 64 * h, 64 * h + 64))
-        gat("v", c("CF", 0, 256), c("FW", 0, 4096), r("OU"))
+        for lo, hi, q in (NAMES if t < STEPS - 1 else NAMES3):
+            gat(q, c("GS", 16 * lo, 16 * hi), DW, c("CRU", lo, hi))
         if t < STEPS - 1:
-            keys()
+            cp(c("CF", 0, 256), r("CU"))
+        else:
+            gat("v", c("CF", 0, 256), c("FW", 0, 4096), r("OU"))
 
     def lower(b, eq, fl):
-        mm((p(b, 0, 128), r("RD"), r(eq, A_, A_, slice(0, 16))), *[(p(b, 16 * j + 16, 128), r("RB"), r(eq, A_, j, slice(16, 128 - 16 * j))) for j in range(7)])
-        tt(r(fl), p(b, 0, 128), c("CT2", 0, 128), O.is_ge)
+        mm((p(b, 0, 128), r("RD"), r(eq, A_, A_, slice(0, 16))), (p(b, 0, 128), r("NID"), c("CT", 0, 128)),
+           *[(p(b, 16 * j + 16, 128), r("RB"), r(eq, A_, j, slice(16, 128 - 16 * j))) for j in range(7)])
+        act(r(fl), p(b, 0, 128), F.Sign, 0.5)
 
     def apply(lst, x, n, u):
-        ts(r(u), lst, 1.0, O.add)
+        ts(r(u), lst, 8193.0, O.add)
         cp(ind(r(n), r(u)), x)
 
     def disk_write(t):
         a, b, s = tile(), tile(), tile()
+        part[:] = "d", t + 1
         lower(a, "EQ3", "FM")
-        mm(*wrap(p(b, 0, 8), ZM, "DDR", 0, 128), *wrap(p(b, 0, 8), Z1, "FM", 0, 128))
+        mm((p(b, 0, 8), r("IDF"), r("MF")), *wrap(p(b, 0, 8), Z1, "FM", 0, 128))
         tt(c("SF", 128, 136), p(b, 0, 8), r("DSM"), O.min)
         mm(*[(p(s, 0, 128), sel(ZT, i), c("GS", i, 2048, 16)) for i in range(16)])
         act(c("SF", 0, 128), p(s, 0, 128))
         to = (((3, 0, "LF1"),), ((3, 2, "LF2"), (1, 3, "LF0")), ((2, 4, "LF0"),), ((1, 5, "YL"),))[t]
         for dst, k, n in to:
-            send(dst, "E%d" % k, 136, r("SF"), "ae%d" % k)
+            last = send(dst, "E%d" % k, 136, r("SF"), "ae%d" % k)
+        if t == 0:
+            send(2, "XL1", 1024, r("XLH"), "ax1", [last - 1])
         if t in (0, 2):
             apply(c("SF", 128, 136), c("SF", 0, 128), "LF%d" % t, "MU")
-            send(*((2, "LF2", 1024, c("LF0", 0, 1024), "af2"), (3, "YL", 1024, c("LF2", 0, 1024), "aff"))[t // 2])
+            last = send(*((2, "LF2", 1024, c("LF0", 0, 1024), "af2"), (3, "YL", 1024, c("LF2", 0, 1024), "aff"))[t // 2])
+        if t == 0:
+            send(1, "XL2", 1024, r("XLH"), "ax2", [last - 1])
         for dst, k, n in to:
             apply(c("E%d" % k, 128, 136), c("E%d" % k, 0, 128), n, "MX")
 
     def claims(t):
         a, b, n, v, e, w = tile(), tile(), tile(), tile(), tile(), tile()
+        part[:] = "k", t + 1
         mm((p(a, 0, 128), c("IN", 0, 128), r("ID")), (p(a, 0, 128), c("IN", 128, 256), r("ID")))
         act(r("NEW"), p(a, 0, 128), F.Relu, 1.0, -1.0)
-        mm((p(b, 0, 128), r("TRI"), r("NEW")), (p(b, 0, 128), r("IDF"), r("BF")), (p(b, 0, 128), r("RI"), r("DDR")))
-        act(r("KE"), r("SS"), F.Identity, col(20), 1024.0); act(r("KO"), r("SS"), F.Identity, col(21), 1024.0)
-        tt(r("KEC", A_, A_, slice(0, 16)), p(b, 0, 128), r("KE"), O.add); tt(r("KEC", A_, A_, slice(16, 32)), p(b, 0, 128), r("KO"), O.add)
+        mm((p(b, 0, 128), r("TRI"), r("NEW")), (p(b, 0, 128), r("IDF"), r("BF")), (p(b, 0, 128), r("RI"), r("DDR")), stop=False)
+        mm((p(b, 0, 128), r("KID"), r("SS")), start=False)
+        act(r("KEC", A_, A_, slice(0, 16)), p(b, 0, 128), F.Identity, col(20)); act(r("KEC", A_, A_, slice(16, 32)), p(b, 0, 128), F.Identity, col(21))
         trn(r("KTC"), r("KEC"))
         scan(r("SNC"), c("RST", 0, 256), r("KTC"), BIG, O.max, O.min)
         cp(r("KI"), c("SNC", 31, 256, 32))
@@ -613,21 +835,28 @@ def rank_program(g, core, T, topo):
         cp(r("PU"), r("PF")); cp(r("BU"), r("BW"))
         act(r("NMP"), ind(r("DG"), r("PU")), F.Copy, 0.0, col(32 + t))
         gat("c", r("DB"), r("DIG"), r("BU"))
-        mm((p(n, 0, 128), r("RN"), r("NMP")))
+        gat("v", r("PLR"), r("NAME"), r("PU"))
         mm((p(v, 0, 128), r("KP"), r("NMP")), (p(v, 0, 128), r("ID"), r("DB")))
         act(r("NV"), p(v, 0, 128))
         for j in range(8):
-            ts(r("EQ2", A_, j, slice(0, 128 - 16 * j)), p(n, 16 * j, 128), c("PF", j, j + 1), O.is_equal)
+            ts(r("EQ2", A_, j, slice(0, 128 - 16 * j)), c("PLR", 16 * j, 128), c("PF", j, j + 1), O.is_equal)
         lower(e, "EQ2", "FL")
         mm((p(w, 0, 8), r("IDF"), r("PF")), *wrap(p(w, 0, 8), Z1, "FL", 0, 128))
-        tt(r("P2"), p(w, 0, 8), r("DSC"), O.min)
-        cp(r("PU2"), r("P2"))
-        cp(ind(r("DG"), r("PU2")), r("NV"))
+        tt(r("P2"), p(w, 0, 8), r("DSP"), O.min)
+        ts(r("PU2"), r("P2"), 8192.0, O.add)
         if t < STEPS - 1:
+            cp(ind(r("DG"), r("PU2")), r("NV"))
             ts(r("XP"), ind(r("V"), r("PU")), ROUND, O.add, ROUND, O.subtract)
             tt(ind(r("V"), r("PU2")), r("XP"), r("DB"), O.add)
+        else:
+            for j in range(8):
+                b = tile("s")
+                mm((p(b, 0, 512), r("RY"), c("DG", 512 * j, 512 * j + 512)))
+                act(c("YT", 512 * j, 512 * j + 512), p(b, 0, 512))
+            mm((p(n, 0, 128), r("RY"), r("NV")))
+            act(r("NY"), p(n, 0, 128))
+            cp(ind(r("YT"), r("PU2")), r("NY"))
 
-    keys()
     for t in range(STEPS):
         choice(t)
         translate(t)
@@ -636,14 +865,18 @@ def rank_program(g, core, T, topo):
     dma("y", r("yq"), r("YQ"))
     claims(STEPS - 1); disk_write(STEPS - 1)
     dma("y", r("yl"), c("YL", 0, 1024))
-    b = tile()
-    mm(*[(p(b, 0, 256), sel(ZY, j), c("DG", 256 * j, 256 * j + 256)) for j in range(16)])
-    act(r("TY"), p(b, 0, 256))
-    dma("y", r("yt"), r("TY"))
+    dma("y", r("yt"), r("YT", slice(0, None, 16), slice(0, 4096)))
 
+    for t in range(STEPS):
+        for line in FIXED:
+            l = [named[n, t] for n in line.split() if (n, t) in named]
+            for a, b in zip(l, l[1:]):
+                ops[b]["pre"].setdefault(a, False)
     if not PLAN:
-        PLAN.append(plan(ops, tiles))
-    order, banks, after = PLAN[0]
+        x = (plan, plan2)[WHICH](ops, tiles)
+        y = polish(ops, x[0], x[2])
+        PLAN.append((y[0], x[1], x[2], y[1], x[3]))
+    order, banks, after = PLAN[0][:3]
     bank.update(banks)
     cnt = {q: 0 for q in psem}
     know = {q: {} for q in eng}

import numpy as np
from concourse.mybir import AluOpType as O, AxisListType, ActivationFunctionType as F

STEPS = 4
CHOICE0 = ((192, 256, "c"), (128, 192, "v"), (64, 128, "v"), (32, 64, "c"), (0, 32, "v"))
CHOICE = ((192, 256, "c"), (128, 192, "v"), (64, 128, "c"), (0, 64, "v"))
TRANS = ((0, 0, 64, "v"), (0, 64, 128, "c"), (1, 0, 64, "v"), (1, 64, 128, "c"))
NAMES = ((0, 64, "v"), (64, 128, "c"))
NAMES3 = ((0, 64, "v"), (64, 128, "c"))
LOADS = ("cx", "tg", "xr", "qx", "lf")
WHICH, SWAPS, TABU = 0, 300, 12
HASHES = ((0, 256),)
BLOCKS0, BLOCKS = (3, 2, 1, 0), (3, 1, 2, 0)
FIXED = ("kKTC0 cXD2048 kSNC0 " + " ".join("kEQ2%d" % (128 * j) for j in range(8)) + " cXD0",
         "tXG0 tROW0 tROW128 tROW256 tXD0 tXD1024 tXG2048 tXD2048 tXD3072 tA0 tV0 tBT0 tGS0 tIN0", "tXG1024 tXG3072 tAB0 tAB3136 tSEL0 tGS1024")
PARTS = ((64, 256), (0, 64))
POOLS = {"s": 4, "x": 4}
SLACK, ROUNDS, PASSES, JIT, WIN = 100, 1, 20, 1000, 5000
CYC, PE, WAKE, GAT, SCA, DMA0, DMAB, REM0, REMB = 0.83, 0.417, 190, 1.56, 3.8, 1200, 0.004, 1500, 0.02


def _scratch():
    S = {}

    def sb(n, w, d="float32"):
        S[n] = ("sbuf", [128] + (w if isinstance(w, list) else [w]), d)
    B, I, U = "bfloat16", "int32", "uint16"
    sb("V", 4224, B); sb("DG", 4224, B); sb("FW", 4224, I); sb("FD", 2048, I); sb("NAME", 4224); sb("YT", 4224)
    for k in (0, 2, 3, 4, 5):
        sb("E%d" % k, 136)
    sb("HU", 1024, U); sb("U0", 1024, U); sb("PLR", 128, U); sb("NY", 128); sb("LFH", 1024, I); sb("LFS", 1024); sb("YL", 1152); sb("XLH", 1024, B)
    for k in range(3):
        sb("LF%d" % k, 1152); sb("XL%d" % k, 1024, B)
    sb("CI", 256, I); sb("CF", 272); sb("CU", 256, U); sb("Q", 272, B)
    sb("XG", 4096, B); sb("XD", 4096, B); sb("AB", [32, 128], B); sb("GS", 2048, B)
    sb("KEY", [16, 32]); sb("KT", 512); sb("SCN", 512); sb("RST", 512)
    sb("OI", 16, I); sb("OF", 16); sb("OU", 16, U); sb("DD", 272, B); sb("OR", 256, U); sb("EQ", [16, 256], B)
    sb("NA", 16, U); sb("Y", 512); sb("HI", 512, I); sb("H1", 272, I); sb("H2", 272, I)
    sb("CA", 256, B); sb("PX", 304, B); sb("ONE", 256, B); sb("JS", [4, 304], B); sb("JV", 768, B); sb("SV", 768, B); sb("RS2", 768, B)
    sb("LS", 4); sb("LU", 8, U); sb("CCU", 256, U); sb("QR", 128, B); sb("DDR", 128, B); sb("ROW", [3, 128], B); sb("MF", 8); sb("BT", 128); sb("DDE", 128, B); sb("CRU", 128, U)
    sb("NU", 8, U); sb("OUF", 8); sb("OUR", 8, U); sb("A", 128, B); sb("BF", 128); sb("CC", 256); sb("D12", 128)
    sb("IN", 256, B); sb("SEL", 128, B); sb("SD", 128); sb("SS", 128); sb("NEW", 128, B); sb("XO", 256, B)
    sb("KEC", [8, 32]); sb("KTC", 256); sb("SNC", 256)
    sb("KI", 8, I); sb("PI", 8, I); sb("BW", 8, I); sb("BU", 8, U); sb("PF", 8); sb("PU", 8, U); sb("P2", 8); sb("PU2", 8, U)
    sb("NMP", 128, B); sb("XP", 128, B); sb("DB", 128, B); sb("NV", 128, B); sb("EQ2", [8, 128], B); sb("EQ3", [8, 128], B); sb("FL", 128, B); sb("FM", 128, B)
    sb("SF", 136); sb("MU", 8, U); sb("MX", 8, U); sb("YQ", 256, B); sb("QX", 256, B); sb("TY", 256)
    sb("COL", 48); sb("IP", 4, I); sb("BO", 128); sb("BO1", 128); sb("OH", 16); sb("TF", 64); sb("POW", 16)
    sb("ZZ", 4 * 144, B); sb("WN", 16, B)
    for n in ("ID", "NID", "HID", "DB1", "DB2", "RY", "RE", "RL", "RD", "RB", "RI", "TRI", "ONB", "KP", "KD"):
        sb(n, 128, B)
    sb("ON128", 128); sb("IDF", 128); sb("NIF", 128); sb("LTF", 128); sb("J16", 16); sb("CT", 256, B); sb("KID", 128)
    sb("SC8", 8); sb("DSC", 8); sb("DSM", 8); sb("DSP", 8); sb("I8", 8)
    sb("TGL", 256, I); sb("DI", 1280, I); sb("DS", 5 * 256, B)
    sb("NB", 64, I); sb("NBD", 256, I); sb("NBB", 320, B); sb("DIG", 1024, B); sb("J256", 256, B)
    for n in range(8):
        S["ps%d" % n] = ("psum", [128, 512], "float32")
    return S


def _pack(S):
    real, virt, width = {}, {}, {}
    for n, (where, sh, d) in S.items():
        if where == "psum" or len(sh) > 2 or sh[1] > 400 or n[0] == "E" and n[1:].isdigit():
            real[n] = (where, sh, d)
        else:
            unit = 8 if d in ("float32", "int32") else 16
            at = width.get(d, 0)
            virt[n] = ("W" + d, at, sh[1])
            width[d] = at + -(-sh[1] // unit) * unit
    for d, w in width.items():
        real["W" + d] = ("sbuf", [128, w], d)
    return real, virt


ALL = _scratch()
SCRATCH, VIRT = _pack(ALL)
ARR = ["ax0", "ax1", "ax2", "af0", "af1", "af2", "aff", "ae0", "ae2", "ae3", "ae4", "ae5"]
SEMAPHORES = ["pv", "pc", "pt", "pg"] + ARR + ["d%d" % k for k in range(60)]
MASKS = {}
PLAN = []
ZK, ZT, ZN, Z1 = range(4)


def first_order(ops, tiles, tail):
    n = len(ops)
    succ = [[] for _ in ops]
    for k, o in enumerate(ops):
        for p, w in o["pre"].items():
            succ[p].append((k, w))
    if tail is None:
        tail, left = [0.0] * n, [len(s) for s in succ]
        todo = [k for k in range(n) if not left[k]]
        for k in todo:
            tail[k] = max([ops[k]["lat"]] + [tail[s] + (WAKE + ops[k]["lat"] if w else ops[k]["busy"]) for s, w in succ[k]])
            for x in ops[k]["pre"]:
                left[x] -= 1
                if not left[x]:
                    todo.append(x)
    left = [len(o["pre"]) for o in ops]
    ready = [0.0] * n
    avail = {q: [] for q in "vctgyn"}
    for k in range(n):
        if not left[k]:
            avail[ops[k]["q"]].append(k)
    free = {q: 0.0 for q in avail}
    begin, end = [0.0] * n, [0.0] * n
    banks, at = {}, 0
    for p, m in POOLS.items():
        banks[p] = [[at + j, None] for j in range(m)]; at += m
    nxt = {p: 0 for p in POOLS}
    todo = [len(t["ops"]) for t in tiles]
    bank, after, order = {}, {}, []

    def start(k):
        s = max(free[ops[k]["q"]], ready[k]) if ops[k]["q"] != "n" else ready[k]
        tl = ops[k].get("opens")
        if tl is None:
            return s, None
        t = tiles[tl]
        if t["pool"] == "s" and t["nth"] != nxt["s"]:
            return None, None
        best = None
        for b in banks[t["pool"]]:
            if b[1] is None or todo[b[1]] == 0:
                e = 0.0 if b[1] is None else max(end[x] for x in tiles[b[1]]["ops"]) + WAKE
                if best is None or e < best[0]:
                    best = (e, b)
        return (None, None) if best is None else (max(s, best[0]), best[1])
    while len(order) < n:
        pick = None
        for q in avail:
            cand = [(k,) + start(k) for k in avail[q]]
            cand = [x for x in cand if x[1] is not None]
            if not cand:
                continue
            cand.sort(key=lambda x: (-tail[x[0]], x[0]))
            best = cand[0]
            for x in cand[1:]:
                if x[1] < best[1]:
                    first = max(x[1] + tail[x[0]], max(best[1], x[1] + ops[x[0]]["busy"]) + tail[best[0]])
                    second = max(best[1] + tail[best[0]], best[1] + ops[best[0]]["busy"] + tail[x[0]])
                    if first <= second + SLACK:
                        best = x
            if pick is None or best[1] < pick[1]:
                pick = best
        k, s, b = pick
        o = ops[k]
        if b is not None:
            tl = o["opens"]
            if b[1] is not None:
                after[k] = list(tiles[b[1]]["ops"])
            b[1] = tl; bank[tl] = b[0]; nxt[tiles[tl]["pool"]] += 1
        for tl in o["tiles"]:
            todo[tl] -= 1
        avail[o["q"]].remove(k)
        free[o["q"]] = s + o["busy"]; begin[k] = s; end[k] = s + o["lat"]
        if "wire" in o:
            end[k] = free[o["wire"][0]] = max(end[k], free.get(o["wire"][0], 0.0) + o["wire"][1])
        order.append(k)
        for x, w in succ[k]:
            ready[x] = max(ready[x], end[k] + WAKE if w else s + o["busy"])
            left[x] -= 1
            if not left[x]:
                avail[ops[x]["q"]].append(x)
    return order, bank, after, max(end)


def gap(line, t, d):
    j = len(line)
    while j and line[j - 1][1] > t:
        j -= 1
    while j < len(line) and line[j][0] < t + d:
        t = max(t, line[j][1]); j += 1
    line.insert(j, (t, t + d))
    return t


def plan(ops, tiles):
    best, late, rng = None, None, np.random.default_rng(0)
    for _ in range(PASSES):
        x = settle(ops, *first_order(ops, tiles, late))
        if best is None or x[0] < best[0]:
            best = x
        at = best[0] * rng.random()
        late = {k: v + (JIT * float(z) if abs(v - at) < WIN else JIT / 2) for (k, v), z in zip(best[4].items(), rng.random(len(ops)))}
    return best[1:4] + best[:1]


def settle(ops, order, bank, after, span):
    pre = [dict(o["pre"]) for o in ops]
    for k, l in after.items():
        for x in l:
            pre[k][x] = pre[k].get(x, False) or ops[x]["q"] != "t"
    succ = [{} for _ in ops]
    for k, d in enumerate(pre):
        for x, w in d.items():
            succ[x][k] = w
    best, now = (span, order), order
    for _ in range(ROUNDS):
        lines, late = {}, {}
        for k in reversed(now):
            o = ops[k]
            e = max([late[x] + WAKE for x, w in succ[k].items() if w] + [0.0])
            if "wire" in o:
                e = gap(lines.setdefault(o["wire"][0], []), e, o["wire"][1])
            e = max([e + o["lat"] - o["busy"]] + [late[x] for x, w in succ[k].items() if not w])
            late[k] = (gap(lines.setdefault(o["q"], []), e, o["busy"]) if o["busy"] else e) + o["busy"]
        pos = {k: j for j, k in enumerate(now)}
        now = sorted(now, key=lambda k: (-late[k], pos[k]))
        lines, begin, end = {}, {}, {}
        for k in now:
            o = ops[k]
            s = max([end[x] + WAKE if w else begin[x] + ops[x]["busy"] for x, w in pre[k].items()] + [0.0])
            begin[k] = gap(lines.setdefault(o["q"], []), s, o["busy"]) if o["busy"] else s
            end[k] = begin[k] + o["lat"]
            if "wire" in o:
                end[k] = gap(lines.setdefault(o["wire"][0], []), end[k] - o["wire"][1], o["wire"][1]) + o["wire"][1]
        pos = {k: j for j, k in enumerate(now)}
        now = sorted(now, key=lambda k: (begin[k], pos[k]))
        if max(end.values()) < best[0]:
            best = (max(end.values()), now)
    return best + (bank, after, late)


def early(ops, pre, late):
    left = [len(d) for d in pre]
    succ = [[] for _ in ops]
    for k, d in enumerate(pre):
        for x in d:
            succ[x].append(k)
    avail = [k for k in range(len(ops)) if not left[k]]
    lines, begin, end, seq = {}, {}, {}, []
    while avail:
        k = max(avail, key=lambda x: (late[x], -x))
        avail.remove(k); seq.append(k)
        o = ops[k]
        s = max([end[x] + WAKE if w else begin[x] + ops[x]["busy"] for x, w in pre[k].items()] + [0.0])
        begin[k] = gap(lines.setdefault(o["q"], []), s, o["busy"]) if o["busy"] else s
        end[k] = begin[k] + o["lat"]
        if "wire" in o:
            end[k] = gap(lines.setdefault(o["wire"][0], []), end[k] - o["wire"][1], o["wire"][1]) + o["wire"][1]
        for x in succ[k]:
            left[x] -= 1
            if not left[x]:
                avail.append(x)
    if len(seq) < len(ops):
        return None
    pos = {k: j for j, k in enumerate(seq)}
    return sorted(seq, key=lambda k: (begin[k], pos[k])), begin, end


def latest(ops, pre, order):
    succ = [{} for _ in ops]
    for k, d in enumerate(pre):
        for x, w in d.items():
            succ[x][k] = w
    lines, late = {}, {}
    for k in reversed(order):
        o = ops[k]
        e = max([late[x] + WAKE for x, w in succ[k].items() if w] + [0.0])
        if "wire" in o:
            e = gap(lines.setdefault(o["wire"][0], []), e, o["wire"][1])
        e = max([e + o["lat"] - o["busy"]] + [late[x] for x, w in succ[k].items() if not w])
        late[k] = (gap(lines.setdefault(o["q"], []), e, o["busy"]) if o["busy"] else e) + o["busy"]
    return late


def plan2(ops, tiles):
    def behind(pre, after, a, b):
        k = tiles[b]["ops"][0]
        after[k] = tiles[a]["ops"]
        pre[k] = dict(pre[k])
        for x in after[k]:
            pre[k][x] = pre[k].get(x, False) or ops[x]["q"] != "t"
    base, after0, bank0 = [o["pre"] for o in ops], {}, {}
    turn = sorted((t["nth"], j) for j, t in enumerate(tiles) if t["pool"] == "s")
    for n, j in turn:
        bank0[j] = n % POOLS["s"]
        if n >= POOLS["s"]:
            behind(base, after0, turn[n - POOLS["s"]][1], j)
    late = [0.0] * len(ops)
    for k in range(len(ops) - 1, -1, -1):
        late[k] += ops[k]["lat"]
        for x, w in base[k].items():
            late[x] = max(late[x], late[k] + (WAKE if w else 0))
    best, rng = None, np.random.default_rng(0)
    for n in range(PASSES):
        order, begin, end = early(ops, base, late)
        pre, after, bank = list(base), dict(after0), dict(bank0)
        last = [None] * POOLS["x"]
        for s, j in sorted((begin[t["ops"][0]], j) for j, t in enumerate(tiles) if t["pool"] == "x" and t["ops"]):
            b = min(range(len(last)), key=lambda b: -1 if last[b] is None else max(end[x] for x in tiles[last[b]]["ops"]))
            if last[b] is not None:
                behind(pre, after, last[b], j)
            last[b] = j; bank[j] = POOLS["s"] + b
        x = early(ops, pre, late)
        if x is not None:
            x = early(ops, pre, latest(ops, pre, x[0]))
            span = max(x[2].values())
            if best is None or span < best[3]:
                best = (x[0], bank, after, span, latest(ops, base, x[0]))
        if best is None:
            late = latest(ops, base, order)
        else:
            at = best[3] * rng.random()
            late = {k: v + (JIT * float(z) if abs(v - at) < WIN else JIT / 2) for (k, v), z in zip(best[4].items(), rng.random(len(ops)))}
    return best


def polish(ops, order, after):
    n = len(ops)
    pre = [dict(o["pre"]) for o in ops]
    for k, l in after.items():
        for x in l:
            pre[k][x] = pre[k].get(x, False) or ops[x]["q"] != "t"
    busy = [o["busy"] for o in ops]; lat = [o["lat"] for o in ops]; wire = [o["wire"][1] if "wire" in o else 0 for o in ops]
    pw = [[x for x, w in d.items() if w] for d in pre]; po = [[x for x, w in d.items() if not w] for d in pre]
    sw, so = [[] for _ in ops], [[] for _ in ops]
    for k in range(n):
        for x in pw[k]:
            sw[x].append(k)
        for x in po[k]:
            so[x].append(k)
    mp, mn, wp, wn, last = [-1] * n, [-1] * n, [-1] * n, [-1] * n, {}
    for k in order:
        for key, a, b in [(ops[k]["q"], mp, mn)] * (ops[k]["q"] != "n") + ([(ops[k]["wire"][0], wp, wn)] if wire[k] else []):
            if key in last:
                a[k] = last[key]; b[last[key]] = k
            last[key] = k
    best, tabu, order = None, {}, list(order)
    for it in range(SWAPS):
        hb, jb, he, tb, jt, te = [0.0] * n, [0.0] * n, [0.0] * n, [0.0] * n, [0.0] * n, [0.0] * n
        for k in order:
            s = 0.0
            for x in pw[k]:
                if he[x] + WAKE > s:
                    s = he[x] + WAKE
            for x in po[k]:
                if hb[x] + busy[x] > s:
                    s = hb[x] + busy[x]
            jb[k] = s
            x = mp[k]
            if x >= 0 and hb[x] + busy[x] > s:
                s = hb[x] + busy[x]
            hb[k] = s; he[k] = s + lat[k]
            if wp[k] >= 0 and he[wp[k]] + wire[k] > he[k]:
                he[k] = he[wp[k]] + wire[k]
        span = max(he)
        if best is None or span < best[0] - 1e-6:
            best = (span, sorted(range(n), key=lambda j: (hb[order[j]], j)), list(order))
        for k in reversed(order):
            e = 0.0
            for x in sw[k]:
                if tb[x] + WAKE > e:
                    e = tb[x] + WAKE
            if wn[k] >= 0 and te[wn[k]] + wire[wn[k]] > e:
                e = te[wn[k]] + wire[wn[k]]
            te[k] = e; e += lat[k]
            for x in so[k]:
                if tb[x] + busy[k] > e:
                    e = tb[x] + busy[k]
            jt[k] = e
            if mn[k] >= 0 and tb[mn[k]] + busy[k] > e:
                e = tb[mn[k]] + busy[k]
            tb[k] = e
        pick = None
        for a in order:
            b = mn[a]
            if b < 0 or wire[a] or wire[b] or a in pre[b] or hb[a] + busy[a] + tb[b] < span - 1e-6:
                continue
            rb = max(jb[b], hb[mp[a]] + busy[mp[a]] if mp[a] >= 0 else 0.0); ra = max(jb[a], rb + busy[b])
            qa = max(jt[a], busy[a] + tb[mn[b]] if mn[b] >= 0 else 0.0); qb = max(jt[b], busy[b] + qa)
            est = max(rb + qb, ra + qa)
            if (tabu.get((a, b), -1) < it or est < best[0] - 1e-6) and (pick is None or est < pick[0]):
                pick = (est, a, b)
        if pick is None:
            break
        _, a, b = pick
        tabu[(b, a)] = it + TABU + (it * 7) % 11
        x, y = mp[a], mn[b]
        mp[b], mn[b], mp[a], mn[a] = x, a, b, y
        if x >= 0:
            mn[x] = b
        if y >= 0:
            mp[y] = a
        i, j = order.index(a), order.index(b)
        need, up = {b}, []
        for k in reversed(order[i + 1:j + 1]):
            if k in need:
                up.append(k); need.update(pre[k]); need.update((mp[k], wp[k]))
        order[i:j + 1] = up[::-1] + [k for k in order[i:j + 1] if k not in need or k == a]
    return [best[2][j] for j in best[1]], best[0]


def rank_program(g, core, T, topo):
    rank = T.rank_of(core)
    if rank is None:
        return
    eng = {"v": g.vector, "c": g.scalar, "t": g.tensor, "g": g, "y": g.sync}
    psem = {"v": "pv", "c": "pc", "t": "pt", "g": "pg"}
    ops, tiles, bank = [], [], {}
    W, R, named, part = {}, {}, {}, ["", 0]
    nd = [0]
    A_ = slice(None)

    def r(name, *idx):
        key = (name, str(idx))
        if key not in MASKS:
            if name in ALL:
                sh = ALL[name][1][1:]
                n = int(np.prod(sh)); f = np.zeros(n, np.uint8)
                f[np.arange(n).reshape(sh)[tuple(idx[1:])].reshape(-1)] = 1
                MASKS[key] = (int.from_bytes(np.packbits(f, bitorder="little").tobytes(), "little"), int(f.sum()))
            else:
                MASKS[key] = (1, int(np.prod(T[name].shape)) // 128)
        m, n = MASKS[key]
        if name in VIRT:
            arena, at, w = VIRT[name]
            cs = idx[1] if len(idx) > 1 else slice(0, w)
            lo, hi, st = cs.indices(w)
            ap = T[arena][idx[0] if idx else A_, at + lo:at + hi:st]
        else:
            ap = T[name][idx] if idx else T[name][:]
        size = 2 if (ALL[name][2] if name in ALL else name) in ("bfloat16", "uint16", "xr", "xl", "qx", "yq") else 4
        return dict(ap=lambda: ap, n=n, size=size, use=[(name, m)], tile=None, ind=False)

    def c(name, a, b, step=1):
        return r(name, A_, slice(a, b, step))

    def tile(pool="x"):
        tiles.append(dict(pool=pool, ops=[], phase=[], nth=None))
        return len(tiles) - 1

    def p(tl, a, b, step=1):
        return dict(ap=lambda: T["ps%d" % bank[tl]][:, a:b:step], n=len(range(a, b, step)), size=4, use=[], tile=tl, ind=False)

    def ind(w, o):
        return dict(ap=lambda: w["ap"]().indirect(o["ap"]()), n=16 * o["n"], size=w["size"], use=w["use"], off=o["use"], tile=None, ind=True)

    def record(q, fns, outs, ins, busy, lat=None, dma=None, rows=None, after=()):
        k = len(ops)
        pre = {x: True for x in after}
        rd = [x for o in ins for x in o["use"]] + [x for o in ins + outs for x in o.get("off", [])]
        wt = [x for o in outs for x in o["use"]]
        for n, m in rd:
            for e in W.get(n, []):
                if e[0] & m:
                    pre[e[1]] = True
        for n, m in wt:
            for e in W.get(n, []):
                if e[0] & m and not (rows and e[2] == rows):
                    pre[e[1]] = True
            for e in R.get(n, []):
                if e[0] & m:
                    pre[e[1]] = True
        op = dict(q=q, fns=fns, pre=pre, busy=busy, lat=busy if lat is None else lat, dma=dma, tiles=sorted({o["tile"] for o in ins + outs if o["tile"] is not None}))
        if wt:
            named.setdefault(("%s%s%d" % (part[0], wt[0][0], (wt[0][1] & -wt[0][1]).bit_length() - 1), part[1]), k)
        for tl in op["tiles"]:
            t = tiles[tl]
            if not t["ops"]:
                op["opens"] = tl
                t["nth"] = sum(1 for x in tiles if x["pool"] == t["pool"] and x["nth"] is not None)
            if t["phase"] and ops[t["phase"][0]]["q"] != q:
                t["before"] = t["phase"]; t["phase"] = []
            for x in t.get("before", []):
                pre[x] = True
            if q == "t" and t["phase"]:
                pre.setdefault(t["phase"][-1], False)
            t["phase"].append(k); t["ops"].append(k)
        for n, m in wt:
            if rows:
                W[n] = W.get(n, []) + [(m, k, rows)]
            else:
                W[n] = [(e[0] & ~m, e[1], e[2]) for e in W.get(n, []) if e[0] & ~m] + [(m, k, rows)]
                R[n] = [(e[0] & ~m, e[1]) for e in R.get(n, []) if e[0] & ~m]
        for n, m in rd:
            R.setdefault(n, []).append((m, k))
        ops.append(op)
        return k

    def cost(o, ins, rate, fix):
        if o["ind"]:
            return fix + o["n"] * SCA * CYC
        if ins[0]["ind"]:
            return fix + o["n"] * GAT * CYC
        return max(64, max(o["n"], ins[0]["n"]) * rate) * CYC

    def half(*x):
        return 0.5 if all(y["size"] == 2 for y in x) else 1

    def val(x):
        return x["ap"]() if isinstance(x, dict) else x

    def dma(q, out, in_, accum=False, rows=None, after=()):
        s = "d%d" % nd[0]; nd[0] += 1
        kw = dict(accum_op=O.add) if accum else {}
        d = 500 + 128 * min(out["n"], in_["n"]) * out["size"] * DMAB * (2 if accum else 1)
        k = record(q, [lambda: eng[q].dma_start(val(out), val(in_), **kw)], [out], [in_], 600 if q == "g" else 50, DMA0 + d, (s, 16, True), rows)
        ops[k]["wire"] = ("dma", d)
        for x in after:
            ops[k]["pre"].setdefault(x, False)
        return k

    def send(dst, name, n, in_, rsem, after=()):
        s = "d%d" % nd[0]; nd[0] += 1
        d = T.cores[(rank + dst) % 4]
        rid, pid, _ = topo.addr(d)
        k = record("g", [lambda: g.remote_dma(T[name][:, 0:n], val(in_), T.sem[rsem], T.sem[s], pid, rid, topo.mask(core, d))], [], [in_], 500,
                   REM0 + 128 * n * in_["size"] * REMB, (s, len(topo.engines(core, d)), False), None, after)
        ops[k]["wire"] = ("port", ops[k]["lat"] - REM0)
        ops.append(dict(q="n", fns=[], pre={k: True}, busy=0, lat=0, dma=(rsem, len(topo.engines(T.cores[(rank - dst) % 4], core)), False), tiles=[]))
        nm, m = c(name, 0, n)["use"][0]
        W[nm] = [(e[0] & ~m, e[1], e[2]) for e in W.get(nm, []) if e[0] & ~m] + [(m, k + 1, None)]
        return k + 1

    def ts(o, i, s1, op, s2=None, op2=None):
        ins = [i] + [s for s in (s1, s2) if isinstance(s, dict)]
        if op2 is None:
            record("v", [lambda: g.vector.tensor_scalar(val(o), val(i), val(s1), None, op)], [o], ins, cost(o, ins, half(o, i), 50))
        else:
            record("v", [lambda: g.vector.tensor_scalar(val(o), val(i), val(s1), val(s2), op, op2)], [o], ins, cost(o, ins, half(o, i), 50))

    def tt(o, a, b, op):
        record("v", [lambda: g.vector.tensor_tensor(val(o), val(a), val(b), op)], [o], [a, b], cost(o, [a], 1 if a["tile"] is not None else 2 * half(o, a, b), 50))

    def cp(o, i):
        record("v", [lambda: g.vector.tensor_copy(val(o), val(i))], [o], [i], cost(o, [i], half(o, i), 50))

    def ms(o, x):
        record("v", [lambda: g.vector.memset(val(o), x)], [o], [], cost(o, [o], half(o), 0))

    def act(o, i, f=F.Identity, bias=0.0, scale=1.0, acc=None):
        ins = [i] + [s for s in (bias, scale) if isinstance(s, dict)]
        kw = {} if acc is None else dict(accum_out=val(acc))
        record("c", [lambda: g.scalar.activation(val(o), val(i), f, bias=val(bias), scale=val(scale), **kw)], [o] + ([acc] if acc else []), ins, cost(o, ins, 1, 65))

    def mm(*l, start=True, stop=True):
        def one(j, x):
            return lambda: g.tensor.matmul(val(x[0]), val(x[1]), val(x[2]), start and j == 0, stop and j == len(l) - 1)
        record("t", [one(j, x) for j, x in enumerate(l)], [x[0] for x in l], [y for x in l for y in x[1:]], sum(max(64, x[2]["n"]) * (4 if x[2]["size"] == 4 else 1) * PE for x in l))

    def iota(o, pat, base, cm, f=False):
        kw = dict(allow_small_or_imprecise_dtypes=True) if f else {}
        record("g", [lambda: g.iota(val(o), pat, base, cm, **kw)], [o], [], 130 + 2 * o["n"] * CYC)

    def aff(o, i, pat, base, cm, op=O.is_ge):
        record("g", [lambda: g.affine_select(val(o), val(i), pat, op, 0.0, base, cm)], [o], [i], 170 + 2 * o["n"] * CYC)

    def gat(q, o, w, l, add=None):
        if q == "c":
            act(o, ind(w, l), F.Identity, 0.0 if add is None else add)
        elif add is None:
            cp(o, ind(w, l))
        else:
            ts(o, ind(w, l), add, O.add)

    def scan(o, d0, d1, init, o0, o1):
        record("v", [lambda: g.vector.tensor_tensor_scan(val(o), val(d0), val(d1), init, o0, o1)], [o], [d0, d1], cost(o, [d0], half(o, d0, d1), 0))

    def trn(o, i):
        record("v", [lambda: g.vector.transpose(val(o), val(i))], [o], [i], cost(o, [i], half(o, i), 0))

    def col(k):
        return c("COL", k, k + 1)

    def sel(z, a):
        return c("ZZ", 144 * z + 15 - a, 144 * z + 143 - a)

    def zcols(z):
        return c("ZZ", 144 * z + 15, 144 * z + 143, 16)

    def scaled(o, i, w):
        act(o, i, F.Copy, 0.0, w if isinstance(w, dict) else float(w))

    def wrap(o, z, x, lo, hi):
        return [(o, sel(z, a), c(x, lo + a, hi, 16)) for a in range(16)]
    SHR, AND = O.logical_shift_right, O.bitwise_and
    B23, B24, B26, BIG, ROUND = 2.0 ** 23, 2.0 ** 24, 2.0 ** 26, 2.0 ** 30, 1.5 * 2.0 ** 23
    VW, DW = c("V", 0, 4096), c("DG", 0, 4096)

    k = []
    for n in LOADS:
        k = [dma("y", {"cx": r("CI"), "tg": r("TGL"), "xr": VW, "qx": r("QX"), "lf": r("LFH")}[n], r(n), after=k)]
    cp(r("CU"), r("CI")); cp(c("CF", 0, 256), r("CI"))
    act(c("Q", 0, 256), r("QX"), F.Identity, 192.0)
    cp(r("HU"), r("LFH")); cp(r("LFS"), r("LFH"))
    first = send(3, "U0", 1024, r("HU"), "af0")
    cp(c("LF0", 0, 1024), r("U0"))

    iota(c("IP", 0, 1), [[1, 1]], 0, 1)
    iota(r("J16"), [[1, 16]], 0, 0, True)
    iota(r("I8"), [[16, 8]], 0, 0, True)
    ms(r("ON128"), 1.0)
    aff(r("IDF"), r("ON128"), [[-1, 128]], 0, 1, O.is_equal)
    aff(r("BO1"), r("ON128"), [[-16, 8], [0, 16]], 0, 1)
    aff(r("BO"), r("BO1"), [[16, 8], [0, 16]], 15, -1)
    aff(r("LTF"), r("BO"), [[1, 128]], -1, -1)
    iota(r("J256"), [[1, 256]], 0, 0, True)
    iota(r("NB"), [[1, 64]], 0, 64)
    for k in range(2):
        iota(c("NAME", 1024 * k, 1024 * k + 1024), [[1, 1024]], 1024 * k, 0, True)
        act(c("NAME", 2048 + 1024 * k, 3072 + 1024 * k), c("NAME", 1024 * k, 1024 * k + 1024), F.Identity, 2048.0)
    act(c("NAME", 4096, 4224), c("NAME", 0, 128), F.Identity, 4096.0)
    ts(c("IP", 1, 2), c("IP", 0, 1), 15, AND); ts(c("IP", 2, 3), c("IP", 0, 1), 4, SHR, 1, AND)
    cp(col(0), c("IP", 1, 2)); cp(col(1), c("IP", 2, 3))
    ts(r("OH"), r("J16"), col(0), O.is_equal)

    def oh(f):
        return c("OH", f, f + 1)
    ts(col(24), col(0), 4096.0, O.mult)
    ts(col(2), col(1), B24, O.mult, col(24), O.add); ts(col(25), col(24), B24, O.add); ts(col(3), col(1), -B24, O.mult, col(25), O.add)
    ts(col(20), col(1), B26, O.mult, B23, O.add); ts(col(21), col(1), -B26, O.mult, B26 + B23, O.add)
    ts(col(26), oh(1), 32.0, O.mult); ts(col(27), oh(2), 256.0, O.mult, col(26), O.add); ts(col(28), oh(3), 2048.0, O.mult, col(27), O.add)
    ts(col(4), oh(0), 16.0, O.mult, col(28), O.add)
    ts(col(29), col(0), 4.0, O.is_lt, oh(9), O.add); ts(col(8), oh(0), -2.0, O.mult, col(29), O.add)
    ts(col(16), col(0), 5.0, O.is_ge)
    ts(col(30), oh(4), 16.0, O.mult); ts(col(11), col(4), 2.0, O.mult, col(30), O.add)
    ts(col(5), oh(6), 256.0, O.mult, oh(5), O.add); ts(col(17), oh(9), 8192.0, O.mult, col(5), O.add)
    tt(col(12), col(17), col(4), O.add)
    ts(col(6), oh(4), -B24, O.mult); ts(col(13), oh(9), B23, O.mult)
    ts(col(9), col(0), 5.0, O.is_lt); tt(col(14), oh(5), oh(6), O.add)
    ts(col(19), col(4), -1.0, O.mult); ts(col(15), oh(6), 16.0, O.mult)
    ts(col(10), col(0), 10.0, O.is_ge, -0.0625, O.mult); ts(col(31), oh(4), -0.0625, O.mult)
    ts(c("COL", 32, 36), c("OH", 10, 14), col(14), O.add); ts(c("COL", 36, 40), c("OH", 10, 14), col(31), O.add)
    ms(c("TF", 0, 16), 0.5); ms(c("TF", 16, 32), 0.0)
    scan(r("POW"), c("TF", 0, 16), c("TF", 16, 32), 65536.0, O.mult, O.add)
    tt(c("TF", 32, 48), r("OH"), r("POW"), O.mult)
    record("v", [lambda: g.vector.tensor_reduce(val(col(7)), val(c("TF", 32, 48)), AxisListType.X, O.add)], [col(7)], [c("TF", 32, 48)], 64 * CYC)
    ms(r("ZZ"), 0.0)
    for z, w in ((ZK, 65536.0), (ZT, col(4)), (ZN, col(12)), (Z1, 512.0)):
        scaled(zcols(z), c("BO", 0, 128, 16), w)
    scaled(c("WN", 0, 8), c("BO", 0, 128, 16), col(19)); scaled(c("WN", 8, 16), c("BO", 0, 128, 16), -65536.0)
    for n, w in (("ID", 1.0), ("NID", -1.0), ("HID", 0.5), ("DB1", -2.0 ** 28), ("DB2", B26), ("KP", col(14)), ("KD", col(9))):
        scaled(r(n), r("IDF"), w)
    scaled(c("KP", 4, 128, 16), c("BO", 0, 128, 16), col(10))
    for n, w in (("RY", col(11)), ("RE", col(6)), ("RL", col(4)), ("RD", col(7)), ("RB", 65536.0), ("RI", col(13))):
        scaled(r(n), r("BO"), w)
    tt(r("BO1"), r("LTF"), r("IDF"), O.subtract); scaled(r("TRI"), r("BO1"), B23)
    ms(r("ONB"), 1.0); scaled(r("KID"), r("IDF"), 1024.0)
    ts(c("CT", 0, 16), r("POW"), 2.0, O.mult)
    for k in (16, 32, 64, 128):
        act(c("CT", k, 2 * k), c("CT", 0, k))
    ms(r("RST"), 0.0); ms(c("RST", 0, 512, 32), BIG)
    ms(r("RS2"), 1.0); ms(c("RS2", 0, 768, 192), 0.0); ms(r("ONE"), 1.0); ms(c("PX", 256, 304), 1024.0)
    ts(r("DSC"), r("I8"), col(0), O.add, 4096.0, O.add); ts(r("SC8"), r("DSC"), 2.0, O.mult, -8191.0, O.add)
    ts(r("DSM"), r("DSC"), -3073.0 - 8192, O.add); ts(r("DSP"), r("DSC"), -8192.0, O.add)
    ms(c("Q", 256, 272), 192.0); ms(c("CF", 256, 272), 0.0); ms(c("H1", 256, 272), 0); ms(c("H2", 256, 272), 0); ms(c("V", 4096, 4224), 0.0)
    scaled(c("DD", 256, 272), c("ON128", 0, 16), oh(9))
    ts(c("TF", 48, 64), r("J16"), oh(6), O.mult)
    for j in range(16):
        if j % 2:
            act(c("DG", 256 * j, 256 * j + 256), r("J256"), F.Identity, c("TF", 48 + j, 49 + j), oh(5))
        else:
            ts(c("DG", 256 * j, 256 * j + 256), r("J256"), oh(5), O.mult, c("TF", 48 + j, 49 + j), O.add)
    act(c("DG", 4096, 4224), c("J256", 0, 128), F.Identity, col(15), oh(5))
    for j, (s, m) in enumerate(((1, 1), (2, 7), (5, 7), (8, 7), (0, 1))):
        ts(c("DI", j * 256, (j + 1) * 256), r("TGL"), s, SHR, m, AND)
    ts(c("DS", 0, 1280), r("DI"), 0.0625, O.mult)
    k = [dma("y", r("DG", slice(f, None, 16), slice(0, 4096)), c("DS", f * 256, f * 256 + 256), rows="DG") for f in range(5)]
    k = [dma("y", r("XLH"), r("xl"), after=k)]
    k = [dma("y", r("FD"), r("fd"), after=k)]
    second = send(3, "XL0", 1024, r("XLH"), "ax0", [first - 1])
    send(2, "LF1", 1024, r("LFS"), "af1", [second])
    for j, (s, m) in enumerate(((0, 1), (1, 7), (4, 7), (7, 7))):
        ts(c("NBD", 64 * j, 64 * j + 64), r("NB"), s, SHR, m, AND)
    ts(c("NBB", 0, 256), r("NBD"), 0.0625, O.mult); ms(c("NBB", 256, 320), 0.0625); ms(r("DIG"), 0.0)
    for f in range(5):
        dma("y", r("DIG", slice(f, None, 16)), c("NBB", 64 * f, 64 * f + 64), rows="DIG", after=k)
    for h in range(2):
        ts(c("FW", 1024 * h, 1024 * h + 1024), c("FD", 1024 * h, 1024 * h + 1024), 4095, AND)
        ts(c("FW", 2048 + 1024 * h, 3072 + 1024 * h), c("FD", 1024 * h, 1024 * h + 1024), 12, SHR)

    def sub(x0, q, lo, u, out):
        b = tile("s")
        mm(*[(p(b, ii * 64, ii * 64 + 64), r("NID"), c(q, lo, lo + 64)) for ii in range(8)], stop=False)
        mm(*[(p(b, ii * 64, ii * 64 + 64), r("ID"), c("XD", x0 + 8 * u + ii, x0 + 1024, 16)) for ii in range(8)], start=False)
        act(out, p(b, 0, 512), F.Abs)

    def choice(t):
        LF = c("LF%d" % (t % 3), 0, 1024)
        part[:] = "c", t
        for lo, hi, q in (CHOICE if t else CHOICE0):
            gat(q, c("XD", 16 * lo, 16 * hi), VW, c("CU", lo, hi), 192.0)
        if t == 0:
            for j in range(8):
                b = tile()
                mm((p(b, 0, 512), r("ID"), c("V", 512 * j, 512 * j + 512)), (p(b, 0, 512), r("KD"), c("DG", 512 * j, 512 * j + 512)))
                act(c("V", 512 * j, 512 * j + 512), p(b, 0, 512))
        else:
            claims(t - 1); disk_write(t - 1)
        part[:] = "c", t
        PC = tile()
        for lo, hi in PARTS:
            PA = tile()
            b0, b1 = lo // 16, hi // 16
            mm((p(PA, lo, hi), r("IDF"), c("CF", lo, hi)), stop=False)
            blocks = [k for k in (BLOCKS if t else BLOCKS0) if lo <= 64 * k < hi]
            for k in blocks:
                for u in range(2):
                    j = 8 * k + 4 * u
                    sub(1024 * k, "Q", 64 * k, u, r("AB", A_, slice(j, j + 4)))
                    mm(*[(p(PA, 64 * k, 64 * k + 64), sel(ZK, 8 * u + ii), r("AB", A_, j + ii // 2, slice(64 * (ii % 2), 64 * (ii % 2) + 64))) for ii in range(8)],
                       start=False, stop=u == 1 and k == blocks[-1])
            act(r("KEY", A_, slice(b0, b1), slice(0, 16)), p(PA, lo, hi), F.Identity, col(2))
            act(r("KEY", A_, slice(b0, b1), slice(16, 32)), p(PA, lo, hi), F.Identity, col(3))
            trn(c("KT", 2 * lo, 2 * hi), r("KEY", A_, slice(b0, b1)))
            scan(c("SCN", 2 * lo, 2 * hi), c("RST", 2 * lo, 2 * hi), c("KT", 2 * lo, 2 * hi), BIG, O.max, O.min)
            cp(c("OI", b0, b1), c("SCN", 2 * lo + 31, 2 * hi, 32))
            ts(c("OI", b0, b1), c("OI", b0, b1), 4095, AND)
            cp(c("OU", b0, b1), c("OI", b0, b1)); cp(c("OF", b0, b1), c("OI", b0, b1))
            gat("v", c("OR", lo, hi), c("NAME", 0, 4096), c("OU", b0, b1))
            for b in range(b0, b1):
                ts(r("EQ", A_, b, slice(0, 256 - 16 * b)), c("OR", 16 * b, 256), c("OF", b, b + 1), O.is_equal)
                if b < 15:
                    opens = b == PARTS[0][0] // 16
                    mm(*[(p(PC, 0, 256), r("NID"), r("CT"))] * opens, (p(PC, 16 * b + 16, 256), r("RB"), r("EQ", A_, b, slice(16, 256 - 16 * b))), start=opens, stop=False)
            mm((p(PC, lo, hi), r("RD"), r("EQ", A_, slice(b0, b1), slice(0, 16))), start=False, stop=False)
        for lo, hi in HASHES:
            PN = tile()
            b0, b1 = lo // 16, hi // 16
            gat("c", c("DD", lo, hi), DW, c("OU", b0, b1))
            mm(*wrap(p(PN, b0, b1), ZT, "DD", lo, hi))
            cp(c("NA", b0, b1), p(PN, b0, b1))
            for w, (add, less, sh) in enumerate(((4.0, 16.0, 3), (592.0, 592.0 ** 2 - 32, 5))):
                act(c("Y", 256 * w + lo, 256 * w + hi), ind(LF, c("NA", b0, b1)), F.Square, add)
                ts(c("HI", 256 * w + lo, 256 * w + hi), c("Y", 256 * w + lo, 256 * w + hi), less, O.subtract)
                ts(c("H%d" % (w + 1), lo, hi), c("HI", 256 * w + lo, 256 * w + hi), sh, SHR, 4095, AND)
        mm((p(PC, 0, 256), r("RE"), c("DD", 0, 256)), start=False)
        act(r("CA"), p(PC, 0, 256), F.Sign, -1048576.5, -1.0)
        scan(c("PX", 0, 256), r("ONE"), r("CA"), 0.0, O.add, O.add)
        for b in range(4):
            act(r("JS", A_, b, slice(0, 304 - 32 * b)), c("PX", 16 * b, 304 - 16 * b), F.Sign, c("SC8", b, b + 1), -1.0, c("LS", b, b + 1))
            ts(c("JV", 192 * b, 192 * b + 192), c("PX", 64, 256), c("SC8", 4 + b, 5 + b), O.is_le)
        scan(r("SV"), r("RS2"), r("JV"), 0.0, O.mult, O.add)
        ts(c("LU", 4, 8), c("SV", 191, 768, 192), 64.0, O.add)
        ts(c("LU", 0, 4), r("LS"), 0.5, O.mult, 152.0, O.add)

    def translate(t):
        part[:] = "t", t
        LF, XL = c("LF%d" % (t % 3), 0, 1024), r("XL%d" % (t % 3))
        gat("v", c("CCU", 0, 128), r("H1"), r("LU")); gat("v", c("CCU", 128, 256), r("H2"), r("LU"))
        gat("c", r("QR"), r("Q"), r("LU")); gat("c", r("DDR"), r("DD"), r("LU")); gat("v", r("CRU"), r("CF"), r("LU"))
        for w, lo, hi, q in TRANS:
            gat(q, c("XG", 2048 * w + 16 * lo, 2048 * w + 16 * hi), VW, c("CCU", 128 * w + lo, 128 * w + hi))
        PL, PT, PD, PS, PQ = tile(), tile(), tile(), tile(), tile()
        for j, w in enumerate((9, 16, 8)):
            ts(r("ROW", A_, j), r("DDR"), col(w), O.mult)
        mm(*[(p(PL, 0, 24), sel(ZN, a), r("ROW", A_, A_, slice(a, 128, 16))) for a in range(16)]); mm((p(PL, 128, 256), r("RL"), r("DDR")))
        cp(r("NU"), p(PL, 0, 8)); tt(r("OUF"), p(PL, 8, 16), r("DSC"), O.min); cp(r("OUR"), r("OUF")); cp(r("MF"), p(PL, 16, 24))
        gat("v", r("BF"), LF, r("NU")); gat("v", r("A"), XL, r("NU"))
        PB = tile()
        mm((p(PB, 0, 128), r("BF"), r("IDF"))); ts(r("BT"), p(PB, 0, 128), -451584.0, O.add)
        for b in range(8):
            ts(r("EQ3", A_, b, slice(0, 128 - 16 * b)), p(PL, 128 + 16 * b, 256), p(PL, b, b + 1), O.is_equal)
        cp(r("CC"), r("CCU")); tt(r("D12"), c("CC", 128, 256), c("CC", 0, 128), O.subtract)
        for w in range(2):
            for h in range(2):
                x0 = 2048 * w + 1024 * h
                ts(c("XD", x0, x0 + 1024), c("XG", x0, x0 + 1024), 192.0, O.add)
                for u in range(2):
                    sub(x0, "QR", 64 * h, u, r("AB", A_, slice(16 * w + 8 * u, 16 * w + 8 * u + 8), slice(64 * h, 64 * h + 64)))
            for x, z in (("XG", zcols(ZT)), ("XD", c("WN", 0, 8))):
                mm(*[(p(PT, 128 * w + i, 128 * w + 128, 16), c(x, 2048 * w + i, 2048 * w + 2048, 16), z) for i in range(16)], start=w == 0 and x == "XG", stop=w == 1 and x == "XD")
        for w in range(2):
            tt(c("IN", 128 * w, 128 * w + 128), p(PT, 128 * w, 128 * w + 128), r("BT"), O.is_equal)
        for w in range(2):
            for u in range(2):
                if w == 1 and u == 1:
                    mm((p(PD, 0, 128), r("DB1"), c("IN", 0, 128)), (p(PD, 0, 128), r("DB2"), c("IN", 128, 256)), start=False, stop=False)
                mm(*[(p(PD, i, 128, 16), r("AB", A_, 16 * w + i), zcols(ZK) if w else c("WN", 8, 16)) for i in range(8 * u, 8 * u + 8)], start=w + u == 0, stop=w + u == 2)
        act(r("SEL"), p(PD, 0, 128), F.Sign, -0.5)
        mm((p(PS, 0, 128), r("ONB"), r("HID")), (p(PS, 0, 128), r("SEL"), r("HID")))
        tt(r("SD"), p(PS, 0, 128), r("D12"), O.mult)
        tt(r("SS"), r("SD"), c("CC", 0, 128), O.add)
        cp(ind(r("FW"), r("OUR")), r("SS"))
        if t < STEPS - 1:
            gat("v", r("CU"), c("FW", 0, 4096), r("OU"))
        tt(ind(r("V"), r("OUR")), r("A"), r("ROW", A_, 0), O.add)
        gat("c", r("XO"), VW, r("OU"), 192.0)
        mm((p(PQ, 0, 256), r("HID"), c("Q", 0, 256)), (p(PQ, 0, 256), r("HID"), r("XO")))
        act(c("Q", 0, 256), p(PQ, 0, 256), F.Identity, -0.25)
        ts(r("DDE"), r("DDR"), col(36 + t), O.add)
        cp(ind(r("DG"), r("OUR")), r("DDE"))
        for lo, hi, q in (NAMES if t < STEPS - 1 else NAMES3):
            gat(q, c("GS", 16 * lo, 16 * hi), DW, c("CRU", lo, hi))
        if t < STEPS - 1:
            cp(c("CF", 0, 256), r("CU"))
        else:
            gat("v", c("CF", 0, 256), c("FW", 0, 4096), r("OU"))

    def lower(b, eq, fl):
        mm((p(b, 0, 128), r("RD"), r(eq, A_, A_, slice(0, 16))), (p(b, 0, 128), r("NID"), c("CT", 0, 128)),
           *[(p(b, 16 * j + 16, 128), r("RB"), r(eq, A_, j, slice(16, 128 - 16 * j))) for j in range(7)])
        act(r(fl), p(b, 0, 128), F.Sign, 0.5)

    def apply(lst, x, n, u):
        ts(r(u), lst, 8193.0, O.add)
        cp(ind(r(n), r(u)), x)

    def disk_write(t):
        a, b, s = tile(), tile(), tile()
        part[:] = "d", t + 1
        lower(a, "EQ3", "FM")
        mm((p(b, 0, 8), r("IDF"), r("MF")), *wrap(p(b, 0, 8), Z1, "FM", 0, 128))
        tt(c("SF", 128, 136), p(b, 0, 8), r("DSM"), O.min)
        mm(*[(p(s, 0, 128), sel(ZT, i), c("GS", i, 2048, 16)) for i in range(16)])
        act(c("SF", 0, 128), p(s, 0, 128))
        to = (((3, 0, "LF1"),), ((3, 2, "LF2"), (1, 3, "LF0")), ((2, 4, "LF0"),), ((1, 5, "YL"),))[t]
        for dst, k, n in to:
            last = send(dst, "E%d" % k, 136, r("SF"), "ae%d" % k)
        if t == 0:
            send(2, "XL1", 1024, r("XLH"), "ax1", [last - 1])
        if t in (0, 2):
            apply(c("SF", 128, 136), c("SF", 0, 128), "LF%d" % t, "MU")
            last = send(*((2, "LF2", 1024, c("LF0", 0, 1024), "af2"), (3, "YL", 1024, c("LF2", 0, 1024), "aff"))[t // 2])
        if t == 0:
            send(1, "XL2", 1024, r("XLH"), "ax2", [last - 1])
        for dst, k, n in to:
            apply(c("E%d" % k, 128, 136), c("E%d" % k, 0, 128), n, "MX")

    def claims(t):
        a, b, n, v, e, w = tile(), tile(), tile(), tile(), tile(), tile()
        part[:] = "k", t + 1
        mm((p(a, 0, 128), c("IN", 0, 128), r("ID")), (p(a, 0, 128), c("IN", 128, 256), r("ID")))
        act(r("NEW"), p(a, 0, 128), F.Relu, 1.0, -1.0)
        mm((p(b, 0, 128), r("TRI"), r("NEW")), (p(b, 0, 128), r("IDF"), r("BF")), (p(b, 0, 128), r("RI"), r("DDR")), stop=False)
        mm((p(b, 0, 128), r("KID"), r("SS")), start=False)
        act(r("KEC", A_, A_, slice(0, 16)), p(b, 0, 128), F.Identity, col(20)); act(r("KEC", A_, A_, slice(16, 32)), p(b, 0, 128), F.Identity, col(21))
        trn(r("KTC"), r("KEC"))
        scan(r("SNC"), c("RST", 0, 256), r("KTC"), BIG, O.max, O.min)
        cp(r("KI"), c("SNC", 31, 256, 32))
        ts(r("PI"), r("KI"), 10, SHR); ts(r("BW"), r("KI"), 1023, AND)
        tt(r("PF"), r("PI"), r("DSC"), O.min)
        cp(r("PU"), r("PF")); cp(r("BU"), r("BW"))
        act(r("NMP"), ind(r("DG"), r("PU")), F.Copy, 0.0, col(32 + t))
        gat("c", r("DB"), r("DIG"), r("BU"))
        gat("v", r("PLR"), r("NAME"), r("PU"))
        mm((p(v, 0, 128), r("KP"), r("NMP")), (p(v, 0, 128), r("ID"), r("DB")))
        act(r("NV"), p(v, 0, 128))
        for j in range(8):
            ts(r("EQ2", A_, j, slice(0, 128 - 16 * j)), c("PLR", 16 * j, 128), c("PF", j, j + 1), O.is_equal)
        lower(e, "EQ2", "FL")
        mm((p(w, 0, 8), r("IDF"), r("PF")), *wrap(p(w, 0, 8), Z1, "FL", 0, 128))
        tt(r("P2"), p(w, 0, 8), r("DSP"), O.min)
        ts(r("PU2"), r("P2"), 8192.0, O.add)
        if t < STEPS - 1:
            cp(ind(r("DG"), r("PU2")), r("NV"))
            ts(r("XP"), ind(r("V"), r("PU")), ROUND, O.add, ROUND, O.subtract)
            tt(ind(r("V"), r("PU2")), r("XP"), r("DB"), O.add)
        else:
            for j in range(8):
                b = tile("s")
                mm((p(b, 0, 512), r("RY"), c("DG", 512 * j, 512 * j + 512)))
                act(c("YT", 512 * j, 512 * j + 512), p(b, 0, 512))
            mm((p(n, 0, 128), r("RY"), r("NV")))
            act(r("NY"), p(n, 0, 128))
            cp(ind(r("YT"), r("PU2")), r("NY"))

    for t in range(STEPS):
        choice(t)
        translate(t)
    dma("y", r("yc"), c("CF", 0, 256))
    act(r("YQ"), c("Q", 0, 256), F.Identity, -192.0)
    dma("y", r("yq"), r("YQ"))
    claims(STEPS - 1); disk_write(STEPS - 1)
    dma("y", r("yl"), c("YL", 0, 1024))
    dma("y", r("yt"), r("YT", slice(0, None, 16), slice(0, 4096)))

    for t in range(STEPS):
        for line in FIXED:
            l = [named[n, t] for n in line.split() if (n, t) in named]
            for a, b in zip(l, l[1:]):
                ops[b]["pre"].setdefault(a, False)
    if not PLAN:
        x = (plan, plan2)[WHICH](ops, tiles)
        y = polish(ops, x[0], x[2])
        PLAN.append((y[0], x[1], x[2], y[1], x[3]))
    order, banks, after = PLAN[0][:3]
    bank.update(banks)
    cnt = {q: 0 for q in psem}
    know = {q: {} for q in eng}
    tok, total = {}, {}
    for k in order:
        o = ops[k]; q = o["q"]
        if q == "n":
            tok[k] = (o["dma"][0], o["dma"][1], {}); total[o["dma"][0]] = o["dma"][1]
            continue
        best = {}
        for x in [x for x, w in o["pre"].items() if w] + [x for x in after.get(k, []) if ops[x]["q"] != "t"]:
            s, v, sn = tok[x]
            if s not in best or best[s][0] < v:
                best[s] = (v, sn)
        need = sorted(best.items(), key=lambda z: -len(z[1][1]))
        for s, (v, sn) in need:
            if know[q].get(s, 0) >= v or any(s2 != s and sn2.get(s, 0) >= v and know[q].get(s2, 0) < v2 for s2, (v2, sn2) in need):
                continue
            eng[q].wait_ge(T.sem[s], v)
            know[q][s] = v
            for a, b in sn.items():
                if know[q].get(a, 0) < b:
                    know[q][a] = b
        for fn in o["fns"]:
            inst = fn()
            if o["dma"] is None:
                cnt[q] += 1
                inst.then_inc(T.sem[psem[q]], 1)
            elif o["dma"][2]:
                inst.then_inc(T.sem[o["dma"][0]], 16)
        s, v = (psem[q], cnt[q]) if o["dma"] is None else o["dma"][:2]
        tok[k] = (s, v, dict(know[q])); total[s] = v
    for s in sorted(total):
        g.wait_ge(T.sem[s], total[s])
